import numpy as np, ml_dtypes
CORES = [78,86,94,102,110,118]
N = 6
BF = ml_dtypes.bfloat16
W, R, P, STEPS, HOPS, SHIFT = 1024, 8192, 512, 3, 3, 2
def parts(rng):
    h = rng.integers(0, 256, (N, 8, 16, P)); w = rng.integers(0, 256, (N, 8, 16, 1)); t = rng.integers(700, 1300, (N, 8, 16, 1))
    m = rng.random((N, 8, W)) < rng.choice(np.array([0.1, 0.25, 0.5]), (N, 8, 1))
    return h, w, t, m, rng.integers(0, R, (N, 8, 16, W)), rng.integers(0, 256, (N, 8, 16, R))
def pack(h, w, t, m, o, r):
    m = m.astype(np.int32); m[..., 0] = 1
    b = lambda v, n: np.ascontiguousarray(v.reshape(N, 128, n)).astype(np.float32).astype(BF)
    i = lambda v, n: np.ascontiguousarray(v.reshape(N, 128, n)).astype(np.int32)
    return {"h0": b(h, P), "w": b(w, 1), "th": i(t, 1), "marks": m, "owner": i(o, W), "hdr": b(r, R)}
def far(rng, h, t, o, r, g, u=None):
    r[:, g] = rng.integers(128, 192, (N, 16, R))
    goal = np.where(np.arange(R) % 2 == 0, 4, 0) + rng.integers(0, 4, (N, R))
    r[:, g, 15] = 128 + ((goal - np.sum(r[:, g, :15], axis=1)) & 63)
    o[:, g] = (o[:, g] & -2) + (np.arange(16) & 1)[:, None]
    h[:, g] = rng.integers(0, 16, (N, 16, P))
    if u is not None: h[:, g, 0] = u >> 4; h[:, g, 1] = u & 15
    h[:, g, 15] = (-np.sum(h[:, g, :15], axis=1)) & 63
    t[:, g] = rng.integers(1300, 1751, (N, 16, 1))
def setup_inputs(rng):
    return pack(*parts(rng))
def setup_inputs_crowd(rng):
    h, w, t, m, o, r = parts(rng)
    w[:, 0::4] = 0; t[:, 0::4] = rng.integers(500, 1100, (N, 2, 16, 1))
    w[:, 1::4] = 0; w[:, 1::4, 0] = rng.integers(1, 4, (N, 2, 1)); h[:, 1::4, 0] = rng.integers(0, 3, (N, 2, P))
    w[:, 2::4] = 128 * rng.integers(0, 2, (N, 2, 16, 1))
    n = P // 16; lane = np.arange(P)
    far(rng, h, t, o, r, 4)
    start = rng.integers(0, n, (N, 16)); start[:, 0::4] = 0; start[:, 1::4] = n - 1; start[:, 3::4] = 1
    near = (lane >> 4) < start[:, lane & 15]
    h[:, 4] = np.where(near[:, None, :], rng.integers(128, 192, (N, 16, P)), h[:, 4])
    k = np.arange(256); found = np.unique((((k * k) >> 5) + k) & (W - 16), return_index=True)[1]
    order = np.argsort(rng.random((N, 16, len(found))), axis=-1)[..., :n]
    far(rng, h, t, o, r, 7, found[order].transpose(0, 2, 1).reshape(N, P))
    w[:, 7] = 0; w[:, 7, 0] = 16; w[:, 7, 1] = 1; m[:, 7] = True
    return pack(h, w, t, m, o, r)
def setup_inputs_ends(rng):
    h, w, t, m, o, r = parts(rng)
    k = np.arange(4096); tops = np.flatnonzero(((((k * k) >> 5) + k) & (W - 16)) == W - 16)
    u = rng.integers(0, 4096, (N, 6, P)); u[..., 0::32] = 0; u[..., 15::32] = rng.choice(tops, u[..., 15::32].shape)
    u[:, 4, 5::8] = rng.choice(tops, u[:, 4, 5::8].shape)
    w[:, :6] = 0; w[:, :6, 0] = 16; w[:, :6, 1] = 1; h[:, :6, 0] = u >> 4; h[:, :6, 1] = u & 15
    m[:, 0] = False; m[:, 1] = True; m[:, 2] = False; m[:, 2, W - 1] = True; m[:, 3] = True; m[:, 3, W - 1] = False; m[:, 4] = False; m[:, 4, 1] = True; m[:, 4, W - 16] = True
    t[:, 0:4:2] = rng.integers(0, 900, (N, 2, 16, 1)); t[:, 1] = rng.choice(np.array([0, 4096]), (N, 16, 1)); t[:, 5] = 0; t[:, 6] = 4096
    w[:, 7] = 255 - rng.integers(0, 16, (N, 16, 1)); h[:, 7] = 255 - rng.integers(0, 24, (N, 16, P)); w[0, 7] = 255; h[0, 7, :, 0::32] = 255
    return pack(h, w, t, m, o, r)
def setup_inputs_ties(rng):
    h, w, t, m, o, r = parts(rng)
    unit = rng.choice(np.array([8, 16]), (N, 8, 1, 1)); h = unit * (h // unit); r = unit * (r // unit)
    t = unit * (t // unit) + rng.choice(np.array([0, 0, 0, 1, -1]), t.shape)
    w[:, :2] = 0; m[:, :2, :16] = True; h[:, 1, :, :16] = 0; h[:, 1, 0, 1:16:2] = 1
    i = np.arange(16)
    for q in range(N):
        t[q, 0, :, 0] = np.sum(np.abs(r[q, 0][:, o[q, 0, :, 0]] - h[q, 0, :, 0:1]), axis=0)
        t[q, 1, :, 0] = np.sum(np.abs(r[q, 1][:, o[q, 1, i, i]] - h[q, 1, :, :16]), axis=0) + (i % 2 == 0)
    return pack(h, w, t, m, o, r)
def setup_inputs_alike(rng):
    h, w, t, m, o, r = parts(rng)
    o[:, ::2] = rng.choice(np.array([0, R - 1, R // 2, 3]), (N, 4, 16, W)); o[:, 1::4] = o[:, 1::4, :1].copy()
    r[..., 0] = 0; r[..., R - 1] = 255
    h[..., 0::7] = 0; h[..., 1::7] = 255; h[..., 3::7] = r[..., R // 2][..., None]
    t[:, 2] = 1
    t[:, 4] = 4080; t[:, 4, 1::4] = rng.choice(np.array([4081, 4096]), (N, 4, 1)); o[:, 4, 1::4] = R - 1; o[:, 4, 12] = 3
    t[:, 6] = 0; o[:, 6, 1::4] = R // 2; o[:, 6, 0] = 3
    return pack(h, w, t, m, o, r)
def setup_inputs_spread(rng):
    h, w, t, m, o, r = parts(rng)
    h = (np.exp2(8 * rng.random((N, 8, 1, P))) * rng.random((N, 8, 16, P))).astype(np.int64)
    r = (np.exp2(8 * rng.random((N, 8, 1, R))) * rng.random((N, 8, 16, R))).astype(np.int64)
    w = np.minimum(np.exp2(8 * rng.random((N, 8, 16, 1))).astype(np.int64), 255)
    t = np.minimum(np.exp2(12 * rng.random((N, 8, 16, 1))).astype(np.int64), 4096)
    m = rng.random((N, 8, W)) < np.exp2(-8 * rng.random((N, 8, 1)))
    o = np.minimum((R * rng.random((N, 8, 16, W)) ** 3).astype(np.int64), R - 1)
    return pack(h, w, t, m, o, r)
def check_inputs(d):
    bad = []
    for k, hi in (("h0", 255), ("w", 255), ("th", 4096), ("marks", 1), ("owner", R - 1), ("hdr", 255)):
        v = np.asarray(d[k]).astype(np.float32)
        if not np.all((v >= 0) & (v <= hi) & (v == np.floor(v))): bad.append("range of " + k)
    if not np.all(np.asarray(d["marks"])[..., 0] == 1): bad.append("address 0 is a boundary")
    return bad
def reference(h0, w, th, marks, owner, hdr):
    h = h0.astype(np.float32).astype(np.int64).reshape(N, 8, 16, P); wt = w.astype(np.float32).astype(np.int64).reshape(N, 8, 16, 1)
    t = th.astype(np.int64).reshape(N, 8, 1, 16); m = marks > 0; o = owner.astype(np.int64).reshape(N, 8, 16, W)
    r = hdr.astype(np.float32).astype(np.int32).reshape(N, 8, 16, R)
    port = np.arange(P) & 15; slot = np.arange(16)
    for step in range(STEPS):
        u = np.add.reduce(wt * h, axis=2) & 4095
        x = ((((u * u) >> 5) + u) & (W - 16)) + port
        top = np.maximum.accumulate(np.where(m, np.arange(W), 0), axis=2)
        a = np.take_along_axis(top, x, 2); b = np.take_along_axis(top, (a - 1) & (W - 1), 2)
        ra = np.take_along_axis(o, a[:, :, None, :], 3); rb = np.take_along_axis(o, b[:, :, None, :], 3)
        new = []
        for q in range(N):
            ids = np.ascontiguousarray(ra[q].transpose(0, 2, 1)).reshape(8, 1, P * 16)
            v = np.take_along_axis(r[q], ids, 2).reshape(8, 16, P, 16)
            d = np.add.reduce(np.abs(v - h[q][..., None]), axis=1)
            n = np.where(d < t[q], slot, (d >> 2) & 15)
            e = np.zeros((8, P), np.int64) + port
            for hop in range(HOPS):
                e = np.take_along_axis(n, e[..., None], 2)[..., 0]
            done = np.take_along_axis(n, e[..., None], 2)[..., 0] == e
            ve = np.take_along_axis(v, e[:, None, :, None], 3)[..., 0]
            new.append(np.where(done[:, None, :], (h[q] + ve) >> 1, np.abs(h[q] - ve)))
            col = np.where(slot[None, :, None] == e[:, None, :], rb[q], ra[q])
            for g in range(8):
                lanes = np.flatnonzero(~done[g])
                xs, first = np.unique(x[q, g, lanes], return_index=True)
                o[q, g][:, xs] = col[g][:, lanes[first]]
                m[q, g, xs] = True
        h = np.roll(np.stack(new), SHIFT, axis=0)
    return {"yh": h.reshape(N, 128, P).astype(np.float32).astype(BF), "yo": o.reshape(N, 128, W).astype(np.float32), "ym": m.astype(np.float32)}

@@ -1,0 +1,408 @@
+from concourse.mybir import dt, AluOpType, AxisListType, ActivationFunctionType
+
+N, W, R, P, STEPS, SHIFT = 6, 1024, 8192, 512, 3, 2
+F32, BF, I32, U16 = "float32", "bfloat16", "int32", "uint16"
+SCRATCH = {}
+
+
+def sb(dtype, cols, names):
+    for n in names.split():
+        SCRATCH[n] = ("psum" if n[0] == "p" and n[1].isupper() else "sbuf", [128, cols], dtype)
+
+
+sb(BF, R, "hdrS")
+sb(I32, W, "owS mkS")
+sb(F32, W, "o4 o5 FW G NM MF AL sg yoS ymS pM Wg WT")
+sb(BF, W, "mkB")
+sb(F32, W + 128, "TB")
+sb(F32, W + 16, "FB")
+sb(BF, 2048, "S WS U")
+sb(BF, 128, "ones rep8 bones idn idh idm tmpa tmpc")
+sb(BF, 16, "wS g8 g8w tmpb")
+sb(I32, 8, "thS pi ci gi")
+sb(F32, 8, "pcol ncol gcol coef thc fth")
+sb(F32, 256, "jmod DIAG RST rst8 ls")
+sb(F32, 32, "bpar b16 ne nb base ep0 dmp dump pmd kb one32 e0 thr0 xmd p4 thr ge dq pr ep eqn win m1 off")
+sb(F32, P, "pU pD pE pK pX pB gm sc ra dr tt y")
+sb(BF, P, "D Rn ab Q hb0 hb1 hb2 hb3 hn0 hn1 hn2")
+sb(BF, 256, "eq8")
+sb(I32, 32, "ui um uo sq zz qi q")
+sb(BF, 32, "key e done")
+sb(U16, 64, "XL PL OL SL")
+LOADS = ["marks", "owner", "w", "th", "h0", "hdr"]
+SEMAPHORES = ["V", "A", "T", "P"] + ["ld_" + n for n in LOADS] \
+    + [n + str(k) for n in ("arr", "loc") for k in range(STEPS)] + ["st_yo0", "st_yo1", "st_ym", "st_yh"]
+TH_TOP = 4081.0
+HALF = 2041.0 / 4096.0
+BIG = 8388608.0
+CYC, PE, WAKE, DMA, SEND, FLY = 0.83, 0.6, 80, 2000, 1200, 2800
+LOOK, TOL = 300, 60
+
+
+def rank_program(g, core, T, topo):
+    rank = T.rank_of(core)
+    if rank is None:
+        return
+    A, AF = AluOpType, ActivationFunctionType
+    queues = {"V": g.vector, "A": g.scalar, "T": g.tensor, "P": g, "Y": g.sync}
+    nodes = []
+
+    def node(q, emit, reads, writes, cost, lat=0.0, sem=None, early=0.0):
+        nodes.append({"q": q, "emit": emit, "r": reads, "w": writes, "cost": cost, "lat": lat, "sem": sem or (q, 1),
+                      "early": early})
+
+    def op(q, fn, reads, writes, cost):
+        node(q, [(fn, reads)], reads, writes, cost)
+
+    vec = {"tt": g.vector.tensor_tensor, "ts": g.vector.tensor_scalar, "cp": g.vector.tensor_copy,
+           "scan": g.vector.tensor_tensor_scan, "tr": g.vector.transpose, "ms": g.vector.memset}
+
+    def V(name, reads, writes, *args, c=64):
+        op("V", lambda: vec[name](*args), reads.split(), writes.split(), c * CYC)
+
+    def ACT(out, in_, func, reads, writes, c=512, bias=0.0, scale=1.0):
+        op("A", lambda: g.scalar.activation(out, in_, func, bias=bias, scale=scale), reads.split(), writes.split(),
+           c * CYC)
+
+    def MM(items, bank, n=64):
+        emit = [((lambda it=it: g.tensor.matmul(it[0], it[1], it[2], it[3], it[4])), it[5].split()) for it in items]
+        node("T", emit, [r for e in emit for r in e[1]], [bank], len(items) * n * PE)
+
+    def dma(out, in_, sem, reads, writes, lat=DMA, early=0.0):
+        node("Y", [((lambda: g.sync.dma_start(out, in_)), reads)], reads, writes, 60, lat, (sem, 16), early)
+
+    def ga(n):
+        return 60 + 1.5 * n
+
+    def is_bank(r):
+        return r[0] == "p" and r[1].isupper()
+
+    def schedule():
+        lastw, rd = {}, {}
+        preds = []
+        for i, d in enumerate(nodes):
+            ps = set()
+            for r in d["r"]:
+                if r in lastw:
+                    ps.add(lastw[r])
+                if is_bank(r):
+                    ps.update(rd.get(r, ()))
+            for w in d["w"]:
+                if w in lastw:
+                    ps.add(lastw[w])
+                ps.update(rd.get(w, ()))
+            ps.discard(i)
+            preds.append(ps)
+            for r in d["r"]:
+                rd.setdefault(r, []).append(i)
+            for w in d["w"]:
+                lastw[w] = i
+                rd[w] = []
+        n = len(nodes)
+        succ = [[] for _ in range(n)]
+        for i, ps in enumerate(preds):
+            for p in ps:
+                succ[p].append(i)
+        prio = [0.0] * n
+        for i in range(n - 1, -1, -1):
+            d = nodes[i]
+            prio[i] = d["cost"] + d["lat"] + max([prio[s] + WAKE for s in succ[i]] + [0.0])
+        left = [len(p) for p in preds]
+        avail = [0.0] * n
+        ready = [i for i in range(n) if not left[i]]
+        free = {q: 0.0 for q in queues}
+        order = []
+        while ready:
+            st = {i: max(free[nodes[i]["q"]], avail[i]) for i in ready}
+            t = min(st.values())
+            q = nodes[min(ready, key=lambda i: (st[i], i))]["q"]
+            cand = sorted([i for i in ready if nodes[i]["q"] == q and st[i] <= t + LOOK],
+                          key=lambda j: (-prio[j] - nodes[j]["early"], j))
+            i = cand[0]
+            for j in cand:
+                if st[j] <= t + 30 and t + nodes[j]["cost"] <= st[i] + TOL:
+                    i = j
+                    break
+            d = nodes[i]
+            ready.remove(i)
+            order.append(i)
+            free[q] = st[i] + d["cost"]
+            for s in succ[i]:
+                avail[s] = max(avail[s], free[q] + d["lat"] + WAKE)
+                left[s] -= 1
+                if not left[s]:
+                    ready.append(s)
+        return order
+
+    def issue(order):
+        known = {q: {} for q in queues}
+        clock, total, lastw, rd = {}, {}, {}, {}
+
+        def wait_for(q, deps):
+            best = {}
+            for s, v in deps:
+                best[s] = max(v, best.get(s, 0))
+            todo = [(s, v) for s, v in best.items() if known[q].get(s, 0) < v]
+            todo = [d for d in todo if not any(o != d and clock[o].get(d[0], 0) >= d[1] for o in todo)]
+            for s, v in todo:
+                queues[q].wait_ge(T.sem[s], v)
+                for a, b in clock[(s, v)].items():
+                    known[q][a] = max(b, known[q].get(a, 0))
+                known[q][s] = max(v, known[q].get(s, 0))
+
+        for i in order:
+            d = nodes[i]
+            q, (sem, inc) = d["q"], d["sem"]
+            ins = None
+            for j, (fn, reads) in enumerate(d["emit"]):
+                deps = []
+                for r in reads:
+                    if r in lastw:
+                        deps.append(lastw[r])
+                    if is_bank(r):
+                        deps += [x for x in rd.get(r, {}).items() if x[0] != sem]
+                for w in d["w"] if j == 0 else []:
+                    if w in lastw and lastw[w][0] != sem:
+                        deps.append(lastw[w])
+                    deps += [x for x in rd.get(w, {}).items() if x[0] != sem]
+                wait_for(q, deps)
+                ins = fn()
+            if inc == 0:
+                key, rkey = d["remote"]
+                for s, v in (key, rkey):
+                    total[s] = v
+                    clock[(s, v)] = {}
+            else:
+                ins.then_inc(T.sem[sem], inc)
+                total[sem] = total.get(sem, 0) + inc
+                clock[(sem, total[sem])] = dict(known[q])
+                key = rkey = (sem, total[sem])
+            for r in d["r"]:
+                rd.setdefault(r, {})[rkey[0]] = rkey[1]
+            for w in d["w"]:
+                lastw[w] = key
+                rd[w] = {}
+        for s, v in total.items():
+            g.wait_ge(T.sem[s], v)
+
+    def halves(n=512):
+        return [(hf, slice(hf * n, hf * n + n)) for hf in range(2)]
+
+    c1 = slice(0, 1)
+    dma(T.mkS[0:8, :], T.marks[:], "ld_marks", [], ["mkS"], early=9e6)
+    dma(T.owS[:], T.owner[:], "ld_owner", [], ["owS"], 4000, early=8e6)
+    dma(T.wS[:, c1], T.w[:], "ld_w", [], ["wS"], 5000, early=7e6)
+    dma(T.thS[:, c1], T.th[:], "ld_th", [], ["thS"], 5000, early=6e6)
+    dma(T.hb0[:], T.h0[:], "ld_h0", [], ["hb0"], 5500, early=5e6)
+    dma(T.hdrS[:], T.hdr[:], "ld_hdr", [], ["hdrS"], 12000)
+
+    def iota(buf, name, pattern, base, cm, c):
+        op("P", lambda: g.iota(buf, pattern, base, cm, allow_small_or_imprecise_dtypes=True), [], [name], 150 + 2 * c)
+
+    def sel(out, in_, pattern, cmp, base, cm, reads, writes, c):
+        op("P", lambda: g.affine_select(out, in_, pattern, cmp, 0.0, base, cm), [reads], [writes], 170 + 2 * c)
+
+    V("ms", "", "ones", T.ones[:], 1.0)
+    op("P", lambda: g.iota(T.pi[:, c1], [[0, 1]], 0, 1), [], ["pi"], 150)
+    sel(T.tmpc[0:8, :], T.ones[0:8, :], [[1, 128]], A.is_ge, 0, -16, "ones", "tmpc", 128)
+    sel(T.rep8[0:8, :], T.tmpc[0:8, :], [[-1, 128]], A.is_ge, 15, 16, "tmpc", "rep8", 128)
+    V("cp", "mkS", "mkB", T.mkB[0:8, :], T.mkS[0:8, :], c=1024)
+    for hf, cs in halves():
+        MM([(T.pM[:, cs], T.rep8[0:8, :], T.mkB[0:8, cs], True, True, "rep8 mkB")], "pM", 512)
+    for hf, cs in halves():
+        sg = ("pE", "pK")[hf]
+        ACT(T[sg][:], T.pM[:, cs], AF.Copy, "pM", sg, bias=-1.0, scale=2.0)
+        V("ts", "owS", "o4_%d" % hf, T.o4[:, cs], T.owS[:, cs], 4096.0, None, A.add, c=512)
+        V("tt", "o4_%d %s" % (hf, sg), "o5_%d" % hf, T.o5[:, cs], T.o4[:, cs], T[sg][:], A.mult, c=512)
+        ACT(T.TB[:, cs], T.o5[:, cs], AF.Copy, "o5_%d" % hf, "TB", bias=-4096.0)
+
+    def tables(first):
+        for hf, cs in halves():
+            ACT(T.AL[:, cs], T.TB[:, cs], AF.Abs, "TB", "AL%d" % hf)
+        for hf, cs in halves():
+            fs = slice(8 + 512 * hf, 520 + 512 * hf)
+            V("scan", ("AL%d TB" % hf) + (" FB" if hf else ""), "FB", T.FB[:, fs],
+              T.AL[:, cs], T.TB[:, cs], T.FB[:, 519:520] if hf else 0.0, A.min, A.max, c=512)
+        for hf, cs in halves():
+            fs = slice(8 + 512 * hf, 520 + 512 * hf)
+            ACT(T.FW[:, cs], T.FB[:, fs], AF.Copy, "FB", "FW", bias=-16777216.0, scale=4096.0)
+        if first:
+            ACT(T.NM[:], T.pM[:], AF.Copy, "pM", "NM", 1024, bias=1.0, scale=-1.0)
+        else:
+            ACT(T.sg[:], T.TB[:, 0:W], AF.Sign, "TB", "sg", 1024, bias=0.5)
+            ACT(T.pM[:], T.sg[:], AF.Relu, "sg", "pM", 1024)
+            ACT(T.NM[:], T.sg[:], AF.Relu, "sg", "NM", 1024, scale=-1.0)
+        V("cp", "FB", "FBw", T.FB[:, 7:8], T.FB[:, 7 + W:8 + W])
+        V("tt", "FB FBw pM", "MF0", T.MF[:, 0:512], T.FB[:, 7:519], T.pM[:, 0:512], A.mult, c=512)
+        V("tt", "FB pM", "MF1", T.MF[:, 512:], T.FB[:, 519:7 + W], T.pM[:, 512:], A.mult, c=512)
+        V("scan", "NM MF0", "G", T.G[:, 0:512], T.NM[:, 0:512], T.MF[:, 0:512], 0.0, A.mult, A.add, c=512)
+        V("scan", "NM MF1 G", "G", T.G[:, 512:], T.NM[:, 512:], T.MF[:, 512:], T.G[:, 511:512], A.mult, A.add, c=512)
+
+    sel(T.tmpb[:, 0:8], T.ones[:, 0:8], [[-16, 8]], A.is_ge, 0, 1, "ones", "tmpb", 8)
+    sel(T.g8[:, 0:8], T.tmpb[:, 0:8], [[16, 8]], A.is_ge, 15, -1, "tmpb", "g8", 8)
+    iota(T.jmod[:], "jmod", [[0, 16], [1, 16]], 0, 0, 256)
+    sel(T.tmpa[:], T.ones[:], [[-16, 8], [0, 16]], A.is_ge, 0, 1, "ones", "tmpa", 128)
+    sel(T.bones[:], T.tmpa[:], [[16, 8], [0, 16]], A.is_ge, 15, -1, "tmpa", "bones", 128)
+    sel(T.idn[:], T.ones[:], [[-1, 128]], A.is_equal, 0, 1, "ones", "idn", 128)
+    iota(T.bpar[:], "bpar", [[0, 16], [1, 2]], 0, 0, 32)
+    iota(T.b16[:], "b16", [[16, 32]], 0, 0, 32)
+    iota(T.dmp[:], "dmp", [[0, 4], [16, 8]], W, 0, 32)
+    iota(T.kb[:], "kb", [[0, 2], [W, 2], [0, 8]], W, 0, 32)
+    iota(T.rst8[:], "rst8i", [[0, 32], [1, 8]], 0, 0, 256)
+    V("ms", "", "S", T.S[:], 0.0, c=1024)
+    V("ms", "", "WS", T.WS[:], 0.0, c=1024)
+    V("ms", "", "one32", T.one32[:], 1.0)
+    V("ts", "pi", "ci", T.ci[:, c1], T.pi[:, c1], 15, None, A.bitwise_and)
+    V("ts", "pi", "gi", T.gi[:, c1], T.pi[:, c1], 4, 1, A.arith_shift_right, A.bitwise_and)
+    V("cp", "ci", "pcol", T.pcol[:, c1], T.ci[:, c1])
+    V("cp", "gi", "gcol", T.gcol[:, c1], T.gi[:, c1])
+    V("ts", "pcol", "ncol", T.ncol[:, c1], T.pcol[:, c1], -1.0, None, A.mult)
+    V("ts", "gcol", "coef", T.coef[:, c1], T.gcol[:, c1], 32.0, 496.0, A.mult, A.add)
+    V("cp", "thS", "thc", T.thc[:, c1], T.thS[:, c1])
+    V("ts", "thc", "fth", T.fth[:, c1], T.thc[:, c1], TH_TOP, None, A.min)
+    V("ts", "g8 wS", "g8w", T.g8w[:, 0:8], T.g8[:, 0:8], T.wS[:, c1], None, A.mult)
+    for c in range(16):
+        V("cp", "g8w", "WS", T.WS[:, 129 * c:128 * (c + 1):16], T.g8w[:, 0:8])
+    for c in range(16):
+        ACT(T.S[:, 129 * c:128 * (c + 1):16], T.g8[:, 0:8], AF.Copy, "g8", "S", 64)
+    pc = T.pcol[:, c1]
+    V("ts", "jmod pcol", "DIAG", T.DIAG[:], T.jmod[:], pc, None, A.is_equal, c=256)
+    V("ts", "jmod", "RST", T.RST[:], T.jmod[:], 0.0, None, A.not_equal, c=256)
+    V("ts", "bpar gcol", "ne", T.ne[:], T.bpar[:], T.gcol[:, c1], None, A.not_equal)
+    V("ts", "ne coef", "nb", T.nb[:], T.ne[:], T.coef[:, c1], None, A.mult)
+    V("tt", "nb b16", "base", T.base[:], T.nb[:], T.b16[:], A.add)
+    V("ts", "base pcol", "ep0", T.ep0[:], T.base[:], pc, None, A.add)
+    V("ts", "one32 pcol", "e0", T.e0[:], T.one32[:], pc, None, A.mult)
+    V("ts", "one32 thc", "thr0", T.thr0[:], T.one32[:], T.thc[:, c1], None, A.mult)
+    V("ts", "dmp pcol", "dump", T.dump[:], T.dmp[:], pc, None, A.add)
+    V("ts", "dmp", "pmd", T.pmd[:], T.dmp[:], -1.0, None, A.mult)
+    V("ts", "idn", "idh", T.idh[:], T.idn[:], 0.5, None, A.mult)
+    V("ts", "idn", "idm", T.idm[:], T.idn[:], -1.0, None, A.mult)
+    V("ts", "rst8i", "rst8", T.rst8[:], T.rst8[:], 0.0, None, A.not_equal, c=256)
+    for c in range(16):
+        V("ts", "bones DIAG", "U", T.U[:, 128 * c:128 * c + 128], T.bones[:], T.DIAG[:, c:c + 1], None, A.mult)
+    tables(True)
+
+    def blk(buf, c):
+        return buf[:, 128 * c:128 * c + 128]
+
+    def spread(src, name, bank):
+        MM([(T[bank][:, c::16], blk(T.U, c), src[:], True, True, "U " + name) for c in range(16)], bank)
+
+    dst = T.cores[(rank + SHIFT) % N]
+    rid, pid, _ = topo.addr(dst)
+    emask = topo.mask(core, dst)
+    n_eng = len(topo.engines(core, dst))
+    Fwin, FWwin, Gwin = T.FB[:, 8:8 + W], T.FW[:, 0:W], T.G[:, 0:W]
+    XL, PL, OL, SL, zz = T.XL, T.PL, T.OL, T.SL, T.zz
+    xl = XL[:, 0:32]
+
+    for k in range(STEPS):
+        hN = "hb%d" % k
+        h = T[hN]
+        MM([(T.pU[:, 0:32], blk(T.WS, c), h[:, c::16], c == 0, c == 15, "WS " + hN) for c in range(16)], "pU")
+        V("cp", "pU", "ui", T.ui[:], T.pU[:, 0:32])
+        V("ts", "ui", "um", T.um[:], T.ui[:], 4095, None, A.bitwise_and)
+        V("ts", "um", "uo", T.uo[:], T.um[:], 32.0, None, A.add)
+        V("tt", "um uo", "sq", T.sq[:], T.um[:], T.uo[:], A.mult)
+        V("ts", "sq", "zz", zz[:], T.sq[:], 5, W - 16, A.arith_shift_right, A.bitwise_and)
+        V("ts", "zz pcol", "XL", XL[:, 0:32], zz[:], pc, None, A.add)
+        V("ts", "zz pcol", "XS", XL[:, 32::2], zz[:, 1::2], pc, None, A.add)
+        V("ts", "zz pcol", "XS", XL[:, 33::2], zz[:, 0::2], pc, None, A.add)
+        for a, ws in halves(16):
+            V("tt", "FB XL DIAG", "gm%d" % a, T.gm[:, 256 * a:256 * a + 256], Fwin.indirect(XL[:, ws]), T.DIAG[:], A.mult,
+              c=ga(256) / CYC)
+        for a in range(2):
+            ACT(T.Wg[:, 512 * a:512 * a + 512], FWwin.indirect(XL[:, 32 * a:32 * a + 32]), AF.Identity,
+                "FW fth " + ("XL", "XS")[a], "Wg%d" % a, ga(512) / CYC, bias=T.fth[:, c1])
+            V("tr", "Wg%d" % a, "WT", T.WT[:, 512 * a:512 * a + 512], T.Wg[:, 512 * a:512 * a + 512], c=512)
+        ACT(T.ra[:], Fwin.indirect(xl), AF.Copy, "FB XL", "ra", ga(512) / CYC)
+        V("tt", "zz kb", "key", T.key[:], zz[:], T.kb[:], A.add)
+        V("tt", "zz pmd", "xmd", T.xmd[:], zz[:], T.pmd[:], A.add)
+        it = []
+        for j in range(8):
+            it.append((T.pB[:, j:256:8], T.idn[:], T.key[:], True, j == 0, "idn key"))
+            if j:
+                it.append((T.pB[:, 9 * j:256:8], T.idm[:], T.key[:, 0:32 - j], False, True, "idm key"))
+        MM(it, "pB")
+        V("ts", "pB", "eq8", T.eq8[:], T.pB[:, 0:256], 0.0, None, A.is_equal, c=256)
+
+        for hop in range(4):
+            e, eN = (T.e0, "e0") if hop == 0 else (T.e, "e")
+            ep, epN = (T.ep0, "ep0") if hop == 0 else (T.ep, "ep")
+            thr, thN = (T.thr0, "thr0") if hop == 0 else (T.thr, "thr")
+            for a, ws in halves(16):
+                cs = slice(256 * a, 256 * a + 256)
+                if hop:
+                    V("tt", "WT OL DIAG", "gm%d" % a, T.gm[:, cs], T.WT[:, 0:W].indirect(OL[:, ws]), T.DIAG[:], A.mult,
+                      c=ga(256) / CYC)
+                V("scan", "RST gm%d" % a, "sc%d" % a, T.sc[:, cs], T.RST[:], T.gm[:, cs], 0.0, A.mult, A.add, c=256)
+                sc15 = T.sc[:, 256 * a + 15:256 * a + 256:16]
+                if hop == 0:
+                    V("cp", "sc%d" % a, "PL%d" % a, PL[:, ws], sc15)
+                else:
+                    V("ts", "sc%d" % a, "PL%d" % a, PL[:, ws], sc15, 1.0 / 4096.0, 4096.0 - HALF, A.mult, A.add)
+                V("tt", "hdrS PL%d %s" % (a, hN), "D%d" % a, T.D[:, cs], T.hdrS[:, 0:R].indirect(PL[:, ws]), h[:, cs],
+                  A.subtract, c=ga(256) / CYC)
+                ACT(T.Rn[:, cs], T.D[:, cs], AF.Abs, "D%d" % a, "Rn%d" % a, 256)
+            MM([(T.pD[:, 0:32], blk(T.S, c), T.Rn[:, c::16], c == 0, c == 15, "S Rn0 Rn1") for c in range(16)], "pD")
+            if hop:
+                V("ts", "PL0 PL1", "p4", T.p4[:], PL[:, 0:32], -4096.0, 4096.0, A.add, A.mult)
+                V("tt", "sc0 sc1 p4", "thr", T.thr[:], T.sc[:, 15::16], T.p4[:], A.subtract)
+            V("cp", "pD", "qi", T.qi[:], T.pD[:, 0:32])
+            V("tt", "pD " + thN, "ge", T.ge[:], T.pD[:, 0:32], thr[:], A.is_ge if hop < 3 else A.is_lt)
+            V("ts", "qi", "q", T.q[:], T.qi[:], 2, 15, A.arith_shift_right, A.bitwise_and)
+            if hop < 3:
+                V("tt", "q " + eN, "dq", T.dq[:], T.q[:], e[:], A.subtract)
+                V("tt", "dq ge", "pr", T.pr[:], T.dq[:], T.ge[:], A.mult)
+                V("tt", "pr " + epN, "ep", T.ep[:], T.pr[:], ep[:], A.add)
+                V("cp", "ep", "OL", OL[:, 0:32], T.ep[:])
+                V("tt", "pr " + eN, "e", T.e[:], T.pr[:], e[:], A.add)
+            else:
+                V("tt", "q e", "eqn", T.eqn[:], T.q[:], T.e[:], A.is_equal)
+                V("tt", "ge eqn", "done", T.done[:], T.ge[:], T.eqn[:], A.max)
+            if hop == 2:
+                spread(T.e, "e", "pE")
+                ACT(T.ab[:], T.pE[:], AF.Abs, "pE ncol", "ab", bias=T.ncol[:, c1])
+                ACT(T.pK[:], T.ab[:], AF.Relu, "ab", "pK", bias=1.0, scale=-1.0)
+                V("tt", "G XL ra", "dr", T.dr[:], Gwin.indirect(xl), T.ra[:], A.subtract, c=ga(512) / CYC)
+                V("tt", "dr pK", "tt", T.tt[:], T.dr[:], T.pK[:], A.mult, c=512)
+
+        spread(T.done, "done", "pE")
+        MM([(T.pX[:], T.idn[:], h[:], True, False, "idn " + hN),
+            (T.pX[:], T.idh[:], T.D[:], False, True, "idh D0 D1")], "pX", 512)
+        ACT(T.y[:], T.pX[:], AF.Identity, "pX", "y", bias=BIG, scale=1.0 - 2.0 ** -11)
+        ACT(T.pB[:], T.y[:], AF.Copy, "y", "pB", bias=-BIG)
+        V("tt", "pB Rn0 Rn1", "Q", T.Q[:], T.pB[:], T.Rn[:], A.subtract, c=512)
+        hn, nx, arr, loc = "hn%d" % k, "hb%d" % (k + 1), "arr%d" % k, "loc%d" % k
+        for a, cs in halves(256):
+            V("tt", "Q pE pX", "t2_%d" % a, T.pX[:, cs], T.Q[:, cs], T.pE[:, cs], A.mult, c=256)
+        for a, cs in halves(256):
+            V("tt", "t2_%d pX Rn%d" % (a, a), hn, T[hn][:, cs], T.pX[:, cs], T.Rn[:, cs], A.add, c=256)
+        node("P", [((lambda hn=hn, nx=nx, arr=arr, loc=loc: g.remote_dma(
+            T[nx][:], T[hn][:], T.sem[arr], T.sem[loc], pid, rid, emask)), [hn])], [hn], [nx], SEND, FLY, (arr, 0))
+        nodes[-1]["remote"] = [(arr, n_eng), (loc, n_eng)]
+        MM([(T.pU[:, 0:256], T.idn[:], T.eq8[:], True, False, "idn eq8")]
+           + [(T.pU[:, 9 * j:256:8], T.idm[:], T.done[:, 0:32 - j], False, j == 7, "idm done")
+              for j in range(1, 8)], "pU")
+        V("scan", "rst8 pU", "ls", T.ls[:], T.rst8[:], T.pU[:, 0:256], 0.0, A.mult, A.max, c=256)
+        V("ts", "done", "win", T.win[:], T.done[:], 0.0, None, A.is_equal)
+        V("tt", "win ls", "win", T.win[:], T.win[:], T.ls[:, 7::8], A.is_gt)
+        V("tt", "win xmd", "m1", T.m1[:], T.win[:], T.xmd[:], A.mult)
+        V("tt", "m1 dump", "off", T.off[:], T.m1[:], T.dump[:], A.add)
+        V("cp", "off", "SL", SL[:, 0:32], T.off[:])
+        for j in reversed(range(4)):
+            cs = slice(128 * j, 128 * j + 128)
+            V("tt", "SL tt ra TB", "TB", T.TB[:, 0:W + 128].indirect(SL[:, 8 * j:8 * j + 8]),
+              T.tt[:, cs], T.ra[:, cs], A.add, c=(50 + 128 * 2.9) / CYC)
+        if k < STEPS - 1:
+            tables(False)
+
+    for hf, cs in halves():
+        ACT(T.AL[:, cs], T.TB[:, cs], AF.Abs, "TB", "AL%d" % hf, bias=4096.0)
+        V("ts", "AL%d" % hf, "yoS%d" % hf, T.yoS[:, cs], T.AL[:, cs], -4096.0, None, A.add, c=512)
+        dma(T.yo[:, cs], T.yoS[:, cs], "st_yo%d" % hf, ["yoS%d" % hf], [])
+    V("ts", "TB", "ymS", T.ymS[:], T.TB[:, 0:W], 0.0, None, A.is_ge, c=1024)
+    dma(T.ym[:], T.ymS[0::16, :], "st_ym", ["ymS"], [])
+    dma(T.yh[:], T["hb%d" % STEPS][:], "st_yh", ["hb%d" % STEPS], [])
+    issue(schedule())

@@ -11,31 +11,34 @@ def sb(dtype, cols, names):
 
 
 sb(BF, R, "hdrS")
-sb(I32, W, "owS mkS")
-sb(F32, W, "o4 o5 FW G NM MF AL sg yoS ymS pM Wg WT")
-sb(BF, W, "mkB")
+sb(I32, W, "owS")
+sb(I32, 64, "mkS")
+sb(BF, 64, "mkB")
+sb(F32, W, "o4 G MF AL yoS ymS")
 sb(F32, W + 128, "TB")
 sb(F32, W + 16, "FB")
 sb(BF, 2048, "S WS U")
-sb(BF, 128, "ones rep8 bones idn idh idm tmpa tmpc")
-sb(BF, 16, "wS g8 g8w tmpb")
-sb(I32, 8, "thS pi ci gi")
-sb(F32, 8, "pcol ncol gcol coef thc fth")
+sb(BF, 128, "ones bones idn idh idm tmpa LT")
+sb(F32, 128, "idf")
+sb(BF, 16, "wS g8 tmpb R3 R3b")
+sb(F32, 8, "g8f")
+sb(I32, 8, "thS pi ci ta tb")
+sb(F32, 8, "pcol ncol taf tbf s32 wa wb wc wd")
 sb(F32, 256, "jmod DIAG RST rst8 ls")
-sb(F32, 32, "bpar b16 ne nb base ep0 dmp dump pmd kb one32 e0 thr0 xmd p4 thr ge dq pr ep eqn win m1 off")
-sb(F32, P, "pU pD pE pK pX pB gm sc ra dr tt y")
-sb(BF, P, "D Rn ab Q hb0 hb1 hb2 hb3 hn0 hn1 hn2")
+sb(F32, 32, "base ep0 e0 thr0 dmp dump pmd kb lan lane xmd thr ge pr av ep e hl win m1 off")
+sb(F32, P, "pU pD pP pW pE pK pR0 pR1 gm sc ra WT dr tt y")
+sb(BF, P, "D ab THW THg hb0 hb1 hb2 hb3 hn0 hn1 hn2")
+sb(BF, W, "RB")
 sb(BF, 256, "eq8")
-sb(I32, 32, "ui um uo sq zz qi q")
-sb(BF, 32, "key e done")
-sb(U16, 64, "XL PL OL SL")
+sb(I32, 32, "ui um uo sq zz qm q")
+sb(BF, 32, "key ew nd")
+sb(U16, 32, "XL PL OL OL0 SL HL")
 LOADS = ["marks", "owner", "w", "th", "h0", "hdr"]
 SEMAPHORES = ["V", "A", "T", "P"] + ["ld_" + n for n in LOADS] \
     + [n + str(k) for n in ("arr", "loc") for k in range(STEPS)] + ["st_yo0", "st_yo1", "st_ym", "st_yh"]
-TH_TOP = 4081.0
-HALF = 2041.0 / 4096.0
+OFF = 4096.0
 BIG = 8388608.0
-CYC, PE, WAKE, DMA, SEND, FLY = 0.83, 0.6, 80, 2000, 1200, 2800
+CYC, PE, GATHER, SCATTER, WAKE, DMA, SEND, FLY = 1.04, 0.53, 1.56, 3.8, 80, 2000, 1200, 3300
 LOOK, TOL = 300, 60
 
 
@@ -55,7 +58,7 @@ def rank_program(g, core, T, topo):
         node(q, [(fn, reads)], reads, writes, cost)
 
     vec = {"tt": g.vector.tensor_tensor, "ts": g.vector.tensor_scalar, "cp": g.vector.tensor_copy,
-           "scan": g.vector.tensor_tensor_scan, "tr": g.vector.transpose, "ms": g.vector.memset}
+           "scan": g.vector.tensor_tensor_scan, "ms": g.vector.memset}
 
     def V(name, reads, writes, *args, c=64):
         op("V", lambda: vec[name](*args), reads.split(), writes.split(), c * CYC)
@@ -72,7 +75,7 @@ def rank_program(g, core, T, topo):
         node("Y", [((lambda: g.sync.dma_start(out, in_)), reads)], reads, writes, 60, lat, (sem, 16), early)
 
     def ga(n):
-        return 60 + 1.5 * n
+        return 60 + GATHER * n
 
     def is_bank(r):
         return r[0] == "p" and r[1].isupper()
@@ -188,103 +191,105 @@ def rank_program(g, core, T, topo):
     def halves(n=512):
         return [(hf, slice(hf * n, hf * n + n)) for hf in range(2)]
 
+    def blk(buf, c):
+        return buf[:, 128 * c:128 * c + 128]
+
     c1 = slice(0, 1)
-    dma(T.mkS[0:8, :], T.marks[:], "ld_marks", [], ["mkS"], early=9e6)
+    dma(T.mkS[:], T.marks[:], "ld_marks", [], ["mkS"], early=9e6)
     dma(T.owS[:], T.owner[:], "ld_owner", [], ["owS"], 4000, early=8e6)
-    dma(T.wS[:, c1], T.w[:], "ld_w", [], ["wS"], 5000, early=7e6)
-    dma(T.thS[:, c1], T.th[:], "ld_th", [], ["thS"], 5000, early=6e6)
-    dma(T.hb0[:], T.h0[:], "ld_h0", [], ["hb0"], 5500, early=5e6)
+    dma(T.wS[:, c1], T.w[:], "ld_w", [], ["wS"], 4200, early=7e6)
+    dma(T.thS[:, c1], T.th[:], "ld_th", [], ["thS"], 4200, early=6e6)
+    dma(T.hb0[:], T.h0[:], "ld_h0", [], ["hb0"], 4700, early=5e6)
     dma(T.hdrS[:], T.hdr[:], "ld_hdr", [], ["hdrS"], 12000)
 
     def iota(buf, name, pattern, base, cm, c):
-        op("P", lambda: g.iota(buf, pattern, base, cm, allow_small_or_imprecise_dtypes=True), [], [name], 150 + 2 * c)
+        op("P", lambda: g.iota(buf, pattern, base, cm, allow_small_or_imprecise_dtypes=True), [], [name], 160 + 2 * c)
 
     def sel(out, in_, pattern, cmp, base, cm, reads, writes, c):
-        op("P", lambda: g.affine_select(out, in_, pattern, cmp, 0.0, base, cm), [reads], [writes], 170 + 2 * c)
+        op("P", lambda: g.affine_select(out, in_, pattern, cmp, 0.0, base, cm), [reads], [writes], 210 + 2 * c)
 
+    pc = T.pcol[:, c1]
     V("ms", "", "ones", T.ones[:], 1.0)
-    op("P", lambda: g.iota(T.pi[:, c1], [[0, 1]], 0, 1), [], ["pi"], 150)
-    sel(T.tmpc[0:8, :], T.ones[0:8, :], [[1, 128]], A.is_ge, 0, -16, "ones", "tmpc", 128)
-    sel(T.rep8[0:8, :], T.tmpc[0:8, :], [[-1, 128]], A.is_ge, 15, 16, "tmpc", "rep8", 128)
-    V("cp", "mkS", "mkB", T.mkB[0:8, :], T.mkS[0:8, :], c=1024)
-    for hf, cs in halves():
-        MM([(T.pM[:, cs], T.rep8[0:8, :], T.mkB[0:8, cs], True, True, "rep8 mkB")], "pM", 512)
-    for hf, cs in halves():
-        sg = ("pE", "pK")[hf]
-        ACT(T[sg][:], T.pM[:, cs], AF.Copy, "pM", sg, bias=-1.0, scale=2.0)
-        V("ts", "owS", "o4_%d" % hf, T.o4[:, cs], T.owS[:, cs], 4096.0, None, A.add, c=512)
-        V("tt", "o4_%d %s" % (hf, sg), "o5_%d" % hf, T.o5[:, cs], T.o4[:, cs], T[sg][:], A.mult, c=512)
-        ACT(T.TB[:, cs], T.o5[:, cs], AF.Copy, "o5_%d" % hf, "TB", bias=-4096.0)
-
-    def tables(first):
-        for hf, cs in halves():
-            ACT(T.AL[:, cs], T.TB[:, cs], AF.Abs, "TB", "AL%d" % hf)
-        for hf, cs in halves():
-            fs = slice(8 + 512 * hf, 520 + 512 * hf)
-            V("scan", ("AL%d TB" % hf) + (" FB" if hf else ""), "FB", T.FB[:, fs],
-              T.AL[:, cs], T.TB[:, cs], T.FB[:, 519:520] if hf else 0.0, A.min, A.max, c=512)
-        for hf, cs in halves():
-            fs = slice(8 + 512 * hf, 520 + 512 * hf)
-            ACT(T.FW[:, cs], T.FB[:, fs], AF.Copy, "FB", "FW", bias=-16777216.0, scale=4096.0)
-        if first:
-            ACT(T.NM[:], T.pM[:], AF.Copy, "pM", "NM", 1024, bias=1.0, scale=-1.0)
-        else:
-            ACT(T.sg[:], T.TB[:, 0:W], AF.Sign, "TB", "sg", 1024, bias=0.5)
-            ACT(T.pM[:], T.sg[:], AF.Relu, "sg", "pM", 1024)
-            ACT(T.NM[:], T.sg[:], AF.Relu, "sg", "NM", 1024, scale=-1.0)
-        V("cp", "FB", "FBw", T.FB[:, 7:8], T.FB[:, 7 + W:8 + W])
-        V("tt", "FB FBw pM", "MF0", T.MF[:, 0:512], T.FB[:, 7:519], T.pM[:, 0:512], A.mult, c=512)
-        V("tt", "FB pM", "MF1", T.MF[:, 512:], T.FB[:, 519:7 + W], T.pM[:, 512:], A.mult, c=512)
-        V("scan", "NM MF0", "G", T.G[:, 0:512], T.NM[:, 0:512], T.MF[:, 0:512], 0.0, A.mult, A.add, c=512)
-        V("scan", "NM MF1 G", "G", T.G[:, 512:], T.NM[:, 512:], T.MF[:, 512:], T.G[:, 511:512], A.mult, A.add, c=512)
-
-    sel(T.tmpb[:, 0:8], T.ones[:, 0:8], [[-16, 8]], A.is_ge, 0, 1, "ones", "tmpb", 8)
-    sel(T.g8[:, 0:8], T.tmpb[:, 0:8], [[16, 8]], A.is_ge, 15, -1, "tmpb", "g8", 8)
-    iota(T.jmod[:], "jmod", [[0, 16], [1, 16]], 0, 0, 256)
+    op("P", lambda: g.iota(T.pi[:, c1], [[0, 1]], 0, 1), [], ["pi"], 160)
     sel(T.tmpa[:], T.ones[:], [[-16, 8], [0, 16]], A.is_ge, 0, 1, "ones", "tmpa", 128)
     sel(T.bones[:], T.tmpa[:], [[16, 8], [0, 16]], A.is_ge, 15, -1, "tmpa", "bones", 128)
     sel(T.idn[:], T.ones[:], [[-1, 128]], A.is_equal, 0, 1, "ones", "idn", 128)
-    iota(T.bpar[:], "bpar", [[0, 16], [1, 2]], 0, 0, 32)
-    iota(T.b16[:], "b16", [[16, 32]], 0, 0, 32)
+    iota(T.jmod[:], "jmod", [[0, 16], [1, 16]], 0, 0, 256)
+    iota(T.base[:], "base", [[16, 32]], 0, 0, 32)
     iota(T.dmp[:], "dmp", [[0, 4], [16, 8]], W, 0, 32)
     iota(T.kb[:], "kb", [[0, 2], [W, 2], [0, 8]], W, 0, 32)
     iota(T.rst8[:], "rst8i", [[0, 32], [1, 8]], 0, 0, 256)
-    V("ms", "", "S", T.S[:], 0.0, c=1024)
-    V("ms", "", "WS", T.WS[:], 0.0, c=1024)
-    V("ms", "", "one32", T.one32[:], 1.0)
+    g8 = T.bones[:, 0::16]
     V("ts", "pi", "ci", T.ci[:, c1], T.pi[:, c1], 15, None, A.bitwise_and)
-    V("ts", "pi", "gi", T.gi[:, c1], T.pi[:, c1], 4, 1, A.arith_shift_right, A.bitwise_and)
-    V("cp", "ci", "pcol", T.pcol[:, c1], T.ci[:, c1])
-    V("cp", "gi", "gcol", T.gcol[:, c1], T.gi[:, c1])
-    V("ts", "pcol", "ncol", T.ncol[:, c1], T.pcol[:, c1], -1.0, None, A.mult)
-    V("ts", "gcol", "coef", T.coef[:, c1], T.gcol[:, c1], 32.0, 496.0, A.mult, A.add)
-    V("cp", "thS", "thc", T.thc[:, c1], T.thS[:, c1])
-    V("ts", "thc", "fth", T.fth[:, c1], T.thc[:, c1], TH_TOP, None, A.min)
-    V("ts", "g8 wS", "g8w", T.g8w[:, 0:8], T.g8[:, 0:8], T.wS[:, c1], None, A.mult)
-    for c in range(16):
-        V("cp", "g8w", "WS", T.WS[:, 129 * c:128 * (c + 1):16], T.g8w[:, 0:8])
-    for c in range(16):
-        ACT(T.S[:, 129 * c:128 * (c + 1):16], T.g8[:, 0:8], AF.Copy, "g8", "S", 64)
-    pc = T.pcol[:, c1]
+    V("cp", "ci", "pcol", pc, T.ci[:, c1])
     V("ts", "jmod pcol", "DIAG", T.DIAG[:], T.jmod[:], pc, None, A.is_equal, c=256)
+    for c in range(16):
+        ACT(blk(T.U, c), T.bones[:], AF.Identity, "bones DIAG", "U", 128, scale=T.DIAG[:, c:c + 1])
+    V("ms", "", "S", T.S[:], 0.0, c=1024)
+    for c in range(16):
+        ACT(T.S[:, 129 * c:128 * (c + 1):16], g8, AF.Copy, "bones", "S", 64)
+    for hf, cs in halves(1024):
+        V("ts", "S wS", "WS%d" % hf, T.WS[:, cs], T.S[:, cs], T.wS[:, c1], None, A.mult, c=512)
+    V("ts", "mkS", "mkB", T.mkB[:], T.mkS[:], 2.0, -1.0, A.mult, A.add)
+    for hf, cs in halves():
+        bank = "pR%d" % hf
+        MM([(T[bank][:, 64 * c:64 * c + 64], blk(T.U, 8 * hf + c), T.mkB[:], True, True, "U mkB") for c in range(8)],
+           bank)
+        V("ts", "owS", "o4_%d" % hf, T.o4[:, cs], T.owS[:, cs], OFF, None, A.add, c=512)
+        V("tt", "o4_%d %s" % (hf, bank), "TB", T.TB[:, cs], T.o4[:, cs], T[bank][:], A.mult, c=512)
+
+    def tables():
+        for hf, cs in halves():
+            ACT(T["pR%d" % hf][:], T.TB[:, cs], AF.Relu, "TB", "pR%d" % hf, scale=-4.0)
+        for hf, cs in halves():
+            fs = slice(8 + 512 * hf, 520 + 512 * hf)
+            V("scan", ("pR%d TB" % hf) + (" FB" if hf else ""), "FB", T.FB[:, fs],
+              T["pR%d" % hf][:], T.TB[:, cs], T.FB[:, 519:520] if hf else 0.0, A.min, A.max, c=512)
+        V("cp", "FB", "FBw", T.FB[:, 7:8], T.FB[:, 7 + W:8 + W])
+        V("tt", "FB FBw pR0", "MF0", T.MF[:, 0:512], T.FB[:, 7:519], T.pR0[:], A.subtract, c=512)
+        V("tt", "FB pR1", "MF1", T.MF[:, 512:], T.FB[:, 519:7 + W], T.pR1[:], A.subtract, c=512)
+        V("scan", "pR0 MF0", "G", T.G[:, 0:512], T.pR0[:], T.MF[:, 0:512], 0.0, A.min, A.max, c=512)
+        V("scan", "pR1 MF1 G", "G", T.G[:, 512:], T.pR1[:], T.MF[:, 512:], T.G[:, 511:512], A.min, A.max, c=512)
+
+    V("ts", "pcol", "ncol", T.ncol[:, c1], pc, -1.0, None, A.mult)
     V("ts", "jmod", "RST", T.RST[:], T.jmod[:], 0.0, None, A.not_equal, c=256)
-    V("ts", "bpar gcol", "ne", T.ne[:], T.bpar[:], T.gcol[:, c1], None, A.not_equal)
-    V("ts", "ne coef", "nb", T.nb[:], T.ne[:], T.coef[:, c1], None, A.mult)
-    V("tt", "nb b16", "base", T.base[:], T.nb[:], T.b16[:], A.add)
     V("ts", "base pcol", "ep0", T.ep0[:], T.base[:], pc, None, A.add)
-    V("ts", "one32 pcol", "e0", T.e0[:], T.one32[:], pc, None, A.mult)
-    V("ts", "one32 thc", "thr0", T.thr0[:], T.one32[:], T.thc[:, c1], None, A.mult)
+    V("ts", "base pcol", "e0", T.e0[:], T.base[:], 0.0, pc, A.mult, A.add)
+    V("cp", "ep0", "OL0", T.OL0[:], T.ep0[:])
+    V("ts", "ep0", "lane", T.lane[:], T.ep0[:], 1.0 / P, None, A.mult)
     V("ts", "dmp pcol", "dump", T.dump[:], T.dmp[:], pc, None, A.add)
     V("ts", "dmp", "pmd", T.pmd[:], T.dmp[:], -1.0, None, A.mult)
-    V("ts", "idn", "idh", T.idh[:], T.idn[:], 0.5, None, A.mult)
-    V("ts", "idn", "idm", T.idm[:], T.idn[:], -1.0, None, A.mult)
     V("ts", "rst8i", "rst8", T.rst8[:], T.rst8[:], 0.0, None, A.not_equal, c=256)
-    for c in range(16):
-        V("ts", "bones DIAG", "U", T.U[:, 128 * c:128 * c + 128], T.bones[:], T.DIAG[:, c:c + 1], None, A.mult)
-    tables(True)
+    ACT(T.idh[:], T.idn[:], AF.Copy, "idn", "idh", 128, scale=0.5)
+    ACT(T.idm[:], T.idn[:], AF.Copy, "idn", "idm", 128, scale=-1.0)
+    ACT(T.idf[:], T.idn[:], AF.Copy, "idn", "idf", 128)
+    ACT(T.g8f[:], g8, AF.Copy, "bones", "g8f", 64)
+    V("ts", "thS", "ta", T.ta[:, c1], T.thS[:, c1], 8192 - 64, None, A.bitwise_and)
+    V("ts", "thS", "tb", T.tb[:, c1], T.thS[:, c1], 63, None, A.bitwise_and)
+    V("ts", "ta", "taf", T.taf[:, c1], T.ta[:, c1], -1.0, None, A.mult)
+    V("ts", "tb", "tbf", T.tbf[:, c1], T.tb[:, c1], -1.0, None, A.mult)
+    V("ts", "pcol", "s32", T.s32[:, c1], pc, 1.0 / 32, None, A.mult)
+    V("ms", "", "LT", T.LT[:], 0.0)
+    for t, n in enumerate(("taf", "tbf", "s32")):
+        ACT(T.LT[:, t::16], T.ones[:, 0:8], AF.Identity, "ones " + n, "LT", 64, scale=T[n][:, c1])
+    MM([(blk(T.pW, b), T.LT[:], T.idn[:], True, True, "LT idn") for b in range(4)], "pW", 128)
+    ACT(T.THW[:], T.pW[:], AF.Copy, "pW", "THW")
+    V("ts", "pcol", "wc", T.wc[:, c1], pc, 2.0, 32.0, A.is_equal, A.mult)
+    V("ts", "wc", "wb", T.wb[:, c1], T.wc[:, c1], -4.0, None, A.mult)
+    V("ts", "pcol", "wd", T.wd[:, c1], pc, 2.0, -1.0, A.is_lt, A.mult)
+    V("tt", "wb wd", "wa", T.wa[:, c1], T.wb[:, c1], T.wd[:, c1], A.add)
+    ACT(T.R3[:, 0::2], g8, AF.Identity, "bones wa", "R3", 64, scale=T.wa[:, c1])
+    ACT(T.R3[:, 1::2], g8, AF.Identity, "bones wc", "R3", 64, scale=T.wc[:, c1])
+    ACT(T.R3b[:, 0:8], g8, AF.Identity, "bones wb", "R3b", 64, scale=T.wb[:, c1])
+    pT = T.pU[:, 256:320]
 
-    def blk(buf, c):
-        return buf[:, 128 * c:128 * c + 128]
+    def thresholds(lst, lN, out, oN):
+        ACT(T.THg[:], T.THW[:, 0:P].indirect(lst), AF.Copy, "THW " + lN, "THg", ga(512))
+        MM([(T.pU[:, 256:288], blk(T.S, c), T.THg[:, c::16], c == 0, c == 15, "S THg") for c in range(16)], "pU")
+        ACT(out, T.pU[:, 256:288], AF.Copy, "pU", oN, 64, scale=-1.0)
+
+    thresholds(T.OL0[:, 0:32], "OL0", T.thr0[:], "thr0")
+    tables()
 
     def spread(src, name, bank):
         MM([(T[bank][:, c::16], blk(T.U, c), src[:], True, True, "U " + name) for c in range(16)], bank)
@@ -293,39 +298,36 @@ def rank_program(g, core, T, topo):
     rid, pid, _ = topo.addr(dst)
     emask = topo.mask(core, dst)
     n_eng = len(topo.engines(core, dst))
-    Fwin, FWwin, Gwin = T.FB[:, 8:8 + W], T.FW[:, 0:W], T.G[:, 0:W]
-    XL, PL, OL, SL, zz = T.XL, T.PL, T.OL, T.SL, T.zz
-    xl = XL[:, 0:32]
+    Fwin, Gwin = T.FB[:, 8:8 + W], T.G[:, 0:W]
+    XL, PL, OL, SL, HL, zz = T.XL, T.PL, T.OL, T.SL, T.HL, T.zz
+    Rn = T.RB[:, P:]
 
     for k in range(STEPS):
         hN = "hb%d" % k
         h = T[hN]
-        MM([(T.pU[:, 0:32], blk(T.WS, c), h[:, c::16], c == 0, c == 15, "WS " + hN) for c in range(16)], "pU")
+        MM([(T.pU[:, 0:32], blk(T.WS, c), h[:, c::16], c == 0, c == 15, "WS%d %s" % (c // 8, hN)) for c in range(16)],
+           "pU")
         V("cp", "pU", "ui", T.ui[:], T.pU[:, 0:32])
         V("ts", "ui", "um", T.um[:], T.ui[:], 4095, None, A.bitwise_and)
         V("ts", "um", "uo", T.uo[:], T.um[:], 32.0, None, A.add)
         V("tt", "um uo", "sq", T.sq[:], T.um[:], T.uo[:], A.mult)
         V("ts", "sq", "zz", zz[:], T.sq[:], 5, W - 16, A.arith_shift_right, A.bitwise_and)
-        V("ts", "zz pcol", "XL", XL[:, 0:32], zz[:], pc, None, A.add)
-        V("ts", "zz pcol", "XS", XL[:, 32::2], zz[:, 1::2], pc, None, A.add)
-        V("ts", "zz pcol", "XS", XL[:, 33::2], zz[:, 0::2], pc, None, A.add)
+        V("ts", "zz pcol", "XL", XL[:], zz[:], pc, None, A.add)
         for a, ws in halves(16):
-            V("tt", "FB XL DIAG", "gm%d" % a, T.gm[:, 256 * a:256 * a + 256], Fwin.indirect(XL[:, ws]), T.DIAG[:], A.mult,
-              c=ga(256) / CYC)
-        for a in range(2):
-            ACT(T.Wg[:, 512 * a:512 * a + 512], FWwin.indirect(XL[:, 32 * a:32 * a + 32]), AF.Identity,
-                "FW fth " + ("XL", "XS")[a], "Wg%d" % a, ga(512) / CYC, bias=T.fth[:, c1])
-            V("tr", "Wg%d" % a, "WT", T.WT[:, 512 * a:512 * a + 512], T.Wg[:, 512 * a:512 * a + 512], c=512)
-        ACT(T.ra[:], Fwin.indirect(xl), AF.Copy, "FB XL", "ra", ga(512) / CYC)
+            cs = slice(256 * a, 256 * a + 256)
+            ACT(T.ra[:, cs], Fwin.indirect(XL[:, ws]), AF.Copy, "FB XL", "ra%d" % a, ga(256))
+            MM([(blk(T.pW, b), blk(T.ra, b), T.idf[:], True, True, "idf ra%d" % a) for b in (2 * a, 2 * a + 1)],
+               "pW", 512)
+        ACT(T.WT[:], T.pW[:], AF.Copy, "pW", "WT")
         V("tt", "zz kb", "key", T.key[:], zz[:], T.kb[:], A.add)
         V("tt", "zz pmd", "xmd", T.xmd[:], zz[:], T.pmd[:], A.add)
         it = []
         for j in range(8):
-            it.append((T.pB[:, j:256:8], T.idn[:], T.key[:], True, j == 0, "idn key"))
+            it.append((T.pE[:, j:256:8], T.idn[:], T.key[:], True, j == 0, "idn key"))
             if j:
-                it.append((T.pB[:, 9 * j:256:8], T.idm[:], T.key[:, 0:32 - j], False, True, "idm key"))
-        MM(it, "pB")
-        V("ts", "pB", "eq8", T.eq8[:], T.pB[:, 0:256], 0.0, None, A.is_equal, c=256)
+                it.append((T.pE[:, 9 * j:256:8], T.idm[:], T.key[:, 0:32 - j], False, True, "idm key"))
+        MM(it, "pE")
+        V("ts", "pE", "eq8", T.eq8[:], T.pE[:, 0:256], 0.0, None, A.is_equal, c=256)
 
         for hop in range(4):
             e, eN = (T.e0, "e0") if hop == 0 else (T.e, "e")
@@ -333,74 +335,89 @@ def rank_program(g, core, T, topo):
             thr, thN = (T.thr0, "thr0") if hop == 0 else (T.thr, "thr")
             for a, ws in halves(16):
                 cs = slice(256 * a, 256 * a + 256)
-                if hop:
-                    V("tt", "WT OL DIAG", "gm%d" % a, T.gm[:, cs], T.WT[:, 0:W].indirect(OL[:, ws]), T.DIAG[:], A.mult,
-                      c=ga(256) / CYC)
-                V("scan", "RST gm%d" % a, "sc%d" % a, T.sc[:, cs], T.RST[:], T.gm[:, cs], 0.0, A.mult, A.add, c=256)
-                sc15 = T.sc[:, 256 * a + 15:256 * a + 256:16]
+                win, lst, rds = (T.WT[:, 0:P], OL, "WT OL") if hop else (Fwin, XL, "FB XL")
+                V("tt", rds + " DIAG", "gm%d" % a, T.gm[:, cs], win.indirect(lst[:, ws]), T.DIAG[:], A.mult, c=ga(256))
                 if hop == 0:
-                    V("cp", "sc%d" % a, "PL%d" % a, PL[:, ws], sc15)
+                    V("scan", "RST gm%d" % a, "sc%d" % a, T.sc[:, cs], T.RST[:], T.gm[:, cs], 0.0, A.mult, A.add, c=256)
+                    V("ts", "sc%d" % a, "PL%d" % a, PL[:, ws], T.sc[:, 256 * a + 15:256 * a + 256:16], -OFF, None, A.add)
                 else:
-                    V("ts", "sc%d" % a, "PL%d" % a, PL[:, ws], sc15, 1.0 / 4096.0, 4096.0 - HALF, A.mult, A.add)
+                    MM([(T.pP[:, 8 * b:8 * b + 8], blk(T.gm, b), T.g8f[:], True, True, "g8f gm%d" % a)
+                        for b in (2 * a, 2 * a + 1)], "pP", 256)
+                    V("ts", "pP", "PL%d" % a, PL[:, ws], T.pP[:, ws], -OFF, None, A.add)
+            if hop in (1, 2):
+                thresholds(OL[:, 0:32], "OL", T.thr[:], "thr")
+            elif hop == 3:
+                ACT(T.THg[:], T.THW[:, 0:P].indirect(OL[:, 0:32]), AF.Copy, "THW OL", "THg", ga(512))
+                MM([(T.pU[:, 256 + 16 * b:272 + 16 * b], blk(T.THg, b), T.R3[:], True, True, "R3 THg")
+                    for b in range(4)], "pU")
+                ACT(T.thr[:], T.pU[:, 256:320:2], AF.Copy, "pU", "thr", 64)
+                ACT(T.ew[:], T.pU[:, 257:320:2], AF.Copy, "pU", "ew", 64)
+            for a, ws in halves(16):
+                cs = slice(256 * a, 256 * a + 256)
                 V("tt", "hdrS PL%d %s" % (a, hN), "D%d" % a, T.D[:, cs], T.hdrS[:, 0:R].indirect(PL[:, ws]), h[:, cs],
-                  A.subtract, c=ga(256) / CYC)
-                ACT(T.Rn[:, cs], T.D[:, cs], AF.Abs, "D%d" % a, "Rn%d" % a, 256)
-            MM([(T.pD[:, 0:32], blk(T.S, c), T.Rn[:, c::16], c == 0, c == 15, "S Rn0 Rn1") for c in range(16)], "pD")
-            if hop:
-                V("ts", "PL0 PL1", "p4", T.p4[:], PL[:, 0:32], -4096.0, 4096.0, A.add, A.mult)
-                V("tt", "sc0 sc1 p4", "thr", T.thr[:], T.sc[:, 15::16], T.p4[:], A.subtract)
-            V("cp", "pD", "qi", T.qi[:], T.pD[:, 0:32])
-            V("tt", "pD " + thN, "ge", T.ge[:], T.pD[:, 0:32], thr[:], A.is_ge if hop < 3 else A.is_lt)
-            V("ts", "qi", "q", T.q[:], T.qi[:], 2, 15, A.arith_shift_right, A.bitwise_and)
+                  A.subtract, c=ga(256))
+                ACT(T.RB[:, P + 256 * a:P + 256 * a + 256], T.D[:, cs], AF.Abs, "D%d" % a, "Rn%d" % a, 256)
+                if hop < 3:
+                    MM([(T.pD[:, 8 * b:8 * b + 8], blk(T.RB, 4 + b), g8, True, True, "bones Rn%d" % a)
+                        for b in (2 * a, 2 * a + 1)], "pD")
             if hop < 3:
-                V("tt", "q " + eN, "dq", T.dq[:], T.q[:], e[:], A.subtract)
-                V("tt", "dq ge", "pr", T.pr[:], T.dq[:], T.ge[:], A.mult)
-                V("tt", "pr " + epN, "ep", T.ep[:], T.pr[:], ep[:], A.add)
-                V("cp", "ep", "OL", OL[:, 0:32], T.ep[:])
-                V("tt", "pr " + eN, "e", T.e[:], T.pr[:], e[:], A.add)
-            else:
-                V("tt", "q e", "eqn", T.eqn[:], T.q[:], T.e[:], A.is_equal)
-                V("tt", "ge eqn", "done", T.done[:], T.ge[:], T.eqn[:], A.max)
-            if hop == 2:
-                spread(T.e, "e", "pE")
-                ACT(T.ab[:], T.pE[:], AF.Abs, "pE ncol", "ab", bias=T.ncol[:, c1])
-                ACT(T.pK[:], T.ab[:], AF.Relu, "ab", "pK", bias=1.0, scale=-1.0)
-                V("tt", "G XL ra", "dr", T.dr[:], Gwin.indirect(xl), T.ra[:], A.subtract, c=ga(512) / CYC)
-                V("tt", "dr pK", "tt", T.tt[:], T.dr[:], T.pK[:], A.mult, c=512)
+                V("tt", "pD " + thN, "ge", T.ge[:], T.pD[:, 0:32], thr[:], A.is_ge)
+                V("tt", "pD ge", "qm", T.qm[:], T.pD[:, 0:32], T.ge[:], A.mult)
+                V("tt", "ge " + eN, "pr", T.pr[:], T.ge[:], e[:], A.mult)
+                V("ts", "qm", "q", T.q[:], T.qm[:], 2, 15, A.arith_shift_right, A.bitwise_and)
+                V("tt", "pr " + epN, "av", T.av[:], ep[:], T.pr[:], A.subtract)
+                V("tt", "q av", "ep", T.ep[:], T.q[:], T.av[:], A.add)
+                V("cp", "ep", "OL", OL[:], T.ep[:])
+                if hop < 2:
+                    V("tt", "ep base", "e", T.e[:], T.ep[:], T.base[:], A.subtract)
+        MM([(T.pD[:, 0:32], blk(T.S, c), T.RB[:, P + c::16], c == 0, False, "S Rn0 Rn1") for c in range(16)]
+           + [(T.pD[:, 8 * b:8 * b + 8], blk(T.THg, b), T.R3b[:, 0:8], False, b == 3, "R3b THg") for b in range(4)],
+           "pD")
+        V("ts", "pD", "qm", T.qm[:], T.pD[:, 0:32], 64.0, None, A.add)
+        V("tt", "pD thr", "ge", T.ge[:], T.pD[:, 0:32], T.thr[:], A.is_ge)
+        V("ts", "qm", "q", T.q[:], T.qm[:], 60, None, A.bitwise_and)
+        V("tt", "q ge", "nd", T.nd[:], T.q[:], T.ge[:], A.min)
+        V("tt", "nd lane", "hl", T.hl[:], T.nd[:], T.lane[:], A.add)
+        V("ts", "hl", "HL", HL[:], T.hl[:], float(P), None, A.mult)
+        spread(T.ew, "ew", "pE")
+        ACT(T.ab[:], T.pE[:], AF.Abs, "pE ncol", "ab", bias=T.ncol[:, c1])
+        ACT(T.pK[:], T.ab[:], AF.Relu, "ab", "pK", bias=1.0, scale=-1.0)
+        for a, ws in halves(16):
+            cs = slice(256 * a, 256 * a + 256)
+            V("tt", "G XL ra%d" % a, "dr%d" % a, T.dr[:, cs], Gwin.indirect(XL[:, ws]), T.ra[:, cs], A.subtract,
+              c=ga(256))
+            V("tt", "dr%d pK" % a, "tt%d" % a, T.tt[:, cs], T.dr[:, cs], T.pK[:, cs], A.mult, c=256)
 
-        spread(T.done, "done", "pE")
-        MM([(T.pX[:], T.idn[:], h[:], True, False, "idn " + hN),
-            (T.pX[:], T.idh[:], T.D[:], False, True, "idh D0 D1")], "pX", 512)
-        ACT(T.y[:], T.pX[:], AF.Identity, "pX", "y", bias=BIG, scale=1.0 - 2.0 ** -11)
-        ACT(T.pB[:], T.y[:], AF.Copy, "y", "pB", bias=-BIG)
-        V("tt", "pB Rn0 Rn1", "Q", T.Q[:], T.pB[:], T.Rn[:], A.subtract, c=512)
+        MM([(T.pW[:], T.idn[:], h[:], True, False, "idn " + hN),
+            (T.pW[:], T.idh[:], T.D[:], False, True, "idh D0 D1")], "pW", 512)
+        for a, cs in halves(256):
+            ACT(T.y[:, cs], T.pW[:, cs], AF.Identity, "pW", "y%d" % a, 256, bias=BIG, scale=1.0 - 2.0 ** -11)
+            ACT(T.RB[:, cs], T.y[:, cs], AF.Copy, "y%d" % a, "B%d" % a, 256, bias=-BIG)
         hn, nx, arr, loc = "hn%d" % k, "hb%d" % (k + 1), "arr%d" % k, "loc%d" % k
-        for a, cs in halves(256):
-            V("tt", "Q pE pX", "t2_%d" % a, T.pX[:, cs], T.Q[:, cs], T.pE[:, cs], A.mult, c=256)
-        for a, cs in halves(256):
-            V("tt", "t2_%d pX Rn%d" % (a, a), hn, T[hn][:, cs], T.pX[:, cs], T.Rn[:, cs], A.add, c=256)
+        V("cp", "B0 B1 Rn0 Rn1 HL", hn + "a", T[hn][:, 0:256], T.RB[:, 0:W].indirect(HL[:, 0:16]), c=ga(256))
+        ACT(T[hn][:, 256:], T.RB[:, 0:W].indirect(HL[:, 16:32]), AF.Copy, "B0 B1 Rn0 Rn1 HL", hn + "b", ga(256))
+        rds = [hn + "a", hn + "b"]
         node("P", [((lambda hn=hn, nx=nx, arr=arr, loc=loc: g.remote_dma(
-            T[nx][:], T[hn][:], T.sem[arr], T.sem[loc], pid, rid, emask)), [hn])], [hn], [nx], SEND, FLY, (arr, 0))
+            T[nx][:], T[hn][:], T.sem[arr], T.sem[loc], pid, rid, emask)), rds)], rds, [nx], SEND, FLY, (arr, 0))
         nodes[-1]["remote"] = [(arr, n_eng), (loc, n_eng)]
-        MM([(T.pU[:, 0:256], T.idn[:], T.eq8[:], True, False, "idn eq8")]
-           + [(T.pU[:, 9 * j:256:8], T.idm[:], T.done[:, 0:32 - j], False, j == 7, "idm done")
+        MM([(T.pU[:, 0:256], T.idh[:], T.eq8[:], True, False, "idh eq8")]
+           + [(T.pU[:, 9 * j:256:8], T.idh[:], T.nd[:, 0:32 - j], False, j == 7, "idh nd")
               for j in range(1, 8)], "pU")
         V("scan", "rst8 pU", "ls", T.ls[:], T.rst8[:], T.pU[:, 0:256], 0.0, A.mult, A.max, c=256)
-        V("ts", "done", "win", T.win[:], T.done[:], 0.0, None, A.is_equal)
-        V("tt", "win ls", "win", T.win[:], T.win[:], T.ls[:, 7::8], A.is_gt)
+        V("tt", "nd ls", "win", T.win[:], T.nd[:], T.ls[:, 7::8], A.is_gt)
         V("tt", "win xmd", "m1", T.m1[:], T.win[:], T.xmd[:], A.mult)
         V("tt", "m1 dump", "off", T.off[:], T.m1[:], T.dump[:], A.add)
-        V("cp", "off", "SL", SL[:, 0:32], T.off[:])
+        V("cp", "off", "SL", SL[:], T.off[:])
         for j in reversed(range(4)):
             cs = slice(128 * j, 128 * j + 128)
-            V("tt", "SL tt ra TB", "TB", T.TB[:, 0:W + 128].indirect(SL[:, 8 * j:8 * j + 8]),
-              T.tt[:, cs], T.ra[:, cs], A.add, c=(50 + 128 * 2.9) / CYC)
+            V("tt", "SL tt%d ra%d TB" % (j // 2, j // 2), "TB", T.TB[:, 0:W + 128].indirect(SL[:, 8 * j:8 * j + 8]),
+              T.tt[:, cs], T.ra[:, cs], A.add, c=60 + 128 * SCATTER)
         if k < STEPS - 1:
-            tables(False)
+            tables()
 
     for hf, cs in halves():
-        ACT(T.AL[:, cs], T.TB[:, cs], AF.Abs, "TB", "AL%d" % hf, bias=4096.0)
-        V("ts", "AL%d" % hf, "yoS%d" % hf, T.yoS[:, cs], T.AL[:, cs], -4096.0, None, A.add, c=512)
+        ACT(T.AL[:, cs], T.TB[:, cs], AF.Abs, "TB", "AL%d" % hf)
+        V("ts", "AL%d" % hf, "yoS%d" % hf, T.yoS[:, cs], T.AL[:, cs], -OFF, None, A.add, c=512)
         dma(T.yo[:, cs], T.yoS[:, cs], "st_yo%d" % hf, ["yoS%d" % hf], [])
     V("ts", "TB", "ymS", T.ymS[:], T.TB[:, 0:W], 0.0, None, A.is_ge, c=1024)
     dma(T.ym[:], T.ymS[0::16, :], "st_ym", ["ymS"], [])

@@ -14,32 +14,38 @@ sb(BF, R, "hdrS")
 sb(I32, W, "owS")
 sb(I32, 64, "mkS")
 sb(BF, 64, "mkB")
-sb(F32, W, "o4 G MF AL yoS ymS")
-sb(F32, W + 128, "TB")
+sb(F32, W, "o4 G MF AL ymS")
+sb(F32, W + 128, "TB RW yoS")
 sb(F32, W + 16, "FB")
 sb(BF, 2048, "S WS U")
-sb(BF, 128, "ones bones idn idh idm tmpa LT")
-sb(F32, 128, "idf")
-sb(BF, 16, "wS g8 tmpb R3 R3b")
+sb(BF, 128, "ones bones idn idh idm idK idL tmpa LT prm")
+sb(F32, 128, "permf zero idf idg")
+sb(BF, 16, "wS R2 R3 R3b")
 sb(F32, 8, "g8f")
 sb(I32, 8, "thS pi ci ta tb")
-sb(F32, 8, "pcol ncol taf tbf s32 wa wb wc wd")
-sb(F32, 256, "jmod DIAG RST rst8 ls")
-sb(F32, 32, "base ep0 e0 thr0 dmp dump pmd kb lan lane xmd thr ge pr av ep e hl win m1 off")
-sb(F32, P, "pU pD pP pW pE pK pR0 pR1 gm sc ra WT dr tt y")
-sb(BF, P, "D ab THW THg hb0 hb1 hb2 hb3 hn0 hn1 hn2")
+sb(F32, 8, "pcol ncol c32 taf tbf s32 wa wb wc wd")
+sb(F32, 256, "jmod DIAG RST")
+sb(F32, 288, "rst9 ls")
+sb(BF, 288, "zb CKa CK AD")
+sb(F32, 64, "DZ0 DZ Z")
+sb(BF, 64, "CX1 CX2")
+sb(F32, 32, "base gcol lane thr ge hl")
+sb(F32, P, "pU pD pP pE pK pR0 pR1 gm sc ra rl WT dr tt y")
+SCRATCH["pW"] = ("psum", [128, 16, 32], F32)
+sb(BF, P, "D ab THW THg THg0 hb0 hb1 hb2 hb3 hn0 hn1 hn2")
 sb(BF, W, "RB")
-sb(BF, 256, "eq8")
 sb(I32, 32, "ui um uo sq zz qm q")
 sb(BF, 32, "key ew nd")
-sb(U16, 32, "XL PL OL OL0 SL HL")
+sb(U16, 32, "XL PL OL OL0 SL HL EL")
 LOADS = ["marks", "owner", "w", "th", "h0", "hdr"]
 SEMAPHORES = ["V", "A", "T", "P"] + ["ld_" + n for n in LOADS] \
     + [n + str(k) for n in ("arr", "loc") for k in range(STEPS)] + ["st_yo0", "st_yo1", "st_ym", "st_yh"]
 OFF = 4096.0
+KS, HUGE = 2.0 ** 22, 2.0 ** 40
 BIG = 8388608.0
 CYC, PE, GATHER, SCATTER, WAKE, DMA, SEND, FLY = 1.04, 0.53, 1.56, 3.8, 80, 2000, 1200, 3300
-LOOK, TOL = 300, 60
+ROUNDS, STEP = 60, 0.5
+ORDER = []
 
 
 def rank_program(g, core, T, topo):
@@ -48,11 +54,18 @@ def rank_program(g, core, T, topo):
         return
     A, AF = AluOpType, ActivationFunctionType
     queues = {"V": g.vector, "A": g.scalar, "T": g.tensor, "P": g, "Y": g.sync}
-    nodes = []
+    nodes, marks, soft = [], {}, {}
 
     def node(q, emit, reads, writes, cost, lat=0.0, sem=None, early=0.0):
         nodes.append({"q": q, "emit": emit, "r": reads, "w": writes, "cost": cost, "lat": lat, "sem": sem or (q, 1),
                       "early": early})
+
+    def mark(name):
+        marks[name] = len(nodes) - 1
+
+    def after(*names):
+        for name in names:
+            soft.setdefault(marks[name], []).append(len(nodes) - 1)
 
     def op(q, fn, reads, writes, cost):
         node(q, [(fn, reads)], reads, writes, cost)
@@ -82,60 +95,65 @@ def rank_program(g, core, T, topo):
 
     def schedule():
         lastw, rd = {}, {}
-        preds = []
+        n = len(nodes)
+        preds, succ = [{} for _ in range(n)], [{} for _ in range(n)]
         for i, d in enumerate(nodes):
-            ps = set()
-            for r in d["r"]:
-                if r in lastw:
-                    ps.add(lastw[r])
-                if is_bank(r):
-                    ps.update(rd.get(r, ()))
+            ps = {}
             for w in d["w"]:
-                if w in lastw:
-                    ps.add(lastw[w])
-                ps.update(rd.get(w, ()))
-            ps.discard(i)
-            preds.append(ps)
+                for p in rd.get(w, []) + lastw.get(w, []):
+                    ps[p] = 0.0 if nodes[p]["sem"][0] == d["sem"][0] else WAKE
+            for r in d["r"]:
+                for p in rd.get(r, []) if is_bank(r) else []:
+                    ps[p] = 0.0 if nodes[p]["sem"][0] == d["sem"][0] else WAKE
+            for r in d["r"]:
+                for p in lastw.get(r, []):
+                    ps[p] = WAKE
+            ps.pop(i, None)
+            for p, gap in ps.items():
+                preds[i][p] = succ[p][i] = gap + nodes[p]["lat"]
             for r in d["r"]:
                 rd.setdefault(r, []).append(i)
             for w in d["w"]:
-                lastw[w] = i
+                lastw[w] = [i]
                 rd[w] = []
-        n = len(nodes)
-        succ = [[] for _ in range(n)]
-        for i, ps in enumerate(preds):
-            for p in ps:
-                succ[p].append(i)
-        prio = [0.0] * n
-        for i in range(n - 1, -1, -1):
-            d = nodes[i]
-            prio[i] = d["cost"] + d["lat"] + max([prio[s] + WAKE for s in succ[i]] + [0.0])
-        left = [len(p) for p in preds]
-        avail = [0.0] * n
-        ready = [i for i in range(n) if not left[i]]
-        free = {q: 0.0 for q in queues}
-        order = []
-        while ready:
-            st = {i: max(free[nodes[i]["q"]], avail[i]) for i in ready}
-            t = min(st.values())
-            q = nodes[min(ready, key=lambda i: (st[i], i))]["q"]
-            cand = sorted([i for i in ready if nodes[i]["q"] == q and st[i] <= t + LOOK],
-                          key=lambda j: (-prio[j] - nodes[j]["early"], j))
-            i = cand[0]
-            for j in cand:
-                if st[j] <= t + 30 and t + nodes[j]["cost"] <= st[i] + TOL:
-                    i = j
+
+        def place(order):
+            end, ready, busy = [0.0] * n, [0.0] * n, {q: [(1e18, 1e18, -1)] for q in queues}
+            for i in order:
+                cost, line = nodes[i]["cost"], busy[nodes[i]["q"]]
+                t = ready[i] = max([end[p] + gap for p, gap in preds[i].items()] + [0.0])
+                at = len(line) - 1
+                while at and line[at - 1][1] > t:
+                    at -= 1
+                while t + cost > line[at][0]:
+                    t = max(t, line[at][1])
+                    at += 1
+                line.insert(at, (t, t + cost, i))
+                end[i] = t + cost
+            ahead = {line[a][2]: line[a - 1][2] for line in busy.values() for a in range(1, len(line))}
+            return end, ready, ahead
+
+        extra, best = [0.0] * n, None
+        for _ in range(ROUNDS):
+            rest = [0.0] * n
+            for i in range(n - 1, -1, -1):
+                rest[i] = nodes[i]["cost"] + extra[i] \
+                    + max([rest[s] + gap for s, gap in succ[i].items()] + [rest[s] for s in soft.get(i, [])]
+                          + [nodes[i]["lat"]])
+            end, ready, ahead = place(sorted(range(n), key=lambda i: (-rest[i] - nodes[i]["early"], i)))
+            i = max(range(n), key=lambda j: end[j] + nodes[j]["lat"])
+            if best is None or end[i] + nodes[i]["lat"] < best[0]:
+                best = (end[i] + nodes[i]["lat"], sorted(range(n), key=lambda j: (end[j] - nodes[j]["cost"], j)))
+            while True:
+                late = end[i] - nodes[i]["cost"] - ready[i]
+                if late > 1.0:
+                    extra[i] += STEP * late
+                    i = ahead[i]
+                elif preds[i]:
+                    i = max(preds[i], key=lambda p: end[p] + preds[i][p])
+                else:
                     break
-            d = nodes[i]
-            ready.remove(i)
-            order.append(i)
-            free[q] = st[i] + d["cost"]
-            for s in succ[i]:
-                avail[s] = max(avail[s], free[q] + d["lat"] + WAKE)
-                left[s] -= 1
-                if not left[s]:
-                    ready.append(s)
-        return order
+        return best[1]
 
     def issue(order):
         known = {q: {} for q in queues}
@@ -205,8 +223,8 @@ def rank_program(g, core, T, topo):
     def iota(buf, name, pattern, base, cm, c):
         op("P", lambda: g.iota(buf, pattern, base, cm, allow_small_or_imprecise_dtypes=True), [], [name], 160 + 2 * c)
 
-    def sel(out, in_, pattern, cmp, base, cm, reads, writes, c):
-        op("P", lambda: g.affine_select(out, in_, pattern, cmp, 0.0, base, cm), [reads], [writes], 210 + 2 * c)
+    def sel(out, in_, pattern, cmp, base, cm, reads, writes, c, fill=0.0):
+        op("P", lambda: g.affine_select(out, in_, pattern, cmp, fill, base, cm), [reads], [writes], 210 + 2 * c)
 
     pc = T.pcol[:, c1]
     V("ms", "", "ones", T.ones[:], 1.0)
@@ -216,9 +234,16 @@ def rank_program(g, core, T, topo):
     sel(T.idn[:], T.ones[:], [[-1, 128]], A.is_equal, 0, 1, "ones", "idn", 128)
     iota(T.jmod[:], "jmod", [[0, 16], [1, 16]], 0, 0, 256)
     iota(T.base[:], "base", [[16, 32]], 0, 0, 32)
-    iota(T.dmp[:], "dmp", [[0, 4], [16, 8]], W, 0, 32)
-    iota(T.kb[:], "kb", [[0, 2], [W, 2], [0, 8]], W, 0, 32)
-    iota(T.rst8[:], "rst8i", [[0, 32], [1, 8]], 0, 0, 256)
+    sel(T.prm[:], T.ones[:], [[-1, 16], [-16, 8]], A.is_equal, 0, 1, "ones", "perm", 128)
+    iota(T.gcol[:], "gcol", [[0, 4], [1, 8]], 0, 0, 32)
+    iota(T.CX1[:], "CX1", [[0, 32], [512, 2]], 0, 0, 64)
+    iota(T.rst9[:], "rst9i", [[0, 32], [1, 9]], 0, 0, 288)
+    ACT(T.zero[:], T.ones[:], AF.Silu, "ones", "zero", 1400, scale=0.0)
+    iota(T.zb[:], "zb", [[0, 288]], 0, 0, 288)
+    iota(T.CKa[:], "CKa", [[0, 4], [16, 8], [0, 9]], -W, 0, 288)
+    sel(T.CK[:], T.CKa[:], [[0, 4], [1, 8], [-1, 9]], A.is_ge, 0, 0, "CKa", "CK", 288, -4.0 * W)
+    V("ms", "", "CK", T.CK[:, 0::9], 0.0)
+    V("ts", "CKa", "CK", T.CK[:, 8::9], T.CKa[:, 8::9], 2.0 * W, None, A.add)
     g8 = T.bones[:, 0::16]
     V("ts", "pi", "ci", T.ci[:, c1], T.pi[:, c1], 15, None, A.bitwise_and)
     V("cp", "ci", "pcol", pc, T.ci[:, c1])
@@ -227,9 +252,9 @@ def rank_program(g, core, T, topo):
         ACT(blk(T.U, c), T.bones[:], AF.Identity, "bones DIAG", "U", 128, scale=T.DIAG[:, c:c + 1])
     V("ms", "", "S", T.S[:], 0.0, c=1024)
     for c in range(16):
-        ACT(T.S[:, 129 * c:128 * (c + 1):16], g8, AF.Copy, "bones", "S", 64)
+        ACT(T.S[:, 129 * c:128 * (c + 1):16], g8, AF.Copy, "bones", "S", 64, scale=KS)
     for hf, cs in halves(1024):
-        V("ts", "S wS", "WS%d" % hf, T.WS[:, cs], T.S[:, cs], T.wS[:, c1], None, A.mult, c=512)
+        V("ts", "S wS", "WS%d" % hf, T.WS[:, cs], T.S[:, cs], T.wS[:, c1], 1.0 / KS, A.mult, A.mult, c=512)
     V("ts", "mkS", "mkB", T.mkB[:], T.mkS[:], 2.0, -1.0, A.mult, A.add)
     for hf, cs in halves():
         bank = "pR%d" % hf
@@ -237,58 +262,56 @@ def rank_program(g, core, T, topo):
            bank)
         V("ts", "owS", "o4_%d" % hf, T.o4[:, cs], T.owS[:, cs], OFF, None, A.add, c=512)
         V("tt", "o4_%d %s" % (hf, bank), "TB", T.TB[:, cs], T.o4[:, cs], T[bank][:], A.mult, c=512)
+        ACT(T.RW[:, cs], T[bank][:], AF.Copy, bank, "RW", bias=0.5, scale=-0.5)
 
     def tables():
-        for hf, cs in halves():
-            ACT(T["pR%d" % hf][:], T.TB[:, cs], AF.Relu, "TB", "pR%d" % hf, scale=-4.0)
-        for hf, cs in halves():
-            fs = slice(8 + 512 * hf, 520 + 512 * hf)
-            V("scan", ("pR%d TB" % hf) + (" FB" if hf else ""), "FB", T.FB[:, fs],
-              T["pR%d" % hf][:], T.TB[:, cs], T.FB[:, 519:520] if hf else 0.0, A.min, A.max, c=512)
+        V("scan", "RW TB", "FB", T.FB[:, 8:8 + W], T.RW[:, 0:W], T.TB[:, 0:W], 0.0, A.mult, A.max, c=1024)
         V("cp", "FB", "FBw", T.FB[:, 7:8], T.FB[:, 7 + W:8 + W])
-        V("tt", "FB FBw pR0", "MF0", T.MF[:, 0:512], T.FB[:, 7:519], T.pR0[:], A.subtract, c=512)
-        V("tt", "FB pR1", "MF1", T.MF[:, 512:], T.FB[:, 519:7 + W], T.pR1[:], A.subtract, c=512)
-        V("scan", "pR0 MF0", "G", T.G[:, 0:512], T.pR0[:], T.MF[:, 0:512], 0.0, A.min, A.max, c=512)
-        V("scan", "pR1 MF1 G", "G", T.G[:, 512:], T.pR1[:], T.MF[:, 512:], T.G[:, 511:512], A.min, A.max, c=512)
+        for a in range(8):
+            bank = "pR%d" % (a // 4)
+            MM([(blk(T[bank], a % 4), T.idg[:], T.FB[:, 8 + 128 * a:136 + 128 * a], True, False, "idg FB")], bank, 512)
+            MM([(blk(T[bank], a % 4), T.idf[:], T.FB[:, 7 + 128 * a:135 + 128 * a], False, True, "idf FB FBw")], bank, 512)
+        for a in range(4):
+            cs, bank = slice(256 * a, 256 * a + 256), "pR%d" % (a // 2)
+            V("scan", "RW " + bank + (" G" if a else ""), "G", T.G[:, cs], T.RW[:, cs],
+              T[bank][:, 256 * (a % 2):256 * (a % 2) + 256], T.G[:, 256 * a - 1:256 * a] if a else 0.0, A.mult, A.add,
+              c=256)
 
-    V("ts", "pcol", "ncol", T.ncol[:, c1], pc, -1.0, None, A.mult)
+    V("ts", "pcol", "ncol", T.ncol[:, c1], pc, -1.0, -0.5, A.mult, A.add)
     V("ts", "jmod", "RST", T.RST[:], T.jmod[:], 0.0, None, A.not_equal, c=256)
-    V("ts", "base pcol", "ep0", T.ep0[:], T.base[:], pc, None, A.add)
-    V("ts", "base pcol", "e0", T.e0[:], T.base[:], 0.0, pc, A.mult, A.add)
-    V("cp", "ep0", "OL0", T.OL0[:], T.ep0[:])
-    V("ts", "ep0", "lane", T.lane[:], T.ep0[:], 1.0 / P, None, A.mult)
-    V("ts", "dmp pcol", "dump", T.dump[:], T.dmp[:], pc, None, A.add)
-    V("ts", "dmp", "pmd", T.pmd[:], T.dmp[:], -1.0, None, A.mult)
-    V("ts", "rst8i", "rst8", T.rst8[:], T.rst8[:], 0.0, None, A.not_equal, c=256)
-    ACT(T.idh[:], T.idn[:], AF.Copy, "idn", "idh", 128, scale=0.5)
-    ACT(T.idm[:], T.idn[:], AF.Copy, "idn", "idm", 128, scale=-1.0)
-    ACT(T.idf[:], T.idn[:], AF.Copy, "idn", "idf", 128)
+    V("ts", "base pcol", "lane", T.lane[:], T.base[:], pc, 1.0 / P, A.add, A.mult)
+    V("ts", "rst9i", "rst9", T.rst9[:], T.rst9[:], 0.0, None, A.not_equal, c=288)
+    V("ts", "pcol", "c32", T.c32[:, c1], pc, 32.0, None, A.mult)
+    V("ts", "gcol c32", "OL0", T.OL0[:], T.gcol[:], T.c32[:, c1], None, A.add)
+    V("ms", "", "DZ0", T.DZ0[:], HUGE)
+    V("ms", "", "DZ", T.DZ[:], HUGE)
+    V("cp", "OL0 DZ0", "DZ0", T.DZ0[:, 1::2], T.OL0[:])
+    V("ms", "", "CX2", T.CX2[:], 0.0)
+    V("cp", "gcol CX2", "CX2", T.CX2[:, 1::2], T.gcol[:])
+    for n, f in (("idf", 1.0), ("idg", -1.0), ("idh", 0.5), ("idm", -1.0), ("idK", 2.0 * W), ("idL", -2.0 * W)):
+        ACT(T[n][:], T.idn[:], AF.Copy, "idn", n, 128, scale=f)
+    ACT(T.permf[:], T.prm[:], AF.Copy, "perm", "permf", 128)
     ACT(T.g8f[:], g8, AF.Copy, "bones", "g8f", 64)
+    ACT(T.R2[:, 0::2], g8, AF.Copy, "bones", "R2", 64, scale=KS)
+    ACT(T.R2[:, 1::2], g8, AF.Copy, "bones", "R2", 64, scale=8.0)
     V("ts", "thS", "ta", T.ta[:, c1], T.thS[:, c1], 8192 - 64, None, A.bitwise_and)
     V("ts", "thS", "tb", T.tb[:, c1], T.thS[:, c1], 63, None, A.bitwise_and)
     V("ts", "ta", "taf", T.taf[:, c1], T.ta[:, c1], -1.0, None, A.mult)
     V("ts", "tb", "tbf", T.tbf[:, c1], T.tb[:, c1], -1.0, None, A.mult)
-    V("ts", "pcol", "s32", T.s32[:, c1], pc, 1.0 / 32, None, A.mult)
+    V("ts", "pcol", "s32", T.s32[:, c1], pc, 0.5, 1.0 / 32, A.add, A.mult)
     V("ms", "", "LT", T.LT[:], 0.0)
     for t, n in enumerate(("taf", "tbf", "s32")):
         ACT(T.LT[:, t::16], T.ones[:, 0:8], AF.Identity, "ones " + n, "LT", 64, scale=T[n][:, c1])
-    MM([(blk(T.pW, b), T.LT[:], T.idn[:], True, True, "LT idn") for b in range(4)], "pW", 128)
+    MM([(T.pW[:, :, 8 * b:8 * b + 8], T.LT[:], T.prm[:], True, True, "LT perm") for b in range(4)], "pW", 128)
     ACT(T.THW[:], T.pW[:], AF.Copy, "pW", "THW")
     V("ts", "pcol", "wc", T.wc[:, c1], pc, 2.0, 32.0, A.is_equal, A.mult)
-    V("ts", "wc", "wb", T.wb[:, c1], T.wc[:, c1], -4.0, None, A.mult)
-    V("ts", "pcol", "wd", T.wd[:, c1], pc, 2.0, -1.0, A.is_lt, A.mult)
+    V("ts", "wc", "wb", T.wb[:, c1], T.wc[:, c1], -4.0 * KS, None, A.mult)
+    V("ts", "pcol", "wd", T.wd[:, c1], pc, 2.0, -KS, A.is_lt, A.mult)
     V("tt", "wb wd", "wa", T.wa[:, c1], T.wb[:, c1], T.wd[:, c1], A.add)
     ACT(T.R3[:, 0::2], g8, AF.Identity, "bones wa", "R3", 64, scale=T.wa[:, c1])
     ACT(T.R3[:, 1::2], g8, AF.Identity, "bones wc", "R3", 64, scale=T.wc[:, c1])
     ACT(T.R3b[:, 0:8], g8, AF.Identity, "bones wb", "R3b", 64, scale=T.wb[:, c1])
-    pT = T.pU[:, 256:320]
-
-    def thresholds(lst, lN, out, oN):
-        ACT(T.THg[:], T.THW[:, 0:P].indirect(lst), AF.Copy, "THW " + lN, "THg", ga(512))
-        MM([(T.pU[:, 256:288], blk(T.S, c), T.THg[:, c::16], c == 0, c == 15, "S THg") for c in range(16)], "pU")
-        ACT(out, T.pU[:, 256:288], AF.Copy, "pU", oN, 64, scale=-1.0)
-
-    thresholds(T.OL0[:, 0:32], "OL0", T.thr0[:], "thr0")
+    ACT(T.THg0[:], T.THW[:, 0:P].indirect(T.OL0[:, 0:32]), AF.Copy, "THW OL0", "THg0", ga(512))
     tables()
 
     def spread(src, name, bank):
@@ -316,82 +339,93 @@ def rank_program(g, core, T, topo):
         for a, ws in halves(16):
             cs = slice(256 * a, 256 * a + 256)
             ACT(T.ra[:, cs], Fwin.indirect(XL[:, ws]), AF.Copy, "FB XL", "ra%d" % a, ga(256))
-            MM([(blk(T.pW, b), blk(T.ra, b), T.idf[:], True, True, "idf ra%d" % a) for b in (2 * a, 2 * a + 1)],
-               "pW", 512)
+            for b in (2 * a, 2 * a + 1):
+                MM([(T.pW[:, :, 8 * b:8 * b + 8], blk(T.ra, b), T.permf[:], True, True, "permf ra%d" % a)], "pW", 512)
         ACT(T.WT[:], T.pW[:], AF.Copy, "pW", "WT")
-        V("tt", "zz kb", "key", T.key[:], zz[:], T.kb[:], A.add)
-        V("tt", "zz pmd", "xmd", T.xmd[:], zz[:], T.pmd[:], A.add)
-        it = []
-        for j in range(8):
-            it.append((T.pE[:, j:256:8], T.idn[:], T.key[:], True, j == 0, "idn key"))
-            if j:
-                it.append((T.pE[:, 9 * j:256:8], T.idm[:], T.key[:, 0:32 - j], False, True, "idm key"))
+        for a, ws in halves(16):
+            ACT(T.dr[:, 256 * a:256 * a + 256], Gwin.indirect(XL[:, ws]), AF.Copy, "G XL", "dr%d" % a, ga(256))
+            mark("dr%d" % a)
+        V("cp", "zz", "key", T.key[:], zz[:])
+        it = [(T.pE[:, 0:288], T.idn[:], T.zb[:], True, False, "idn zb")]
+        for j in range(1, 8):
+            it.append((T.pE[:, j:288:9], T.idn[:], T.key[:], False, False, "idn key"))
+            it.append((T.pE[:, 10 * j:288:9], T.idm[:], T.key[:, 0:32 - j], False, j == 7, "idm key"))
         MM(it, "pE")
-        V("ts", "pE", "eq8", T.eq8[:], T.pE[:, 0:256], 0.0, None, A.is_equal, c=256)
+        ACT(T.AD[:], T.pE[:, 0:288], AF.Abs, "pE", "AD", 288, scale=256.0)
+        MM([(T.pU[:, 0:288], T.idn[:], T.CK[:], True, False, "idn CK"),
+            (T.pU[:, 0:288], T.idm[:], T.AD[:], False, False, "idm AD"),
+            (T.pU[:, 0:288:9], T.idn[:], T.key[:], False, False, "idn key")], "pU", 220)
 
         for hop in range(4):
-            e, eN = (T.e0, "e0") if hop == 0 else (T.e, "e")
-            ep, epN = (T.ep0, "ep0") if hop == 0 else (T.ep, "ep")
-            thr, thN = (T.thr0, "thr0") if hop == 0 else (T.thr, "thr")
             for a, ws in halves(16):
                 cs = slice(256 * a, 256 * a + 256)
-                win, lst, rds = (T.WT[:, 0:P], OL, "WT OL") if hop else (Fwin, XL, "FB XL")
-                V("tt", rds + " DIAG", "gm%d" % a, T.gm[:, cs], win.indirect(lst[:, ws]), T.DIAG[:], A.mult, c=ga(256))
                 if hop == 0:
-                    V("scan", "RST gm%d" % a, "sc%d" % a, T.sc[:, cs], T.RST[:], T.gm[:, cs], 0.0, A.mult, A.add, c=256)
+                    V("tt", "FB XL DIAG", "gm%d gm%d" % (2 * a, 2 * a + 1), T.gm[:, cs], Fwin.indirect(XL[:, ws]),
+                      T.DIAG[:], A.mult, c=ga(256))
+                    V("scan", "RST gm%d gm%d" % (2 * a, 2 * a + 1), "sc%d" % a, T.sc[:, cs], T.RST[:], T.gm[:, cs], 0.0,
+                      A.mult, A.add, c=256)
                     V("ts", "sc%d" % a, "PL%d" % a, PL[:, ws], T.sc[:, 256 * a + 15:256 * a + 256:16], -OFF, None, A.add)
-                else:
-                    MM([(T.pP[:, 8 * b:8 * b + 8], blk(T.gm, b), T.g8f[:], True, True, "g8f gm%d" % a)
-                        for b in (2 * a, 2 * a + 1)], "pP", 256)
-                    V("ts", "pP", "PL%d" % a, PL[:, ws], T.pP[:, ws], -OFF, None, A.add)
-            if hop in (1, 2):
-                thresholds(OL[:, 0:32], "OL", T.thr[:], "thr")
-            elif hop == 3:
+                    continue
+                pP = ("pP", "pK")[a]
+                for b in (2 * a, 2 * a + 1):
+                    V("tt", "WT OL DIAG", "gm%d" % b, blk(T.gm, b), T.WT[:, 8 * b:P].indirect(OL[:, 8 * b:8 * b + 8]),
+                      T.DIAG[:, 0:128], A.mult, c=ga(128))
+                    if b:
+                        after("gm")
+                    if hop == 3:
+                        after("dr0", "dr1")
+                    mark("gm")
+                    MM([(T[pP][:, 8 * b:8 * b + 8], blk(T.gm, b), T.g8f[:], True, True, "g8f gm%d" % b)], pP, 256)
+                V("ts", pP, "PL%d" % a, PL[:, ws], T[pP][:, ws], -OFF, None, A.add)
+            thN = "THg" if hop else "THg0"
+            if hop:
                 ACT(T.THg[:], T.THW[:, 0:P].indirect(OL[:, 0:32]), AF.Copy, "THW OL", "THg", ga(512))
-                MM([(T.pU[:, 256 + 16 * b:272 + 16 * b], blk(T.THg, b), T.R3[:], True, True, "R3 THg")
-                    for b in range(4)], "pU")
-                ACT(T.thr[:], T.pU[:, 256:320:2], AF.Copy, "pU", "thr", 64)
-                ACT(T.ew[:], T.pU[:, 257:320:2], AF.Copy, "pU", "ew", 64)
+            if hop < 3:
+                MM([(T.pD[:, 0:64], T.idn[:], T.CX1[:], True, False, "idn CX1"),
+                    (T.pD[:, 0:64], T.idn[:], T.CX2[:], False, False, "idn CX2")], "pD")
+                for c0 in range(0, 16, 4):
+                    MM([(T.pD[:, 0:64:2], blk(T.S, c), T[thN][:, c::16], False, False, "S " + thN)
+                        for c in range(c0, c0 + 4)], "pD")
+            else:
+                MM([(T.pE[:, 16 * b:16 + 16 * b], blk(T.THg, b), T.R3[:], True, True, "R3 THg")
+                    for b in range(4)], "pE")
+                V("ts", "pE", "EL", T.EL[:], T.pE[:, 1:64:2], -0.5, None, A.add)
+                ACT(T.thr[:], T.pE[:, 0:64:2], AF.Copy, "pE", "thr", 64)
+                MM([(T.pD[:, 0:32], T.idn[:], T.zb[:, 0:32], True, False, "idn zb")]
+                   + [(T.pD[:, 8 * b:8 * b + 8], blk(T.THg, b), T.R3b[:, 0:8], False, False, "R3b THg")
+                      for b in range(4)], "pD")
             for a, ws in halves(16):
                 cs = slice(256 * a, 256 * a + 256)
                 V("tt", "hdrS PL%d %s" % (a, hN), "D%d" % a, T.D[:, cs], T.hdrS[:, 0:R].indirect(PL[:, ws]), h[:, cs],
                   A.subtract, c=ga(256))
                 ACT(T.RB[:, P + 256 * a:P + 256 * a + 256], T.D[:, cs], AF.Abs, "D%d" % a, "Rn%d" % a, 256)
                 if hop < 3:
-                    MM([(T.pD[:, 8 * b:8 * b + 8], blk(T.RB, 4 + b), g8, True, True, "bones Rn%d" % a)
+                    MM([(T.pD[:, 16 * b:16 * b + 16], blk(T.RB, 4 + b), T.R2[:], False, b == 3, "R2 Rn%d" % a)
                         for b in (2 * a, 2 * a + 1)], "pD")
             if hop < 3:
-                V("tt", "pD " + thN, "ge", T.ge[:], T.pD[:, 0:32], thr[:], A.is_ge)
-                V("tt", "pD ge", "qm", T.qm[:], T.pD[:, 0:32], T.ge[:], A.mult)
-                V("tt", "ge " + eN, "pr", T.pr[:], T.ge[:], e[:], A.mult)
-                V("ts", "qm", "q", T.q[:], T.qm[:], 2, 15, A.arith_shift_right, A.bitwise_and)
-                V("tt", "pr " + epN, "av", T.av[:], ep[:], T.pr[:], A.subtract)
-                V("tt", "q av", "ep", T.ep[:], T.q[:], T.av[:], A.add)
-                V("cp", "ep", "OL", OL[:], T.ep[:])
+                dz = "DZ" if hop else "DZ0"
+                V("scan", "pD " + dz, "Z", T.Z[:], T[dz][:], T.pD[:, 0:64], 0.0, A.max, A.min)
+                V("cp", "Z", "qm", T.qm[:], T.Z[:, 1::2])
+                V("ts", "qm", "q", T.q[:], T.qm[:], 15 * 32 + 7, None, A.bitwise_and)
+                V("cp", "q", "OL", OL[:], T.q[:])
                 if hop < 2:
-                    V("tt", "ep base", "e", T.e[:], T.ep[:], T.base[:], A.subtract)
-        MM([(T.pD[:, 0:32], blk(T.S, c), T.RB[:, P + c::16], c == 0, False, "S Rn0 Rn1") for c in range(16)]
-           + [(T.pD[:, 8 * b:8 * b + 8], blk(T.THg, b), T.R3b[:, 0:8], False, b == 3, "R3b THg") for b in range(4)],
-           "pD")
-        V("ts", "pD", "qm", T.qm[:], T.pD[:, 0:32], 64.0, None, A.add)
+                    V("cp", "q", "DZ", T.DZ[:, 1::2], T.q[:])
+        MM([(T.pD[:, 0:32], blk(T.S, c), T.RB[:, P + c::16], False, c == 15, "S Rn0 Rn1") for c in range(16)], "pD")
+        V("ts", "pD", "qm", T.qm[:], T.pD[:, 0:32], 1.0 / KS, 66.0, A.mult, A.add)
         V("tt", "pD thr", "ge", T.ge[:], T.pD[:, 0:32], T.thr[:], A.is_ge)
         V("ts", "qm", "q", T.q[:], T.qm[:], 60, None, A.bitwise_and)
         V("tt", "q ge", "nd", T.nd[:], T.q[:], T.ge[:], A.min)
         V("tt", "nd lane", "hl", T.hl[:], T.nd[:], T.lane[:], A.add)
         V("ts", "hl", "HL", HL[:], T.hl[:], float(P), None, A.mult)
-        spread(T.ew, "ew", "pE")
-        ACT(T.ab[:], T.pE[:], AF.Abs, "pE ncol", "ab", bias=T.ncol[:, c1])
-        ACT(T.pK[:], T.ab[:], AF.Relu, "ab", "pK", bias=1.0, scale=-1.0)
         for a, ws in halves(16):
             cs = slice(256 * a, 256 * a + 256)
-            V("tt", "G XL ra%d" % a, "dr%d" % a, T.dr[:, cs], Gwin.indirect(XL[:, ws]), T.ra[:, cs], A.subtract,
-              c=ga(256))
-            V("tt", "dr%d pK" % a, "tt%d" % a, T.tt[:, cs], T.dr[:, cs], T.pK[:, cs], A.mult, c=256)
+            V("tt", "dr%d EL DIAG" % a, "tt%d" % a, T.tt[:, cs], T.DIAG[:, 0:16].indirect(T.EL[:, ws]), T.dr[:, cs],
+              A.mult, c=ga(256))
 
         MM([(T.pW[:], T.idn[:], h[:], True, False, "idn " + hN),
             (T.pW[:], T.idh[:], T.D[:], False, True, "idh D0 D1")], "pW", 512)
         for a, cs in halves(256):
-            ACT(T.y[:, cs], T.pW[:, cs], AF.Identity, "pW", "y%d" % a, 256, bias=BIG, scale=1.0 - 2.0 ** -11)
+            ACT(T.y[:, cs], T.pW[:, 8 * a:8 * a + 8, :], AF.Identity, "pW", "y%d" % a, 256, bias=BIG, scale=1.0 - 2.0 ** -11)
             ACT(T.RB[:, cs], T.y[:, cs], AF.Copy, "y%d" % a, "B%d" % a, 256, bias=-BIG)
         hn, nx, arr, loc = "hn%d" % k, "hb%d" % (k + 1), "arr%d" % k, "loc%d" % k
         V("cp", "B0 B1 Rn0 Rn1 HL", hn + "a", T[hn][:, 0:256], T.RB[:, 0:W].indirect(HL[:, 0:16]), c=ga(256))
@@ -400,26 +434,32 @@ def rank_program(g, core, T, topo):
         node("P", [((lambda hn=hn, nx=nx, arr=arr, loc=loc: g.remote_dma(
             T[nx][:], T[hn][:], T.sem[arr], T.sem[loc], pid, rid, emask)), rds)], rds, [nx], SEND, FLY, (arr, 0))
         nodes[-1]["remote"] = [(arr, n_eng), (loc, n_eng)]
-        MM([(T.pU[:, 0:256], T.idh[:], T.eq8[:], True, False, "idh eq8")]
-           + [(T.pU[:, 9 * j:256:8], T.idh[:], T.nd[:, 0:32 - j], False, j == 7, "idh nd")
-              for j in range(1, 8)], "pU")
-        V("scan", "rst8 pU", "ls", T.ls[:], T.rst8[:], T.pU[:, 0:256], 0.0, A.mult, A.max, c=256)
-        V("tt", "nd ls", "win", T.win[:], T.nd[:], T.ls[:, 7::8], A.is_gt)
-        V("tt", "win xmd", "m1", T.m1[:], T.win[:], T.xmd[:], A.mult)
-        V("tt", "m1 dump", "off", T.off[:], T.m1[:], T.dump[:], A.add)
-        V("cp", "off", "SL", SL[:], T.off[:])
+        MM([(T.pU[:, 10 * j:288:9], T.idK[:], T.nd[:, 0:32 - j], False, False, "idK nd") for j in range(1, 8)]
+           + [(T.pU[:, 8:288:9], T.idL[:], T.nd[:], False, True, "idL nd")], "pU")
+        V("scan", "rst9 pU", "ls", T.ls[:], T.rst9[:], T.pU[:, 0:288], 0.0, A.mult, A.max, c=288)
+        V("ts", "ls pcol", "SL", SL[:], T.ls[:, 8::9], pc, None, A.add)
+        tab, col = "TB", "ra"
+        if k == STEPS - 1:
+            tab, col = "yoS", "rl"
+            for hf, cs in halves():
+                ACT(T.AL[:, cs], T.TB[:, cs], AF.Abs, "TB", "AL%d" % hf)
+                ACT(T.yoS[:, cs], T.AL[:, cs], AF.Copy, "AL%d" % hf, "yoS", bias=-OFF)
+            for a, cs in halves(256):
+                ACT(T.rl[:, cs], T.ra[:, cs], AF.Copy, "ra%d" % a, "rl%d" % a, 256, bias=-OFF)
         for j in reversed(range(4)):
-            cs = slice(128 * j, 128 * j + 128)
-            V("tt", "SL tt%d ra%d TB" % (j // 2, j // 2), "TB", T.TB[:, 0:W + 128].indirect(SL[:, 8 * j:8 * j + 8]),
-              T.tt[:, cs], T.ra[:, cs], A.add, c=60 + 128 * SCATTER)
+            cs, sl = slice(128 * j, 128 * j + 128), SL[:, 8 * j:8 * j + 8]
+            V("tt", "SL tt%d %s%d %s" % (j // 2, col, j // 2, tab), tab, T[tab][:, 0:W + 128].indirect(sl),
+              T.tt[:, cs], T[col][:, cs], A.add, c=60 + 128 * SCATTER)
+            op("A", lambda sl=sl: g.scalar.activation(T.RW[:, 0:W + 128].indirect(sl), T.zero[:], AF.Silu),
+               ["SL", "zero", "RW"], ["RW"], (70 + 128 * SCATTER) * CYC)
         if k < STEPS - 1:
             tables()
 
     for hf, cs in halves():
-        ACT(T.AL[:, cs], T.TB[:, cs], AF.Abs, "TB", "AL%d" % hf)
-        V("ts", "AL%d" % hf, "yoS%d" % hf, T.yoS[:, cs], T.AL[:, cs], -OFF, None, A.add, c=512)
-        dma(T.yo[:, cs], T.yoS[:, cs], "st_yo%d" % hf, ["yoS%d" % hf], [])
-    V("ts", "TB", "ymS", T.ymS[:], T.TB[:, 0:W], 0.0, None, A.is_ge, c=1024)
+        dma(T.yo[:, cs], T.yoS[:, cs], "st_yo%d" % hf, ["yoS"], [], 4000)
+    ACT(T.ymS[:], T.RW[:, 0:W], AF.Copy, "RW", "ymS", 1024, bias=1.0, scale=-1.0)
     dma(T.ym[:], T.ymS[0::16, :], "st_ym", ["ymS"], [])
     dma(T.yh[:], T["hb%d" % STEPS][:], "st_yh", ["hb%d" % STEPS], [])
-    issue(schedule())
+    if not ORDER:
+        ORDER.extend(schedule())
+    issue(ORDER)

@@ -20,15 +20,17 @@ sb(F32, W + 16, "FB")
 sb(BF, 2048, "S WS U")
 sb(BF, 128, "ones bones idn idh idm idK idL tmpa LT prm")
 sb(F32, 128, "permf zero idf idg")
-sb(BF, 16, "wS R2 R3 R3b")
+sb(BF, 16, "wS R2 R2m R3 R3b")
 sb(F32, 8, "g8f")
 sb(I32, 8, "thS pi ci ta tb")
 sb(F32, 8, "pcol ncol c32 taf tbf s32 wa wb wc wd")
 sb(F32, 256, "jmod DIAG RST")
 sb(F32, 288, "rst9 ls")
 sb(BF, 288, "zb CKa CK AD")
-sb(F32, 64, "DZ0 DZ Z")
-sb(BF, 64, "CX1 CX2")
+sb(F32, 64, "Z0")
+sb(I32, 64, "Z1 Z2 Z3")
+sb(BF, 64, "CX2")
+sb(BF, 192, "CX1")
 sb(F32, 32, "base gcol lane thr ge hl")
 sb(F32, P, "pU pD pP pE pK pR0 pR1 gm sc ra rl WT dr tt y")
 SCRATCH["pW"] = ("psum", [128, 16, 32], F32)
@@ -41,7 +43,7 @@ LOADS = ["marks", "owner", "w", "th", "h0", "hdr"]
 SEMAPHORES = ["V", "A", "T", "P"] + ["ld_" + n for n in LOADS] \
     + [n + str(k) for n in ("arr", "loc") for k in range(STEPS)] + ["st_yo0", "st_yo1", "st_ym", "st_yh"]
 OFF = 4096.0
-KS, HUGE = 2.0 ** 22, 2.0 ** 40
+KS, HUGE = 2.0 ** 18, 2.0 ** 30
 BIG = 8388608.0
 CYC, PE, GATHER, SCATTER, WAKE, DMA, SEND, FLY = 1.04, 0.53, 1.56, 3.8, 80, 2000, 1200, 3300
 ROUNDS, STEP = 60, 0.5
@@ -236,7 +238,9 @@ def rank_program(g, core, T, topo):
     iota(T.base[:], "base", [[16, 32]], 0, 0, 32)
     sel(T.prm[:], T.ones[:], [[-1, 16], [-16, 8]], A.is_equal, 0, 1, "ones", "perm", 128)
     iota(T.gcol[:], "gcol", [[0, 4], [1, 8]], 0, 0, 32)
-    iota(T.CX1[:], "CX1", [[0, 32], [512, 2]], 0, 0, 64)
+    for hop in range(3):
+        V("ms", "", "CX1", T.CX1[:, 64 * hop:64 * hop + 64:2], 0.0)
+        V("ms", "", "CX1", T.CX1[:, 64 * hop + 1:64 * hop + 64:2], max(512.0, 33792.0 * hop))
     iota(T.rst9[:], "rst9i", [[0, 32], [1, 9]], 0, 0, 288)
     ACT(T.zero[:], T.ones[:], AF.Silu, "ones", "zero", 1400, scale=0.0)
     iota(T.zb[:], "zb", [[0, 288]], 0, 0, 288)
@@ -283,28 +287,28 @@ def rank_program(g, core, T, topo):
     V("ts", "rst9i", "rst9", T.rst9[:], T.rst9[:], 0.0, None, A.not_equal, c=288)
     V("ts", "pcol", "c32", T.c32[:, c1], pc, 32.0, None, A.mult)
     V("ts", "gcol c32", "OL0", T.OL0[:], T.gcol[:], T.c32[:, c1], None, A.add)
-    V("ms", "", "DZ0", T.DZ0[:], HUGE)
-    V("ms", "", "DZ", T.DZ[:], HUGE)
-    V("cp", "OL0 DZ0", "DZ0", T.DZ0[:, 1::2], T.OL0[:])
+    V("ms", "", "Z0", T.Z0[:], HUGE)
+    V("cp", "OL0 Z0", "Z0", T.Z0[:, 1::2], T.OL0[:])
     V("ms", "", "CX2", T.CX2[:], 0.0)
     V("cp", "gcol CX2", "CX2", T.CX2[:, 1::2], T.gcol[:])
     for n, f in (("idf", 1.0), ("idg", -1.0), ("idh", 0.5), ("idm", -1.0), ("idK", 2.0 * W), ("idL", -2.0 * W)):
         ACT(T[n][:], T.idn[:], AF.Copy, "idn", n, 128, scale=f)
     ACT(T.permf[:], T.prm[:], AF.Copy, "perm", "permf", 128)
     ACT(T.g8f[:], g8, AF.Copy, "bones", "g8f", 64)
-    ACT(T.R2[:, 0::2], g8, AF.Copy, "bones", "R2", 64, scale=KS)
-    ACT(T.R2[:, 1::2], g8, AF.Copy, "bones", "R2", 64, scale=8.0)
+    for n, f in (("R2", 2.0), ("R2m", -1.0)):
+        ACT(T[n][:, 0::2], g8, AF.Copy, "bones", n, 64, scale=f * KS)
+        ACT(T[n][:, 1::2], g8, AF.Copy, "bones", n, 64, scale=f * 8.0)
     V("ts", "thS", "ta", T.ta[:, c1], T.thS[:, c1], 8192 - 64, None, A.bitwise_and)
     V("ts", "thS", "tb", T.tb[:, c1], T.thS[:, c1], 63, None, A.bitwise_and)
     V("ts", "ta", "taf", T.taf[:, c1], T.ta[:, c1], -1.0, None, A.mult)
     V("ts", "tb", "tbf", T.tbf[:, c1], T.tb[:, c1], -1.0, None, A.mult)
-    V("ts", "pcol", "s32", T.s32[:, c1], pc, 0.5, 1.0 / 32, A.add, A.mult)
+    V("ts", "pcol", "s32", T.s32[:, c1], pc, 32.0, 1.0 / 64, A.add, A.mult)
     V("ms", "", "LT", T.LT[:], 0.0)
     for t, n in enumerate(("taf", "tbf", "s32")):
         ACT(T.LT[:, t::16], T.ones[:, 0:8], AF.Identity, "ones " + n, "LT", 64, scale=T[n][:, c1])
     MM([(T.pW[:, :, 8 * b:8 * b + 8], T.LT[:], T.prm[:], True, True, "LT perm") for b in range(4)], "pW", 128)
     ACT(T.THW[:], T.pW[:], AF.Copy, "pW", "THW")
-    V("ts", "pcol", "wc", T.wc[:, c1], pc, 2.0, 32.0, A.is_equal, A.mult)
+    V("ts", "pcol", "wc", T.wc[:, c1], pc, 2.0, 64.0, A.is_equal, A.mult)
     V("ts", "wc", "wb", T.wb[:, c1], T.wc[:, c1], -4.0 * KS, None, A.mult)
     V("ts", "pcol", "wd", T.wd[:, c1], pc, 2.0, -KS, A.is_lt, A.mult)
     V("tt", "wb wd", "wa", T.wa[:, c1], T.wb[:, c1], T.wd[:, c1], A.add)
@@ -381,15 +385,17 @@ def rank_program(g, core, T, topo):
             if hop:
                 ACT(T.THg[:], T.THW[:, 0:P].indirect(OL[:, 0:32]), AF.Copy, "THW OL", "THg", ga(512))
             if hop < 3:
-                MM([(T.pD[:, 0:64], T.idn[:], T.CX1[:], True, False, "idn CX1"),
-                    (T.pD[:, 0:64], T.idn[:], T.CX2[:], False, False, "idn CX2")], "pD")
+                MM([(T.pD[:, 0:64], T.idn[:], T.CX1[:, 64 * hop:64 * hop + 64], True, False, "idn CX1"),
+                    (T.pD[:, 0:64], T.idn[:], T.CX2[:], False, False, "idn CX2")]
+                   + [(T.pD[:, 16 * b:16 * b + 16], blk(h, b), T.R2m[:], False, False, "R2m " + hN) for b in range(4)],
+                   "pD")
                 for c0 in range(0, 16, 4):
                     MM([(T.pD[:, 0:64:2], blk(T.S, c), T[thN][:, c::16], False, False, "S " + thN)
                         for c in range(c0, c0 + 4)], "pD")
             else:
                 MM([(T.pE[:, 16 * b:16 + 16 * b], blk(T.THg, b), T.R3[:], True, True, "R3 THg")
                     for b in range(4)], "pE")
-                V("ts", "pE", "EL", T.EL[:], T.pE[:, 1:64:2], -0.5, None, A.add)
+                V("ts", "pE", "EL", T.EL[:], T.pE[:, 1:64:2], -32.0, None, A.add)
                 ACT(T.thr[:], T.pE[:, 0:64:2], AF.Copy, "pE", "thr", 64)
                 MM([(T.pD[:, 0:32], T.idn[:], T.zb[:, 0:32], True, False, "idn zb")]
                    + [(T.pD[:, 8 * b:8 * b + 8], blk(T.THg, b), T.R3b[:, 0:8], False, False, "R3b THg")
@@ -397,21 +403,23 @@ def rank_program(g, core, T, topo):
             for a, ws in halves(16):
                 cs = slice(256 * a, 256 * a + 256)
                 V("tt", "hdrS PL%d %s" % (a, hN), "D%d" % a, T.D[:, cs], T.hdrS[:, 0:R].indirect(PL[:, ws]), h[:, cs],
-                  A.subtract, c=ga(256))
-                ACT(T.RB[:, P + 256 * a:P + 256 * a + 256], T.D[:, cs], AF.Abs, "D%d" % a, "Rn%d" % a, 256)
+                  A.max if hop < 3 else A.subtract, c=ga(256))
+                rn = T.RB[:, P + 256 * a:P + 256 * a + 256]
                 if hop < 3:
-                    MM([(T.pD[:, 16 * b:16 * b + 16], blk(T.RB, 4 + b), T.R2[:], False, b == 3, "R2 Rn%d" % a)
+                    ACT(rn, T.hdrS[:, 0:R].indirect(PL[:, ws]), AF.Copy, "hdrS PL%d" % a, "Rn%d" % a, ga(256))
+                    MM([(T.pD[:, 16 * b:16 * b + 16], blk(T.RB, 4 + b), T.R2m[:], False, False, "R2m Rn%d" % a)
                         for b in (2 * a, 2 * a + 1)], "pD")
+                    MM([(T.pD[:, 16 * b:16 * b + 16], blk(T.D, b), T.R2[:], False, b == 3, "R2 D%d" % a)
+                        for b in (2 * a, 2 * a + 1)], "pD")
+                else:
+                    ACT(rn, T.D[:, cs], AF.Abs, "D%d" % a, "Rn%d" % a, 256)
             if hop < 3:
-                dz = "DZ" if hop else "DZ0"
-                V("scan", "pD " + dz, "Z", T.Z[:], T[dz][:], T.pD[:, 0:64], 0.0, A.max, A.min)
-                V("cp", "Z", "qm", T.qm[:], T.Z[:, 1::2])
-                V("ts", "qm", "q", T.q[:], T.qm[:], 15 * 32 + 7, None, A.bitwise_and)
+                z0, z1 = "Z%d" % hop, "Z%d" % (hop + 1)
+                V("scan", "pD " + z0, z1, T[z1][:], T[z0][:], T.pD[:, 0:64], 0.0, A.max, A.min)
+                V("ts", z1, "q", T.q[:], T[z1][:, 1::2], 15 * 32 + 7, None, A.bitwise_and)
                 V("cp", "q", "OL", OL[:], T.q[:])
-                if hop < 2:
-                    V("cp", "q", "DZ", T.DZ[:, 1::2], T.q[:])
         MM([(T.pD[:, 0:32], blk(T.S, c), T.RB[:, P + c::16], False, c == 15, "S Rn0 Rn1") for c in range(16)], "pD")
-        V("ts", "pD", "qm", T.qm[:], T.pD[:, 0:32], 1.0 / KS, 66.0, A.mult, A.add)
+        V("ts", "pD", "qm", T.qm[:], T.pD[:, 0:32], 1.0 / KS, 192.0, A.mult, A.add)
         V("tt", "pD thr", "ge", T.ge[:], T.pD[:, 0:32], T.thr[:], A.is_ge)
         V("ts", "qm", "q", T.q[:], T.qm[:], 60, None, A.bitwise_and)
         V("tt", "q ge", "nd", T.nd[:], T.q[:], T.ge[:], A.min)

@@ -1,6 +1,8 @@
+import numpy
 from concourse.mybir import dt, AluOpType, AxisListType, ActivationFunctionType
 
 N, W, R, P, STEPS, SHIFT = 6, 1024, 8192, 512, 3, 2
+H = P // 2
 F32, BF, I32, U16 = "float32", "bfloat16", "int32", "uint16"
 SCRATCH = {}
 
@@ -14,7 +16,7 @@ sb(BF, R, "hdrS")
 sb(I32, W, "owS")
 sb(I32, 64, "mkS")
 sb(BF, 64, "mkB")
-sb(F32, W, "o4 G MF AL ymS")
+sb(F32, W, "o4 G AL ymS")
 sb(F32, W + 128, "TB RW yoS")
 sb(F32, W + 16, "FB")
 sb(BF, 2048, "S WS U")
@@ -23,30 +25,41 @@ sb(F32, 128, "permf zero idf idg")
 sb(BF, 16, "wS R2 R2m R3 R3b")
 sb(F32, 8, "g8f")
 sb(I32, 8, "thS pi ci ta tb")
-sb(F32, 8, "pcol ncol c32 taf tbf s32 wa wb wc wd")
+sb(F32, 8, "pcol c32 taf tbf s32 wa wb wc wd")
 sb(F32, 256, "jmod DIAG RST")
-sb(F32, 288, "rst9 ls")
-sb(BF, 288, "zb CKa CK AD")
-sb(F32, 64, "Z0")
+sb(F32, 144, "rst9")
+sb(BF, 144, "zb CKa CK")
+sb(F32, 288, "ls")
+sb(BF, 288, "AD")
+sb(F32, 32, "Z0")
 sb(I32, 64, "Z1 Z2 Z3")
-sb(BF, 64, "CX2")
-sb(BF, 192, "CX1")
-sb(F32, 32, "base gcol lane thr ge hl")
-sb(F32, P, "pU pD pP pE pK pR0 pR1 gm sc ra rl WT dr tt y")
+sb(BF, 32, "CX2")
+sb(BF, 96, "CX1")
+sb(F32, 16, "base gcol")
+sb(F32, 32, "thr")
+sb(F32, 64, "gl hl")
+sb(F32, P, "pU pD0 pD1 pP0 pP1 pR0 pR1 gm sc ra rl WT0 WT1 dr tt y")
 SCRATCH["pW"] = ("psum", [128, 16, 32], F32)
-sb(BF, P, "D ab THW THg THg0 hb0 hb1 hb2 hb3 hn0 hn1 hn2")
-sb(BF, W, "RB")
-sb(I32, 32, "ui um uo sq zz qm q")
-sb(BF, 32, "key ew nd")
+sb(BF, P, "D THW THg RB0 RB1")
+sb(BF, H, "THg0")
+for k in range(STEPS + 1):
+    sb(BF, H, "hb%d0 hb%d1" % (k, k))
+for k in range(STEPS):
+    sb(BF, H, "hn%d0 hn%d1" % (k, k))
+sb(I32, 32, "ui zz qm q")
+sb(I32, 64, "q2")
+sb(I32, 96, "ua ub sq")
+sb(BF, 32, "key nd")
 sb(U16, 32, "XL PL OL OL0 SL HL EL")
-LOADS = ["marks", "owner", "w", "th", "h0", "hdr"]
+LOADS = ["marks", "owner", "w", "th", "h0", "h1", "hdr"]
 SEMAPHORES = ["V", "A", "T", "P"] + ["ld_" + n for n in LOADS] \
-    + [n + str(k) for n in ("arr", "loc") for k in range(STEPS)] + ["st_yo0", "st_yo1", "st_ym", "st_yh"]
+    + ["%s%d%d" % (n, k, a) for n in ("arr", "loc") for k in range(STEPS) for a in range(2)] \
+    + ["st_yo0", "st_yo1", "st_ym", "st_yh0", "st_yh1"]
 OFF = 4096.0
 KS, HUGE = 2.0 ** 18, 2.0 ** 30
 BIG = 8388608.0
-CYC, PE, GATHER, SCATTER, WAKE, DMA, SEND, FLY = 1.04, 0.53, 1.56, 3.8, 80, 2000, 1200, 3300
-ROUNDS, STEP = 60, 0.5
+CYC, PE, GATHER, SCATTER, WAKE, DMA, SEND, FLY = 0.87, 0.44, 1.4, 3.4, 200, 2000, 1000, 1800
+ROUNDS = 4000
 ORDER = []
 
 
@@ -135,26 +148,28 @@ def rank_program(g, core, T, topo):
             ahead = {line[a][2]: line[a - 1][2] for line in busy.values() for a in range(1, len(line))}
             return end, ready, ahead
 
-        extra, best = [0.0] * n, None
+        rnd = numpy.random.RandomState(0)
+        extra, best, chain = [0.0] * n, None, []
         for _ in range(ROUNDS):
+            ex = list(extra)
+            for _ in range(2 ** rnd.randint(4) if chain else 0):
+                i = chain[rnd.randint(len(chain))] if rnd.randint(2) else rnd.randint(n)
+                ex[i] += rnd.randn() * 100.0 * 4 ** rnd.randint(3)
             rest = [0.0] * n
             for i in range(n - 1, -1, -1):
-                rest[i] = nodes[i]["cost"] + extra[i] \
+                rest[i] = max(1.0, nodes[i]["cost"] + ex[i]) \
                     + max([rest[s] + gap for s, gap in succ[i].items()] + [rest[s] for s in soft.get(i, [])]
                           + [nodes[i]["lat"]])
             end, ready, ahead = place(sorted(range(n), key=lambda i: (-rest[i] - nodes[i]["early"], i)))
             i = max(range(n), key=lambda j: end[j] + nodes[j]["lat"])
-            if best is None or end[i] + nodes[i]["lat"] < best[0]:
-                best = (end[i] + nodes[i]["lat"], sorted(range(n), key=lambda j: (end[j] - nodes[j]["cost"], j)))
-            while True:
-                late = end[i] - nodes[i]["cost"] - ready[i]
-                if late > 1.0:
-                    extra[i] += STEP * late
-                    i = ahead[i]
-                elif preds[i]:
-                    i = max(preds[i], key=lambda p: end[p] + preds[i][p])
-                else:
-                    break
+            if best is not None and end[i] + nodes[i]["lat"] > best[0]:
+                continue
+            best = (end[i] + nodes[i]["lat"], sorted(range(n), key=lambda j: (end[j] - nodes[j]["cost"], j)))
+            extra, chain = ex, [i]
+            while end[i] - nodes[i]["cost"] - ready[i] > 1.0 or preds[i]:
+                late = end[i] - nodes[i]["cost"] - ready[i] > 1.0
+                i = ahead[i] if late else max(preds[i], key=lambda p: end[p] + preds[i][p])
+                chain.append(i)
         return best[1]
 
     def issue(order):
@@ -208,8 +223,8 @@ def rank_program(g, core, T, topo):
         for s, v in total.items():
             g.wait_ge(T.sem[s], v)
 
-    def halves(n=512):
-        return [(hf, slice(hf * n, hf * n + n)) for hf in range(2)]
+    def part(a, n):
+        return slice(a * n, a * n + n)
 
     def blk(buf, c):
         return buf[:, 128 * c:128 * c + 128]
@@ -219,33 +234,34 @@ def rank_program(g, core, T, topo):
     dma(T.owS[:], T.owner[:], "ld_owner", [], ["owS"], 4000, early=8e6)
     dma(T.wS[:, c1], T.w[:], "ld_w", [], ["wS"], 4200, early=7e6)
     dma(T.thS[:, c1], T.th[:], "ld_th", [], ["thS"], 4200, early=6e6)
-    dma(T.hb0[:], T.h0[:], "ld_h0", [], ["hb0"], 4700, early=5e6)
+    for a in range(2):
+        dma(T["hb0%d" % a][:], T.h0[:, part(a, H)], "ld_h%d" % a, [], ["hb0%d" % a], 4700, early=5e6)
     dma(T.hdrS[:], T.hdr[:], "ld_hdr", [], ["hdrS"], 12000)
 
     def iota(buf, name, pattern, base, cm, c):
-        op("P", lambda: g.iota(buf, pattern, base, cm, allow_small_or_imprecise_dtypes=True), [], [name], 160 + 2 * c)
+        op("P", lambda: g.iota(buf, pattern, base, cm, allow_small_or_imprecise_dtypes=True), [], [name], 140 + 2 * c)
 
     def sel(out, in_, pattern, cmp, base, cm, reads, writes, c, fill=0.0):
-        op("P", lambda: g.affine_select(out, in_, pattern, cmp, fill, base, cm), [reads], [writes], 210 + 2 * c)
+        op("P", lambda: g.affine_select(out, in_, pattern, cmp, fill, base, cm), [reads], [writes], 180 + 2 * c)
 
     pc = T.pcol[:, c1]
     V("ms", "", "ones", T.ones[:], 1.0)
-    op("P", lambda: g.iota(T.pi[:, c1], [[0, 1]], 0, 1), [], ["pi"], 160)
+    op("P", lambda: g.iota(T.pi[:, c1], [[0, 1]], 0, 1), [], ["pi"], 140)
     sel(T.tmpa[:], T.ones[:], [[-16, 8], [0, 16]], A.is_ge, 0, 1, "ones", "tmpa", 128)
     sel(T.bones[:], T.tmpa[:], [[16, 8], [0, 16]], A.is_ge, 15, -1, "tmpa", "bones", 128)
     sel(T.idn[:], T.ones[:], [[-1, 128]], A.is_equal, 0, 1, "ones", "idn", 128)
     iota(T.jmod[:], "jmod", [[0, 16], [1, 16]], 0, 0, 256)
-    iota(T.base[:], "base", [[16, 32]], 0, 0, 32)
+    iota(T.base[:], "base", [[16, 16]], 0, 0, 16)
     sel(T.prm[:], T.ones[:], [[-1, 16], [-16, 8]], A.is_equal, 0, 1, "ones", "perm", 128)
-    iota(T.gcol[:], "gcol", [[0, 4], [1, 8]], 0, 0, 32)
+    iota(T.gcol[:], "gcol", [[0, 2], [1, 8]], 0, 0, 16)
     for hop in range(3):
-        V("ms", "", "CX1", T.CX1[:, 64 * hop:64 * hop + 64:2], 0.0)
-        V("ms", "", "CX1", T.CX1[:, 64 * hop + 1:64 * hop + 64:2], max(512.0, 33792.0 * hop))
-    iota(T.rst9[:], "rst9i", [[0, 32], [1, 9]], 0, 0, 288)
+        V("ms", "", "CX1", T.CX1[:, 32 * hop:32 * hop + 32:2], 0.0)
+        V("ms", "", "CX1", T.CX1[:, 32 * hop + 1:32 * hop + 32:2], max(512.0, 33792.0 * hop))
+    iota(T.rst9[:], "rst9i", [[0, 16], [1, 9]], 0, 0, 144)
     ACT(T.zero[:], T.ones[:], AF.Silu, "ones", "zero", 1400, scale=0.0)
-    iota(T.zb[:], "zb", [[0, 288]], 0, 0, 288)
-    iota(T.CKa[:], "CKa", [[0, 4], [16, 8], [0, 9]], -W, 0, 288)
-    sel(T.CK[:], T.CKa[:], [[0, 4], [1, 8], [-1, 9]], A.is_ge, 0, 0, "CKa", "CK", 288, -4.0 * W)
+    V("ms", "", "zb", T.zb[:], 0.0)
+    iota(T.CKa[:], "CKa", [[0, 2], [16, 8], [0, 9]], -W, 0, 144)
+    sel(T.CK[:], T.CKa[:], [[0, 2], [1, 8], [-1, 9]], A.is_ge, 0, 0, "CKa", "CK", 144, -4.0 * W)
     V("ms", "", "CK", T.CK[:, 0::9], 0.0)
     V("ts", "CKa", "CK", T.CK[:, 8::9], T.CKa[:, 8::9], 2.0 * W, None, A.add)
     g8 = T.bones[:, 0::16]
@@ -257,11 +273,12 @@ def rank_program(g, core, T, topo):
     V("ms", "", "S", T.S[:], 0.0, c=1024)
     for c in range(16):
         ACT(T.S[:, 129 * c:128 * (c + 1):16], g8, AF.Copy, "bones", "S", 64, scale=KS)
-    for hf, cs in halves(1024):
+    for hf in range(2):
+        cs = part(hf, 1024)
         V("ts", "S wS", "WS%d" % hf, T.WS[:, cs], T.S[:, cs], T.wS[:, c1], 1.0 / KS, A.mult, A.mult, c=512)
     V("ts", "mkS", "mkB", T.mkB[:], T.mkS[:], 2.0, -1.0, A.mult, A.add)
-    for hf, cs in halves():
-        bank = "pR%d" % hf
+    for hf in range(2):
+        cs, bank = part(hf, 512), "pR%d" % hf
         MM([(T[bank][:, 64 * c:64 * c + 64], blk(T.U, 8 * hf + c), T.mkB[:], True, True, "U mkB") for c in range(8)],
            bank)
         V("ts", "owS", "o4_%d" % hf, T.o4[:, cs], T.owS[:, cs], OFF, None, A.add, c=512)
@@ -270,25 +287,29 @@ def rank_program(g, core, T, topo):
 
     def tables():
         V("scan", "RW TB", "FB", T.FB[:, 8:8 + W], T.RW[:, 0:W], T.TB[:, 0:W], 0.0, A.mult, A.max, c=1024)
+        mark("FB")
         V("cp", "FB", "FBw", T.FB[:, 7:8], T.FB[:, 7 + W:8 + W])
         for a in range(8):
             bank = "pR%d" % (a // 4)
             MM([(blk(T[bank], a % 4), T.idg[:], T.FB[:, 8 + 128 * a:136 + 128 * a], True, False, "idg FB")], bank, 512)
             MM([(blk(T[bank], a % 4), T.idf[:], T.FB[:, 7 + 128 * a:135 + 128 * a], False, True, "idf FB FBw")], bank, 512)
         for a in range(4):
-            cs, bank = slice(256 * a, 256 * a + 256), "pR%d" % (a // 2)
-            V("scan", "RW " + bank + (" G" if a else ""), "G", T.G[:, cs], T.RW[:, cs],
-              T[bank][:, 256 * (a % 2):256 * (a % 2) + 256], T.G[:, 256 * a - 1:256 * a] if a else 0.0, A.mult, A.add,
-              c=256)
+            cs, bank = part(a, 256), "pR%d" % (a // 2)
+            V("scan", "RW " + bank + (" G" if a else ""), "G", T.G[:, cs], T.RW[:, cs], T[bank][:, part(a % 2, 256)],
+              T.G[:, 256 * a - 1:256 * a] if a else 0.0, A.mult, A.add, c=256)
 
-    V("ts", "pcol", "ncol", T.ncol[:, c1], pc, -1.0, -0.5, A.mult, A.add)
     V("ts", "jmod", "RST", T.RST[:], T.jmod[:], 0.0, None, A.not_equal, c=256)
-    V("ts", "base pcol", "lane", T.lane[:], T.base[:], pc, 1.0 / P, A.add, A.mult)
-    V("ts", "rst9i", "rst9", T.rst9[:], T.rst9[:], 0.0, None, A.not_equal, c=288)
+    V("ms", "", "q2", T.q2[:], 0)
+    V("ms", "", "ua", T.ua[:], 32)
+    V("ms", "", "ub", T.ub[:], 1)
+    for a in range(2):
+        V("ts", "base pcol", "gl", T.gl[:, 32 * a + 1:32 * a + 32:2], T.base[:], pc, 1.0 / H, A.add, A.mult)
+    V("ms", "ub", "ub", T.ub[:, 0::3], 0)
+    V("ts", "rst9i", "rst9", T.rst9[:], T.rst9[:], 0.0, None, A.not_equal, c=144)
     V("ts", "pcol", "c32", T.c32[:, c1], pc, 32.0, None, A.mult)
-    V("ts", "gcol c32", "OL0", T.OL0[:], T.gcol[:], T.c32[:, c1], None, A.add)
+    V("ts", "gcol c32", "OL0", T.OL0[:, 0:16], T.gcol[:], T.c32[:, c1], None, A.add)
     V("ms", "", "Z0", T.Z0[:], HUGE)
-    V("cp", "OL0 Z0", "Z0", T.Z0[:, 1::2], T.OL0[:])
+    V("cp", "OL0 Z0", "Z0", T.Z0[:, 1::2], T.OL0[:, 0:16])
     V("ms", "", "CX2", T.CX2[:], 0.0)
     V("cp", "gcol CX2", "CX2", T.CX2[:, 1::2], T.gcol[:])
     for n, f in (("idf", 1.0), ("idg", -1.0), ("idh", 0.5), ("idm", -1.0), ("idK", 2.0 * W), ("idL", -2.0 * W)):
@@ -315,159 +336,155 @@ def rank_program(g, core, T, topo):
     ACT(T.R3[:, 0::2], g8, AF.Identity, "bones wa", "R3", 64, scale=T.wa[:, c1])
     ACT(T.R3[:, 1::2], g8, AF.Identity, "bones wc", "R3", 64, scale=T.wc[:, c1])
     ACT(T.R3b[:, 0:8], g8, AF.Identity, "bones wb", "R3b", 64, scale=T.wb[:, c1])
-    ACT(T.THg0[:], T.THW[:, 0:P].indirect(T.OL0[:, 0:32]), AF.Copy, "THW OL0", "THg0", ga(512))
+    ACT(T.THg0[:], T.THW[:, 0:P].indirect(T.OL0[:, 0:16]), AF.Copy, "THW OL0", "THgc", ga(H))
     tables()
-
-    def spread(src, name, bank):
-        MM([(T[bank][:, c::16], blk(T.U, c), src[:], True, True, "U " + name) for c in range(16)], bank)
 
     dst = T.cores[(rank + SHIFT) % N]
     rid, pid, _ = topo.addr(dst)
     emask = topo.mask(core, dst)
     n_eng = len(topo.engines(core, dst))
-    Fwin, Gwin = T.FB[:, 8:8 + W], T.G[:, 0:W]
-    XL, PL, OL, SL, HL, zz = T.XL, T.PL, T.OL, T.SL, T.HL, T.zz
-    Rn = T.RB[:, P:]
+    Fwin, Gwin, Hwin = T.FB[:, 8:8 + W], T.G[:, 0:W], T.hdrS[:, 0:R]
 
-    for k in range(STEPS):
-        hN = "hb%d" % k
-        h = T[hN]
-        MM([(T.pU[:, 0:32], blk(T.WS, c), h[:, c::16], c == 0, c == 15, "WS%d %s" % (c // 8, hN)) for c in range(16)],
-           "pU")
-        V("cp", "pU", "ui", T.ui[:], T.pU[:, 0:32])
-        V("ts", "ui", "um", T.um[:], T.ui[:], 4095, None, A.bitwise_and)
-        V("ts", "um", "uo", T.uo[:], T.um[:], 32.0, None, A.add)
-        V("tt", "um uo", "sq", T.sq[:], T.um[:], T.uo[:], A.mult)
-        V("ts", "sq", "zz", zz[:], T.sq[:], 5, W - 16, A.arith_shift_right, A.bitwise_and)
-        V("ts", "zz pcol", "XL", XL[:], zz[:], pc, None, A.add)
-        for a, ws in halves(16):
-            cs = slice(256 * a, 256 * a + 256)
-            ACT(T.ra[:, cs], Fwin.indirect(XL[:, ws]), AF.Copy, "FB XL", "ra%d" % a, ga(256))
-            for b in (2 * a, 2 * a + 1):
-                MM([(T.pW[:, :, 8 * b:8 * b + 8], blk(T.ra, b), T.permf[:], True, True, "permf ra%d" % a)], "pW", 512)
-        ACT(T.WT[:], T.pW[:], AF.Copy, "pW", "WT")
-        for a, ws in halves(16):
-            ACT(T.dr[:, 256 * a:256 * a + 256], Gwin.indirect(XL[:, ws]), AF.Copy, "G XL", "dr%d" % a, ga(256))
-            mark("dr%d" % a)
-        V("cp", "zz", "key", T.key[:], zz[:])
-        it = [(T.pE[:, 0:288], T.idn[:], T.zb[:], True, False, "idn zb")]
+    def start(k, a):
+        n = lambda s: s.replace("#", str(a))
+        ws, cs, ns = part(a, 16), part(a, H), part(a, 144)
+        hN, pD, pR = "hb%d%d" % (k, a), n("pD#"), n("pR#")
+        xl, zz, key = T.XL[:, ws], T.zz[:, ws], T.key[:, ws]
+        MM([(T[pD][:, 0:16], blk(T.WS, c), T[hN][:, c::16], c == 0, c == 15, "WS%d %s" % (c // 8, hN))
+            for c in range(16)], pD)
+        V("cp", pD, n("ui#"), T.ui[:, ws], T[pD][:, 0:16])
+        us = part(a, 48)
+        V("ts", n("ui# ua"), n("ua#"), T.ua[:, 48 * a + 1:48 * a + 48:3], T.ui[:, ws], 4095, None, A.bitwise_and)
+        V("ts", n("ui# ub"), n("ub#"), T.ub[:, 48 * a + 2:48 * a + 48:3], T.ui[:, ws], 4095, None, A.bitwise_and)
+        V("scan", n("ua# ub#"), n("sq#"), T.sq[:, us], T.ua[:, us], T.ub[:, us], 0.0, A.add, A.mult)
+        V("ts", n("sq#"), n("zz#"), zz, T.sq[:, 48 * a + 2:48 * a + 48:3], 5, W - 16, A.arith_shift_right,
+          A.bitwise_and)
+        V("ts", n("zz# pcol"), n("XL#"), xl, zz, pc, None, A.add)
+        V("tt", n("FB XL# DIAG"), n("gm#0 gm#1"), T.gm[:, cs], Fwin.indirect(xl), T.DIAG[:], A.mult, c=ga(H))
+        V("scan", n("RST gm#0 gm#1"), n("sc#"), T.sc[:, cs], T.RST[:], T.gm[:, cs], 0.0, A.mult, A.add, c=H)
+        V("ts", n("sc#"), n("PL#"), T.PL[:, ws], T.sc[:, H * a + 15:H * a + H:16], -OFF, None, A.add)
+        ACT(T.ra[:, cs], Fwin.indirect(xl), AF.Copy, n("FB XL#"), n("ra#"), ga(H))
+        for b in range(2):
+            MM([(T.pW[:, :, 8 * b:8 * b + 8], blk(T.ra, 2 * a + b), T.permf[:], True, True, n("permf ra#"))], "pW", 512)
+        ACT(T[n("WT#")][:], T.pW[:], AF.Copy, "pW", n("WT#"))
+        ACT(T.dr[:, cs], Gwin.indirect(xl), AF.Copy, n("G XL#"), n("dr#"), ga(H))
+        mark(n("dr#"))
+        V("cp", n("zz#"), n("key#"), key, zz)
+        it = [(T.pU[:, 0:144], T.idn[:], T.zb[:], True, False, "idn zb")]
         for j in range(1, 8):
-            it.append((T.pE[:, j:288:9], T.idn[:], T.key[:], False, False, "idn key"))
-            it.append((T.pE[:, 10 * j:288:9], T.idm[:], T.key[:, 0:32 - j], False, j == 7, "idm key"))
-        MM(it, "pE")
-        ACT(T.AD[:], T.pE[:, 0:288], AF.Abs, "pE", "AD", 288, scale=256.0)
-        MM([(T.pU[:, 0:288], T.idn[:], T.CK[:], True, False, "idn CK"),
-            (T.pU[:, 0:288], T.idm[:], T.AD[:], False, False, "idm AD"),
-            (T.pU[:, 0:288:9], T.idn[:], T.key[:], False, False, "idn key")], "pU", 220)
+            it.append((T.pU[:, j:144:9], T.idn[:], key, False, False, n("idn key#")))
+            it.append((T.pU[:, 10 * j:144:9], T.idm[:], T.key[:, 16 * a:16 * a + 16 - j], False, j == 7, n("idm key#")))
+        MM(it, "pU")
+        ACT(T.AD[:, ns], T.pU[:, 0:144], AF.Abs, "pU", n("AD#"), 144, scale=256.0)
+        MM([(T[pR][:, 0:144], T.idn[:], T.CK[:], True, False, "idn CK"),
+            (T[pR][:, 0:144], T.idm[:], T.AD[:, ns], False, False, n("idm AD#")),
+            (T[pR][:, 0:144:9], T.idn[:], key, False, False, n("idn key#"))], pR, 120)
 
-        for hop in range(4):
-            for a, ws in halves(16):
-                cs = slice(256 * a, 256 * a + 256)
-                if hop == 0:
-                    V("tt", "FB XL DIAG", "gm%d gm%d" % (2 * a, 2 * a + 1), T.gm[:, cs], Fwin.indirect(XL[:, ws]),
-                      T.DIAG[:], A.mult, c=ga(256))
-                    V("scan", "RST gm%d gm%d" % (2 * a, 2 * a + 1), "sc%d" % a, T.sc[:, cs], T.RST[:], T.gm[:, cs], 0.0,
-                      A.mult, A.add, c=256)
-                    V("ts", "sc%d" % a, "PL%d" % a, PL[:, ws], T.sc[:, 256 * a + 15:256 * a + 256:16], -OFF, None, A.add)
-                    continue
-                pP = ("pP", "pK")[a]
-                for b in (2 * a, 2 * a + 1):
-                    V("tt", "WT OL DIAG", "gm%d" % b, blk(T.gm, b), T.WT[:, 8 * b:P].indirect(OL[:, 8 * b:8 * b + 8]),
-                      T.DIAG[:, 0:128], A.mult, c=ga(128))
-                    if b:
-                        after("gm")
-                    if hop == 3:
-                        after("dr0", "dr1")
-                    mark("gm")
-                    MM([(T[pP][:, 8 * b:8 * b + 8], blk(T.gm, b), T.g8f[:], True, True, "g8f gm%d" % b)], pP, 256)
-                V("ts", pP, "PL%d" % a, PL[:, ws], T[pP][:, ws], -OFF, None, A.add)
-            thN = "THg" if hop else "THg0"
-            if hop:
-                ACT(T.THg[:], T.THW[:, 0:P].indirect(OL[:, 0:32]), AF.Copy, "THW OL", "THg", ga(512))
-            if hop < 3:
-                MM([(T.pD[:, 0:64], T.idn[:], T.CX1[:, 64 * hop:64 * hop + 64], True, False, "idn CX1"),
-                    (T.pD[:, 0:64], T.idn[:], T.CX2[:], False, False, "idn CX2")]
-                   + [(T.pD[:, 16 * b:16 * b + 16], blk(h, b), T.R2m[:], False, False, "R2m " + hN) for b in range(4)],
-                   "pD")
-                for c0 in range(0, 16, 4):
-                    MM([(T.pD[:, 0:64:2], blk(T.S, c), T[thN][:, c::16], False, False, "S " + thN)
-                        for c in range(c0, c0 + 4)], "pD")
-            else:
-                MM([(T.pE[:, 16 * b:16 + 16 * b], blk(T.THg, b), T.R3[:], True, True, "R3 THg")
-                    for b in range(4)], "pE")
-                V("ts", "pE", "EL", T.EL[:], T.pE[:, 1:64:2], -32.0, None, A.add)
-                ACT(T.thr[:], T.pE[:, 0:64:2], AF.Copy, "pE", "thr", 64)
-                MM([(T.pD[:, 0:32], T.idn[:], T.zb[:, 0:32], True, False, "idn zb")]
-                   + [(T.pD[:, 8 * b:8 * b + 8], blk(T.THg, b), T.R3b[:, 0:8], False, False, "R3b THg")
-                      for b in range(4)], "pD")
-            for a, ws in halves(16):
-                cs = slice(256 * a, 256 * a + 256)
-                V("tt", "hdrS PL%d %s" % (a, hN), "D%d" % a, T.D[:, cs], T.hdrS[:, 0:R].indirect(PL[:, ws]), h[:, cs],
-                  A.max if hop < 3 else A.subtract, c=ga(256))
-                rn = T.RB[:, P + 256 * a:P + 256 * a + 256]
-                if hop < 3:
-                    ACT(rn, T.hdrS[:, 0:R].indirect(PL[:, ws]), AF.Copy, "hdrS PL%d" % a, "Rn%d" % a, ga(256))
-                    MM([(T.pD[:, 16 * b:16 * b + 16], blk(T.RB, 4 + b), T.R2m[:], False, False, "R2m Rn%d" % a)
-                        for b in (2 * a, 2 * a + 1)], "pD")
-                    MM([(T.pD[:, 16 * b:16 * b + 16], blk(T.D, b), T.R2[:], False, b == 3, "R2 D%d" % a)
-                        for b in (2 * a, 2 * a + 1)], "pD")
-                else:
-                    ACT(rn, T.D[:, cs], AF.Abs, "D%d" % a, "Rn%d" % a, 256)
-            if hop < 3:
-                z0, z1 = "Z%d" % hop, "Z%d" % (hop + 1)
-                V("scan", "pD " + z0, z1, T[z1][:], T[z0][:], T.pD[:, 0:64], 0.0, A.max, A.min)
-                V("ts", z1, "q", T.q[:], T[z1][:, 1::2], 15 * 32 + 7, None, A.bitwise_and)
-                V("cp", "q", "OL", OL[:], T.q[:])
-        MM([(T.pD[:, 0:32], blk(T.S, c), T.RB[:, P + c::16], False, c == 15, "S Rn0 Rn1") for c in range(16)], "pD")
-        V("ts", "pD", "qm", T.qm[:], T.pD[:, 0:32], 1.0 / KS, 192.0, A.mult, A.add)
-        V("tt", "pD thr", "ge", T.ge[:], T.pD[:, 0:32], T.thr[:], A.is_ge)
-        V("ts", "qm", "q", T.q[:], T.qm[:], 60, None, A.bitwise_and)
-        V("tt", "q ge", "nd", T.nd[:], T.q[:], T.ge[:], A.min)
-        V("tt", "nd lane", "hl", T.hl[:], T.nd[:], T.lane[:], A.add)
-        V("ts", "hl", "HL", HL[:], T.hl[:], float(P), None, A.mult)
-        for a, ws in halves(16):
-            cs = slice(256 * a, 256 * a + 256)
-            V("tt", "dr%d EL DIAG" % a, "tt%d" % a, T.tt[:, cs], T.DIAG[:, 0:16].indirect(T.EL[:, ws]), T.dr[:, cs],
-              A.mult, c=ga(256))
+    def hop_of(k, a, hop):
+        n = lambda s: s.replace("#", str(a))
+        ws, cs = part(a, 16), part(a, H)
+        hN, pDn, pPn = "hb%d%d" % (k, a), n("pD#"), n("pP#")
+        h, pD, pP, RB, pl = T[hN], T[pDn], T[pPn], T[n("RB#")], T.PL[:, ws]
+        th, thN = (T.THg, n("THg#")) if hop else (T.THg0, "THgc")
+        t0 = H * a if hop else 0
+        if hop:
+            for b in range(2):
+                V("tt", n("WT# OL# DIAG"), n("gm#%d" % b), blk(T.gm, 2 * a + b),
+                  T[n("WT#")][:, 8 * b:P].indirect(T.OL[:, 16 * a + 8 * b:16 * a + 8 * b + 8]), T.DIAG[:, 0:128], A.mult,
+                  c=ga(128))
+                if hop == 3:
+                    after(n("dr#"))
+                MM([(pP[:, 8 * b:8 * b + 8], blk(T.gm, 2 * a + b), T.g8f[:], True, True, n("g8f gm#%d" % b))], pPn, 256)
+            V("ts", pPn, n("PL#"), pl, pP[:, 0:16], -OFF, None, A.add)
+            ACT(T.THg[:, cs], T.THW[:, 0:P].indirect(T.OL[:, ws]), AF.Copy, n("THW OL#"), thN, ga(H))
+        if hop < 3:
+            MM([(pD[:, 0:32], T.idn[:], T.CX1[:, part(hop, 32)], True, False, "idn CX1"),
+                (pD[:, 0:32], T.idn[:], T.CX2[:], False, False, "idn CX2")]
+               + [(pD[:, part(b, 16)], blk(h, b), T.R2m[:], False, False, "R2m " + hN) for b in range(2)], pDn)
+            for c0 in range(0, 16, 4):
+                MM([(pD[:, 0:32:2], blk(T.S, c), th[:, t0 + c:t0 + H:16], False, False, "S " + thN)
+                    for c in range(c0, c0 + 4)], pDn)
+            V("tt", n("hdrS PL# ") + hN, n("D#"), T.D[:, cs], Hwin.indirect(pl), h[:], A.max, c=ga(H))
+            ACT(RB[:, H:], Hwin.indirect(pl), AF.Copy, n("hdrS PL#"), n("Rn#"), ga(H))
+            MM([(pD[:, part(b, 16)], blk(RB, 2 + b), T.R2m[:], False, False, n("R2m Rn#")) for b in range(2)], pDn)
+            MM([(pD[:, part(b, 16)], blk(T.D, 2 * a + b), T.R2[:], False, b == 1, n("R2 D#")) for b in range(2)], pDn)
+            z0, z1 = (T["Z%d" % hop][:, part(a, 32)], n("Z%d#" % hop)) if hop else (T.Z0[:], "Z0"), T["Z%d" % (hop + 1)]
+            V("scan", pDn + " " + z0[1], n("Z%d#" % (hop + 1)), z1[:, part(a, 32)], z0[0], pD[:, 0:32], 0.0, A.max, A.min)
+            V("ts", n("Z%d#" % (hop + 1)), n("q#"), T.q[:, ws], z1[:, 32 * a + 1:32 * a + 32:2], 15 * 32 + 7, None,
+              A.bitwise_and)
+            V("cp", n("q#"), n("OL#"), T.OL[:, ws], T.q[:, ws])
+            return
+        MM([(pP[:, 32 + 16 * b:48 + 16 * b], blk(T.THg, 2 * a + b), T.R3[:], True, True, "R3 " + thN) for b in range(2)],
+           pPn)
+        V("ts", pPn, n("EL#"), T.EL[:, ws], pP[:, 33:64:2], -32.0, None, A.add)
+        ACT(T.thr[:, ws], pP[:, 32:64:2], AF.Copy, pPn, n("thr#"), 64)
+        MM([(pD[:, 0:16], T.idn[:], T.zb[:, 0:16], True, False, "idn zb")]
+           + [(pD[:, part(b, 8)], blk(T.THg, 2 * a + b), T.R3b[:, 0:8], False, False, "R3b " + thN) for b in range(2)],
+           pDn)
+        V("tt", n("hdrS PL# ") + hN, n("D#"), T.D[:, cs], Hwin.indirect(pl), h[:], A.subtract, c=ga(H))
+        ACT(RB[:, H:], T.D[:, cs], AF.Abs, n("D#"), n("Rn#"), H)
+        MM([(pD[:, 0:16], blk(T.S, c), RB[:, H + c::16], False, c == 15, n("S Rn#")) for c in range(16)], pDn)
+        V("ts", pDn, n("qm#"), T.qm[:, ws], pD[:, 0:16], 1.0 / KS, 192.0, A.mult, A.add)
+        ge, q2 = T.gl[:, 32 * a:32 * a + 32:2], T.q2[:, 32 * a + 1:32 * a + 32:2]
+        V("tt", n("pD# thr# gl"), n("ge#"), ge, pD[:, 0:16], T.thr[:, ws], A.is_ge)
+        V("ts", n("qm# q2"), n("q2#"), q2, T.qm[:, ws], 60, None, A.bitwise_and)
+        V("tt", n("q2# ge#"), n("nd#"), T.nd[:, ws], q2, ge, A.min)
+        V("tt", n("dr# EL# DIAG"), n("tt#"), T.tt[:, cs], T.DIAG[:, 0:16].indirect(T.EL[:, ws]), T.dr[:, cs], A.mult,
+          c=ga(H))
 
-        MM([(T.pW[:], T.idn[:], h[:], True, False, "idn " + hN),
-            (T.pW[:], T.idh[:], T.D[:], False, True, "idh D0 D1")], "pW", 512)
-        for a, cs in halves(256):
-            ACT(T.y[:, cs], T.pW[:, 8 * a:8 * a + 8, :], AF.Identity, "pW", "y%d" % a, 256, bias=BIG, scale=1.0 - 2.0 ** -11)
-            ACT(T.RB[:, cs], T.y[:, cs], AF.Copy, "y%d" % a, "B%d" % a, 256, bias=-BIG)
-        hn, nx, arr, loc = "hn%d" % k, "hb%d" % (k + 1), "arr%d" % k, "loc%d" % k
-        V("cp", "B0 B1 Rn0 Rn1 HL", hn + "a", T[hn][:, 0:256], T.RB[:, 0:W].indirect(HL[:, 0:16]), c=ga(256))
-        ACT(T[hn][:, 256:], T.RB[:, 0:W].indirect(HL[:, 16:32]), AF.Copy, "B0 B1 Rn0 Rn1 HL", hn + "b", ga(256))
-        rds = [hn + "a", hn + "b"]
-        node("P", [((lambda hn=hn, nx=nx, arr=arr, loc=loc: g.remote_dma(
-            T[nx][:], T[hn][:], T.sem[arr], T.sem[loc], pid, rid, emask)), rds)], rds, [nx], SEND, FLY, (arr, 0))
+    def finish(k, a):
+        n = lambda s: s.replace("#", str(a))
+        ws, cs, ns = part(a, 16), part(a, H), part(a, 144)
+        hN, pPn, pRn = "hb%d%d" % (k, a), n("pP#"), n("pR#")
+        pX, pR, RB = T[pPn][:, H:], T[pRn], T[n("RB#")]
+        V("scan", n("q2# ge#"), n("hl#"), T.hl[:, part(a, 32)], T.q2[:, part(a, 32)], T.gl[:, part(a, 32)], 0.0,
+          A.min, A.add)
+        V("ts", n("hl#"), n("HL#"), T.HL[:, ws], T.hl[:, 32 * a + 1:32 * a + 32:2], float(H), None, A.mult)
+        MM([(pX, T.idn[:], T[hN][:], True, False, "idn " + hN), (pX, T.idh[:], T.D[:, cs], False, True, n("idh D#"))],
+           pPn, H)
+        ACT(T.y[:, cs], pX, AF.Identity, pPn, n("y#"), H, bias=BIG, scale=1.0 - 2.0 ** -11)
+        ACT(RB[:, 0:H], T.y[:, cs], AF.Copy, n("y#"), n("B#"), H, bias=-BIG)
+        hn, nx, arr, loc = ["%s%d%d" % (s, j, a) for s, j in (("hn", k), ("hb", k + 1), ("arr", k), ("loc", k))]
+        ACT(T[hn][:], RB[:, 0:P].indirect(T.HL[:, ws]), AF.Copy, n("B# Rn# HL#"), hn, ga(H))
+        node("P", [((lambda: g.remote_dma(T[nx][:], T[hn][:], T.sem[arr], T.sem[loc], pid, rid, emask)), [hn])],
+             [hn], [nx], SEND, FLY, (arr, 0))
         nodes[-1]["remote"] = [(arr, n_eng), (loc, n_eng)]
-        MM([(T.pU[:, 10 * j:288:9], T.idK[:], T.nd[:, 0:32 - j], False, False, "idK nd") for j in range(1, 8)]
-           + [(T.pU[:, 8:288:9], T.idL[:], T.nd[:], False, True, "idL nd")], "pU")
-        V("scan", "rst9 pU", "ls", T.ls[:], T.rst9[:], T.pU[:, 0:288], 0.0, A.mult, A.max, c=288)
-        V("ts", "ls pcol", "SL", SL[:], T.ls[:, 8::9], pc, None, A.add)
+        MM([(pR[:, 10 * j:144:9], T.idK[:], T.nd[:, 16 * a:16 * a + 16 - j], False, False, n("idK nd#"))
+            for j in range(1, 8)] + [(pR[:, 8:144:9], T.idL[:], T.nd[:, ws], False, True, n("idL nd#"))], pRn)
+        V("scan", "rst9 " + pRn, n("ls#"), T.ls[:, ns], T.rst9[:], pR[:, 0:144], 0.0, A.mult, A.max, c=144)
+        V("ts", n("ls# pcol"), n("SL#"), T.SL[:, ws], T.ls[:, 144 * a + 8:144 * a + 144:9], pc, None, A.add)
         tab, col = "TB", "ra"
         if k == STEPS - 1:
             tab, col = "yoS", "rl"
-            for hf, cs in halves():
+            ACT(T.rl[:, cs], T.ra[:, cs], AF.Copy, n("ra#"), n("rl#"), H, bias=-OFF)
+        for j in (2 * a + 1, 2 * a):
+            sl = T.SL[:, part(j, 8)]
+            V("tt", n("SL# tt# %s# %s" % (col, tab)), tab, T[tab][:, 0:W + 128].indirect(sl), blk(T.tt, j),
+              blk(T[col], j), A.add, c=60 + 128 * SCATTER)
+            op("A", lambda sl=sl: g.scalar.activation(T.RW[:, 0:W + 128].indirect(sl), T.zero[:], AF.Silu),
+               [n("SL#"), "zero", "RW"], ["RW"], (70 + 128 * SCATTER) * CYC)
+
+    for k in range(STEPS):
+        if k == STEPS - 1:
+            for hf in range(2):
+                cs = part(hf, 512)
                 ACT(T.AL[:, cs], T.TB[:, cs], AF.Abs, "TB", "AL%d" % hf)
                 ACT(T.yoS[:, cs], T.AL[:, cs], AF.Copy, "AL%d" % hf, "yoS", bias=-OFF)
-            for a, cs in halves(256):
-                ACT(T.rl[:, cs], T.ra[:, cs], AF.Copy, "ra%d" % a, "rl%d" % a, 256, bias=-OFF)
-        for j in reversed(range(4)):
-            cs, sl = slice(128 * j, 128 * j + 128), SL[:, 8 * j:8 * j + 8]
-            V("tt", "SL tt%d %s%d %s" % (j // 2, col, j // 2, tab), tab, T[tab][:, 0:W + 128].indirect(sl),
-              T.tt[:, cs], T[col][:, cs], A.add, c=60 + 128 * SCATTER)
-            op("A", lambda sl=sl: g.scalar.activation(T.RW[:, 0:W + 128].indirect(sl), T.zero[:], AF.Silu),
-               ["SL", "zero", "RW"], ["RW"], (70 + 128 * SCATTER) * CYC)
+        for a in (1, 0):
+            start(k, a)
+        for hop in range(4):
+            for a in (1, 0):
+                hop_of(k, a, hop)
+        for a in (1, 0):
+            finish(k, a)
         if k < STEPS - 1:
             tables()
 
-    for hf, cs in halves():
-        dma(T.yo[:, cs], T.yoS[:, cs], "st_yo%d" % hf, ["yoS"], [], 4000)
+    for hf in range(2):
+        dma(T.yo[:, part(hf, 512)], T.yoS[:, part(hf, 512)], "st_yo%d" % hf, ["yoS"], [], 4000)
+        dma(T.yh[:, part(hf, H)], T["hb%d%d" % (STEPS, hf)][:], "st_yh%d" % hf, ["hb%d%d" % (STEPS, hf)], [])
     ACT(T.ymS[:], T.RW[:, 0:W], AF.Copy, "RW", "ymS", 1024, bias=1.0, scale=-1.0)
     dma(T.ym[:], T.ymS[0::16, :], "st_ym", ["ymS"], [])
-    dma(T.yh[:], T["hb%d" % STEPS][:], "st_yh", ["hb%d" % STEPS], [])
     if not ORDER:
         ORDER.extend(schedule())
     issue(ORDER)

@@ -14,52 +14,61 @@ def sb(dtype, cols, names):
 
 sb(BF, R, "hdrS")
 sb(I32, W, "owS")
-sb(I32, 64, "mkS")
-sb(BF, 64, "mkB")
-sb(F32, W, "o4 G AL ymS")
+sb(I32, 256, "mkS")
+sb(BF, 256, "mkB")
+sb(BF, 512, "U hb0")
+sb(BF, 128, "wR")
+sb(I32, 128, "thR")
+sb(F32, 128, "thF")
+sb(F32, W, "G ymS")
 sb(F32, W + 128, "TB RW yoS")
 sb(F32, W + 16, "FB")
-sb(BF, 2048, "S WS U")
+sb(BF, 512, "S WS WN")
+sb(BF, 64, "R2 R2m R3b")
 sb(BF, 128, "ones bones idn idh idm idK idL tmpa LT prm")
 sb(F32, 128, "permf zero idf idg")
-sb(BF, 16, "wS R2 R2m R3 R3b")
-sb(F32, 8, "g8f")
-sb(I32, 8, "thS pi ci ta tb")
-sb(F32, 8, "pcol c32 taf tbf s32 wa wb wc wd")
+sb(BF, 16, "wS wN R3")
+sb(F32, 8, "g8f one")
+sb(I32, 8, "thS pi ci ta")
+sb(F32, 8, "pcol c32 taf wa wb wc wd")
 sb(F32, 256, "jmod DIAG RST")
 sb(F32, 144, "rst9")
 sb(BF, 144, "zb CKa CK")
 sb(F32, 288, "ls")
 sb(BF, 288, "AD")
-sb(F32, 32, "Z0")
-sb(I32, 64, "Z1 Z2 Z3")
-sb(BF, 32, "CX2")
-sb(BF, 96, "CX1")
+sb(I32, 128, "DZ")
+sb(I32, 256, "DY Z")
+sb(BF, 128, "CX1 CX2 CU idF")
+sb(BF, 64, "CM CF")
+sb(F32, 64, "DH im")
+sb(F32, 128, "DU")
 sb(F32, 16, "base gcol")
 sb(F32, 32, "thr")
 sb(F32, 64, "gl hl")
-sb(F32, P, "pU pD0 pD1 pP0 pP1 pR0 pR1 gm sc ra rl WT0 WT1 dr tt y")
+sb(F32, P, "pU pD0 pD1 pP0 pP1 pR0 pR1 gm sc ra WT0 WT1 dr tt y")
 SCRATCH["pW"] = ("psum", [128, 16, 32], F32)
 sb(BF, P, "D THW THg RB0 RB1")
 sb(BF, H, "THg0")
-for k in range(STEPS + 1):
-    sb(BF, H, "hb%d0 hb%d1" % (k, k))
 for k in range(STEPS):
-    sb(BF, H, "hn%d0 hn%d1" % (k, k))
-sb(I32, 32, "ui zz qm q")
+    sb(BF, P, "hb%d hn%d" % (k + 1, k))
+sb(I32, 32, "zz")
 sb(I32, 64, "q2")
-sb(I32, 96, "ua ub sq")
+sb(I32, 128, "qm")
+sb(I32, 256, "ui")
+sb(I32, 72, "uq0 uq1")
+sb(I32, 128, "sq")
 sb(BF, 32, "key nd")
-sb(U16, 32, "XL PL OL OL0 SL HL EL")
-LOADS = ["marks", "owner", "w", "th", "h0", "h1", "hdr"]
+sb(U16, 32, "XL0 XL1 XL2 XO0 XO1 PL OL OL0 SL HL EL")
+LOADS = ["marks", "owner", "w", "th", "h0", "hdr"]
 SEMAPHORES = ["V", "A", "T", "P"] + ["ld_" + n for n in LOADS] \
-    + ["%s%d%d" % (n, k, a) for n in ("arr", "loc") for k in range(STEPS) for a in range(2)] \
-    + ["st_yo0", "st_yo1", "st_ym", "st_yh0", "st_yh1"]
-OFF = 4096.0
-KS, HUGE = 2.0 ** 18, 2.0 ** 30
+    + ["%s%d%d" % (n, k, a) for n in ("arrh", "loch") for k in range(STEPS) for a in range(2)] \
+    + ["%s%d" % (n, k) for n in ("arrx", "locx") for k in range(STEPS - 1)] \
+    + ["arrw", "locw", "st_yo", "st_ym", "st_yh"]
+KS, HUGE = 2.0 ** 18, 3 * 2.0 ** 29
+FAR = 2.0 ** 32
 BIG = 8388608.0
-CYC, PE, GATHER, SCATTER, WAKE, DMA, SEND, FLY = 0.87, 0.44, 1.4, 3.4, 200, 2000, 1000, 1800
-ROUNDS = 4000
+CYC, PE, GATHER, SCATTER, WAKE, DMA, SEND, FLY = 0.87, 0.44, 1.4, 3.4, 200, 2000, 1200, 2400
+ROUNDS, SLACK = 20000, 15.0
 ORDER = []
 
 
@@ -126,15 +135,21 @@ def rank_program(g, core, T, topo):
             ps.pop(i, None)
             for p, gap in ps.items():
                 preds[i][p] = succ[p][i] = gap + nodes[p]["lat"]
+            if d["early"] and i:
+                preds[i][i - 1] = succ[i - 1][i] = 0.0
             for r in d["r"]:
                 rd.setdefault(r, []).append(i)
             for w in d["w"]:
                 lastw[w] = [i]
                 rd[w] = []
 
-        def place(order):
-            end, ready, busy = [0.0] * n, [0.0] * n, {q: [(1e18, 1e18, -1)] for q in queues}
-            for i in order:
+        def place(order, keep, end, ready):
+            end, ready, busy = list(end), list(ready), {q: [] for q in queues}
+            for i in order[:keep]:
+                busy[nodes[i]["q"]].append((end[i] - nodes[i]["cost"], end[i], i))
+            for line in busy.values():
+                line.append((1e18, 1e18, -1))
+            for i in order[keep:]:
                 cost, line = nodes[i]["cost"], busy[nodes[i]["q"]]
                 t = ready[i] = max([end[p] + gap for p, gap in preds[i].items()] + [0.0])
                 at = len(line) - 1
@@ -149,23 +164,34 @@ def rank_program(g, core, T, topo):
             return end, ready, ahead
 
         rnd = numpy.random.RandomState(0)
-        extra, best, chain = [0.0] * n, None, []
-        for _ in range(ROUNDS):
-            ex = list(extra)
-            for _ in range(2 ** rnd.randint(4) if chain else 0):
-                i = chain[rnd.randint(len(chain))] if rnd.randint(2) else rnd.randint(n)
-                ex[i] += rnd.randn() * 100.0 * 4 ** rnd.randint(3)
-            rest = [0.0] * n
-            for i in range(n - 1, -1, -1):
-                rest[i] = max(1.0, nodes[i]["cost"] + ex[i]) \
-                    + max([rest[s] + gap for s, gap in succ[i].items()] + [rest[s] for s in soft.get(i, [])]
-                          + [nodes[i]["lat"]])
-            end, ready, ahead = place(sorted(range(n), key=lambda i: (-rest[i] - nodes[i]["early"], i)))
+        rest = [0.0] * n
+        for i in range(n - 1, -1, -1):
+            rest[i] = nodes[i]["cost"] + max([rest[s] + gap for s, gap in succ[i].items()]
+                                             + [rest[s] for s in soft.get(i, [])] + [nodes[i]["lat"]])
+        order = sorted(range(n), key=lambda i: (-rest[i] - nodes[i]["early"], i))
+        best, now, chain, lo, times = None, None, [], 0, ([0.0] * n, [0.0] * n)
+        for r in range(ROUNDS):
+            new = order
+            if chain:
+                i, back = chain[rnd.randint(len(chain))], rnd.rand() < 0.5
+                i = rnd.randint(n) if rnd.rand() > 0.7 else before.get(i, i) if back else i
+                pos, far = {v: j for j, v in enumerate(order)}, (2, 5, 10, 25, 60)[rnd.randint(5)]
+                lo, hi = (pos[i], pos[i] + far) if back else (max(0, pos[i] - far), pos[i])
+                need, todo = {i}, [i]
+                while todo:
+                    more = [p for p in (succ if back else preds)[todo.pop()] if lo <= pos[p] <= hi and p not in need]
+                    need.update(more)
+                    todo += more
+                new = order[:lo] + sorted(order[lo:hi + 1], key=lambda v: (v in need) == back) + order[hi + 1:]
+            end, ready, ahead = place(new, lo, *times)
             i = max(range(n), key=lambda j: end[j] + nodes[j]["lat"])
-            if best is not None and end[i] + nodes[i]["lat"] > best[0]:
+            span = end[i] + nodes[i]["lat"]
+            if now is not None and span > now + SLACK * (1.0 - r / ROUNDS) * rnd.exponential():
                 continue
-            best = (end[i] + nodes[i]["lat"], sorted(range(n), key=lambda j: (end[j] - nodes[j]["cost"], j)))
-            extra, chain = ex, [i]
+            now, order, chain = span, sorted(range(n), key=lambda j: (end[j] - nodes[j]["cost"], j)), [i]
+            before, times = ahead, (end, ready)
+            if best is None or span < best[0]:
+                best = (span, order)
             while end[i] - nodes[i]["cost"] - ready[i] > 1.0 or preds[i]:
                 late = end[i] - nodes[i]["cost"] - ready[i] > 1.0
                 i = ahead[i] if late else max(preds[i], key=lambda p: end[p] + preds[i][p])
@@ -230,13 +256,12 @@ def rank_program(g, core, T, topo):
         return buf[:, 128 * c:128 * c + 128]
 
     c1 = slice(0, 1)
-    dma(T.mkS[:], T.marks[:], "ld_marks", [], ["mkS"], early=9e6)
+    dma(T.mkS[0:32, :], T.marks[:], "ld_marks", [], ["mkS"], early=9e6)
     dma(T.owS[:], T.owner[:], "ld_owner", [], ["owS"], 4000, early=8e6)
-    dma(T.wS[:, c1], T.w[:], "ld_w", [], ["wS"], 4200, early=7e6)
-    dma(T.thS[:, c1], T.th[:], "ld_th", [], ["thS"], 4200, early=6e6)
-    for a in range(2):
-        dma(T["hb0%d" % a][:], T.h0[:, part(a, H)], "ld_h%d" % a, [], ["hb0%d" % a], 4700, early=5e6)
-    dma(T.hdrS[:], T.hdr[:], "ld_hdr", [], ["hdrS"], 12000)
+    dma(T.wR[0:1, :], T.w[:], "ld_w", [], ["wR"], 4200, early=7e6)
+    dma(T.thR[0:1, :], T.th[:], "ld_th", [], ["thR"], 4200, early=6e6)
+    dma(T.hb0[:], T.h0[:], "ld_h0", [], ["hb00", "hb01"], 4700, early=5e6)
+    dma(T.hdrS[:], T.hdr[:], "ld_hdr", [], ["hdrS"], 7000, early=1.0)
 
     def iota(buf, name, pattern, base, cm, c):
         op("P", lambda: g.iota(buf, pattern, base, cm, allow_small_or_imprecise_dtypes=True), [], [name], 140 + 2 * c)
@@ -254,35 +279,49 @@ def rank_program(g, core, T, topo):
     iota(T.base[:], "base", [[16, 16]], 0, 0, 16)
     sel(T.prm[:], T.ones[:], [[-1, 16], [-16, 8]], A.is_equal, 0, 1, "ones", "perm", 128)
     iota(T.gcol[:], "gcol", [[0, 2], [1, 8]], 0, 0, 16)
-    for hop in range(3):
-        V("ms", "", "CX1", T.CX1[:, 32 * hop:32 * hop + 32:2], 0.0)
-        V("ms", "", "CX1", T.CX1[:, 32 * hop + 1:32 * hop + 32:2], max(512.0, 33792.0 * hop))
+    iota(T.im[:], "im", [[0, 16], [1, 4]], 0, 0, 64)
     iota(T.rst9[:], "rst9i", [[0, 16], [1, 9]], 0, 0, 144)
     ACT(T.zero[:], T.ones[:], AF.Silu, "ones", "zero", 1400, scale=0.0)
     V("ms", "", "zb", T.zb[:], 0.0)
-    iota(T.CKa[:], "CKa", [[0, 2], [16, 8], [0, 9]], -W, 0, 144)
-    sel(T.CK[:], T.CKa[:], [[0, 2], [1, 8], [-1, 9]], A.is_ge, 0, 0, "CKa", "CK", 144, -4.0 * W)
+    iota(T.CKa[:], "CKa", [[0, 2], [1, 8], [0, 9]], -64, 0, 144)
+    sel(T.CK[:], T.CKa[:], [[0, 2], [1, 8], [-1, 9]], A.is_ge, 0, 0, "CKa", "CK", 144, -256.0)
     V("ms", "", "CK", T.CK[:, 0::9], 0.0)
-    V("ts", "CKa", "CK", T.CK[:, 8::9], T.CKa[:, 8::9], 2.0 * W, None, A.add)
+    V("ts", "CKa", "CK", T.CK[:, 8::9], T.CKa[:, 8::9], 128.0, None, A.add)
     g8 = T.bones[:, 0::16]
     V("ts", "pi", "ci", T.ci[:, c1], T.pi[:, c1], 15, None, A.bitwise_and)
     V("cp", "ci", "pcol", pc, T.ci[:, c1])
     V("ts", "jmod pcol", "DIAG", T.DIAG[:], T.jmod[:], pc, None, A.is_equal, c=256)
-    for c in range(16):
-        ACT(blk(T.U, c), T.bones[:], AF.Identity, "bones DIAG", "U", 128, scale=T.DIAG[:, c:c + 1])
-    V("ms", "", "S", T.S[:], 0.0, c=1024)
-    for c in range(16):
-        ACT(T.S[:, 129 * c:128 * (c + 1):16], g8, AF.Copy, "bones", "S", 64, scale=KS)
-    for hf in range(2):
-        cs = part(hf, 1024)
-        V("ts", "S wS", "WS%d" % hf, T.WS[:, cs], T.S[:, cs], T.wS[:, c1], 1.0 / KS, A.mult, A.mult, c=512)
-    V("ts", "mkS", "mkB", T.mkB[:], T.mkS[:], 2.0, -1.0, A.mult, A.add)
+    V("ms", "", "U", T.U[0:32, :], 1.0, c=256)
+    sel(T.U[0:32, :], T.U[0:32, :], [[-1, 4], [-4, 8], [0, 16]], A.is_equal, 0, 1, "U", "U", 512)
+    V("cp", "thR", "thF", T.thF[0:1, :], T.thR[0:1, :], c=128)
+    V("ms", "", "one", T.one[0:1, c1], 1.0)
+    MM([(T.pP0[:, 0:1], T.wR[0:1, :], T.ones[0:1, c1], True, True, "wR ones")], "pP0")
+    MM([(T.pP1[:, 0:1], T.thF[0:1, :], T.one[0:1, c1], True, True, "thF one")], "pP1", 256)
+    V("cp", "pP1", "thS", T.thS[:, c1], T.pP1[:, 0:1])
+    V("ms", "", "S", T.S[:], 0.0, c=256)
+    for r in range(4):
+        ACT(T.S[:, 129 * r:128 * (r + 1):4], T.bones[:, r::4], AF.Copy, "bones", "S", 64, scale=KS)
+    V("ts", "S pP0", "WS", T.WS[:], T.S[:], T.pP0[:, 0:1], 1.0 / KS, A.mult, A.mult, c=256)
+    c2 = slice(1, 2)
+    V("ts", "ci", "ci2", T.ci[:, c2], T.ci[:, c1], 2, None, A.arith_shift_right)
+    V("cp", "ci2", "pq", T.pcol[:, c2], T.ci[:, c2])
+    V("ts", "im pq", "CF", T.CF[:], T.im[:], T.pcol[:, c2], FAR, A.not_equal, A.mult)
+    V("ts", "CF", "CM", T.CM[:], T.CF[:], 256.0 * KS, None, A.add)
+    V("cp", "CF", "CU", T.CU[:, 0::2], T.CF[:])
+    V("ts", "CF", "CU", T.CU[:, 1::2], T.CF[:], 2.0 ** 21, None, A.add)
+    V("cp", "CF", "CX1", T.CX1[:, 0::2], T.CF[:])
+    V("ms", "", "CX1", T.CX1[:, 1::2], FAR)
+    V("ms", "CX1", "CX1", T.CX1[:, 7::8], 512.0)
+    V("ms", "", "CX2", T.CX2[:], 0.0)
+    for n, step, kind in (("DZ", 8, int), ("DY", 8, int), ("DU", 8, float), ("DH", 4, float)):
+        V("ms", "", n, T[n][:], kind(-HUGE), c=128)
+        V("ms", n, n, T[n][:, 0::step], kind(HUGE))
+    V("ts", "mkS", "mkB", T.mkB[0:32, :], T.mkS[0:32, :], 2.0, -1.0, A.mult, A.add, c=256)
     for hf in range(2):
         cs, bank = part(hf, 512), "pR%d" % hf
-        MM([(T[bank][:, 64 * c:64 * c + 64], blk(T.U, 8 * hf + c), T.mkB[:], True, True, "U mkB") for c in range(8)],
-           bank)
-        V("ts", "owS", "o4_%d" % hf, T.o4[:, cs], T.owS[:, cs], OFF, None, A.add, c=512)
-        V("tt", "o4_%d %s" % (hf, bank), "TB", T.TB[:, cs], T.o4[:, cs], T[bank][:], A.mult, c=512)
+        MM([(T[bank][:, part(c, 256)], T.U[0:32, part(2 * hf + c, 128)], T.mkB[0:32, :], True, True, "U mkB")
+            for c in range(2)], bank, 256)
+        V("tt", "owS " + bank, "TB", T.TB[:, cs], T.owS[:, cs], T[bank][:], A.mult, c=512)
         ACT(T.RW[:, cs], T[bank][:], AF.Copy, bank, "RW", bias=0.5, scale=-0.5)
 
     def tables():
@@ -300,33 +339,31 @@ def rank_program(g, core, T, topo):
 
     V("ts", "jmod", "RST", T.RST[:], T.jmod[:], 0.0, None, A.not_equal, c=256)
     V("ms", "", "q2", T.q2[:], 0)
-    V("ms", "", "ua", T.ua[:], 32)
-    V("ms", "", "ub", T.ub[:], 1)
     for a in range(2):
+        for j, v in enumerate((0, 1, 0, 32)):
+            V("ms", "", "uq%d" % a, T["uq%d" % a][:, j::4], v)
         V("ts", "base pcol", "gl", T.gl[:, 32 * a + 1:32 * a + 32:2], T.base[:], pc, 1.0 / H, A.add, A.mult)
-    V("ms", "ub", "ub", T.ub[:, 0::3], 0)
     V("ts", "rst9i", "rst9", T.rst9[:], T.rst9[:], 0.0, None, A.not_equal, c=144)
     V("ts", "pcol", "c32", T.c32[:, c1], pc, 32.0, None, A.mult)
     V("ts", "gcol c32", "OL0", T.OL0[:, 0:16], T.gcol[:], T.c32[:, c1], None, A.add)
-    V("ms", "", "Z0", T.Z0[:], HUGE)
-    V("cp", "OL0 Z0", "Z0", T.Z0[:, 1::2], T.OL0[:, 0:16])
-    V("ms", "", "CX2", T.CX2[:], 0.0)
-    V("cp", "gcol CX2", "CX2", T.CX2[:, 1::2], T.gcol[:])
-    for n, f in (("idf", 1.0), ("idg", -1.0), ("idh", 0.5), ("idm", -1.0), ("idK", 2.0 * W), ("idL", -2.0 * W)):
+    V("cp", "OL0 DZ", "DZ", T.DZ[:, 7::8], T.OL0[:, 0:16])
+    V("cp", "gcol CX2", "CX2", T.CX2[:, 7::8], T.gcol[:])
+    for n, f in (("idf", 1.0), ("idg", -1.0), ("idh", 0.5), ("idm", -1.0), ("idK", 128.0), ("idL", -128.0),
+                 ("idF", FAR)):
         ACT(T[n][:], T.idn[:], AF.Copy, "idn", n, 128, scale=f)
     ACT(T.permf[:], T.prm[:], AF.Copy, "perm", "permf", 128)
     ACT(T.g8f[:], g8, AF.Copy, "bones", "g8f", 64)
     for n, f in (("R2", 2.0), ("R2m", -1.0)):
-        ACT(T[n][:, 0::2], g8, AF.Copy, "bones", n, 64, scale=f * KS)
-        ACT(T[n][:, 1::2], g8, AF.Copy, "bones", n, 64, scale=f * 8.0)
+        ACT(T[n][:, 0::2], T.bones[:, 0::4], AF.Copy, "bones", n, 64, scale=f * KS)
+        ACT(T[n][:, 1::2], T.bones[:, 0::4], AF.Copy, "bones", n, 64, scale=0.0)
+        ACT(T[n][:, 7::8], g8, AF.Copy, "bones " + n, n, 64, scale=f * 8.0)
     V("ts", "thS", "ta", T.ta[:, c1], T.thS[:, c1], 8192 - 64, None, A.bitwise_and)
-    V("ts", "thS", "tb", T.tb[:, c1], T.thS[:, c1], 63, None, A.bitwise_and)
-    V("ts", "ta", "taf", T.taf[:, c1], T.ta[:, c1], -1.0, None, A.mult)
-    V("ts", "tb", "tbf", T.tbf[:, c1], T.tb[:, c1], -1.0, None, A.mult)
-    V("ts", "pcol", "s32", T.s32[:, c1], pc, 32.0, 1.0 / 64, A.add, A.mult)
+    V("ts", "thS", "tb", T.ta[:, c2], T.thS[:, c1], 63, None, A.bitwise_and)
+    V("ts", "ta tb", "taf", T.taf[:, 0:2], T.ta[:, 0:2], -1.0, None, A.mult)
+    V("ts", "pcol", "s32", T.taf[:, 2:3], pc, 32.0, 1.0 / 64, A.add, A.mult)
     V("ms", "", "LT", T.LT[:], 0.0)
-    for t, n in enumerate(("taf", "tbf", "s32")):
-        ACT(T.LT[:, t::16], T.ones[:, 0:8], AF.Identity, "ones " + n, "LT", 64, scale=T[n][:, c1])
+    for t in range(3):
+        ACT(T.LT[:, t::16], T.ones[:, 0:8], AF.Identity, "ones taf s32", "LT", 64, scale=T.taf[:, t:t + 1])
     MM([(T.pW[:, :, 8 * b:8 * b + 8], T.LT[:], T.prm[:], True, True, "LT perm") for b in range(4)], "pW", 128)
     ACT(T.THW[:], T.pW[:], AF.Copy, "pW", "THW")
     V("ts", "pcol", "wc", T.wc[:, c1], pc, 2.0, 64.0, A.is_equal, A.mult)
@@ -335,45 +372,68 @@ def rank_program(g, core, T, topo):
     V("tt", "wb wd", "wa", T.wa[:, c1], T.wb[:, c1], T.wd[:, c1], A.add)
     ACT(T.R3[:, 0::2], g8, AF.Identity, "bones wa", "R3", 64, scale=T.wa[:, c1])
     ACT(T.R3[:, 1::2], g8, AF.Identity, "bones wc", "R3", 64, scale=T.wc[:, c1])
-    ACT(T.R3b[:, 0:8], g8, AF.Identity, "bones wb", "R3b", 64, scale=T.wb[:, c1])
+    ACT(T.R3b[:, 0:32], T.bones[:, 0::4], AF.Identity, "bones wb", "R3b", 64, scale=T.wb[:, c1])
     ACT(T.THg0[:], T.THW[:, 0:P].indirect(T.OL0[:, 0:16]), AF.Copy, "THW OL0", "THgc", ga(H))
     tables()
 
     dst = T.cores[(rank + SHIFT) % N]
-    rid, pid, _ = topo.addr(dst)
-    emask = topo.mask(core, dst)
-    n_eng = len(topo.engines(core, dst))
     Fwin, Gwin, Hwin = T.FB[:, 8:8 + W], T.G[:, 0:W], T.hdrS[:, 0:R]
 
-    def start(k, a):
+    def send(out, in_, reads, writes, name, to, fly):
+        rid, pid, _ = topo.addr(to)
+        count = len(topo.engines(core, to))
+        node("P", [((lambda: g.remote_dma(out, in_, T.sem["arr" + name], T.sem["loc" + name], pid, rid,
+                                          topo.mask(core, to))), reads)], reads, writes.split(), SEND, fly, (name, 0))
+        nodes[-1]["remote"] = [("arr" + name, count), ("loc" + name, count)]
+
+    def wrap(out, mat, mN, src, first, sN, bank, stop):
+        MM([(out, blk(mat, r), src[:, first + r:first + H:4], False, stop and r == 3, mN + " " + sN) for r in range(4)],
+           bank)
+
+    def address(a, ui, out, oN):
         n = lambda s: s.replace("#", str(a))
+        uq = T[n("uq#")]
+        V("ts", n("ui# uq#"), n("uq#"), uq[:, 2:64:4], ui, 4095, None, A.bitwise_and)
+        V("scan", n("uq#"), n("sq#"), T.sq[:, part(a, 64)], uq[:, 0:64], uq[:, 2:66], 0.0, A.mult, A.add)
+        V("ts", n("sq#"), n("zz#"), T.zz[:, part(a, 16)], T.sq[:, 64 * a + 2:64 * a + 64:4], 9, 63,
+          A.arith_shift_right, A.bitwise_and)
+        V("ts", n("zz# pcol"), oN, out, T.zz[:, part(a, 16)], 16.0, pc, A.mult, A.add)
+
+    def h0_of(k, a):
+        return H * a
+
+    def key_of(k, a, n):
+        return T.key[:, 16 * a:16 * a + n]
+
+    V("cp", "pP0", "wS", T.wS[:, c1], T.pP0[:, 0:1])
+    send(T.wN[:, c1], T.wS[:, c1], ["wS"], "wN", "w", T.cores[(rank - SHIFT) % N], FLY - 700)
+    V("ts", "S wN", "WN", T.WN[:], T.S[:], T.wN[:, c1], 1.0 / KS, A.mult, A.mult, c=256)
+    for a in (1, 0):
+        pD = "pD%d" % a
+        MM([(T[pD][:, 0:64], T.idn[:], T.CF[:], True, False, "idn CF")], pD)
+        wrap(T[pD][:, 0:64], T.WS, "WS", T.hb0, H * a, "hb0%d" % a, pD, True)
+        V("scan", pD + " DH", "ui%d" % a, T.ui[:, 128 * a:128 * a + 64], T.DH[:], T[pD][:, 0:64], 0.0, A.max, A.min)
+        address(a, T.ui[:, 128 * a + 3:128 * a + 64:4], T.XL0[:, part(a, 16)], "XL0%d" % a)
+
+    def start(k, a):
+        n = lambda s: s.replace("XL", "XL%d" % k).replace("#", str(a))
         ws, cs, ns = part(a, 16), part(a, H), part(a, 144)
-        hN, pD, pR = "hb%d%d" % (k, a), n("pD#"), n("pR#")
-        xl, zz, key = T.XL[:, ws], T.zz[:, ws], T.key[:, ws]
-        MM([(T[pD][:, 0:16], blk(T.WS, c), T[hN][:, c::16], c == 0, c == 15, "WS%d %s" % (c // 8, hN))
-            for c in range(16)], pD)
-        V("cp", pD, n("ui#"), T.ui[:, ws], T[pD][:, 0:16])
-        us = part(a, 48)
-        V("ts", n("ui# ua"), n("ua#"), T.ua[:, 48 * a + 1:48 * a + 48:3], T.ui[:, ws], 4095, None, A.bitwise_and)
-        V("ts", n("ui# ub"), n("ub#"), T.ub[:, 48 * a + 2:48 * a + 48:3], T.ui[:, ws], 4095, None, A.bitwise_and)
-        V("scan", n("ua# ub#"), n("sq#"), T.sq[:, us], T.ua[:, us], T.ub[:, us], 0.0, A.add, A.mult)
-        V("ts", n("sq#"), n("zz#"), zz, T.sq[:, 48 * a + 2:48 * a + 48:3], 5, W - 16, A.arith_shift_right,
-          A.bitwise_and)
-        V("ts", n("zz# pcol"), n("XL#"), xl, zz, pc, None, A.add)
+        pR = n("pR#")
+        xl, key = T["XL%d" % k][:, ws], key_of(k, a, 16)
+        V("ts", n("XL# pcol"), n("key#"), key, xl, pc, 1.0 / 16, A.subtract, A.mult)
         V("tt", n("FB XL# DIAG"), n("gm#0 gm#1"), T.gm[:, cs], Fwin.indirect(xl), T.DIAG[:], A.mult, c=ga(H))
         V("scan", n("RST gm#0 gm#1"), n("sc#"), T.sc[:, cs], T.RST[:], T.gm[:, cs], 0.0, A.mult, A.add, c=H)
-        V("ts", n("sc#"), n("PL#"), T.PL[:, ws], T.sc[:, H * a + 15:H * a + H:16], -OFF, None, A.add)
+        V("cp", n("sc#"), n("PL#"), T.PL[:, ws], T.sc[:, H * a + 15:H * a + H:16])
         ACT(T.ra[:, cs], Fwin.indirect(xl), AF.Copy, n("FB XL#"), n("ra#"), ga(H))
         for b in range(2):
             MM([(T.pW[:, :, 8 * b:8 * b + 8], blk(T.ra, 2 * a + b), T.permf[:], True, True, n("permf ra#"))], "pW", 512)
         ACT(T[n("WT#")][:], T.pW[:], AF.Copy, "pW", n("WT#"))
         ACT(T.dr[:, cs], Gwin.indirect(xl), AF.Copy, n("G XL#"), n("dr#"), ga(H))
         mark(n("dr#"))
-        V("cp", n("zz#"), n("key#"), key, zz)
         it = [(T.pU[:, 0:144], T.idn[:], T.zb[:], True, False, "idn zb")]
         for j in range(1, 8):
             it.append((T.pU[:, j:144:9], T.idn[:], key, False, False, n("idn key#")))
-            it.append((T.pU[:, 10 * j:144:9], T.idm[:], T.key[:, 16 * a:16 * a + 16 - j], False, j == 7, n("idm key#")))
+            it.append((T.pU[:, 10 * j:144:9], T.idm[:], key_of(k, a, 16 - j), False, j == 7, n("idm key#")))
         MM(it, "pU")
         ACT(T.AD[:, ns], T.pU[:, 0:144], AF.Abs, "pU", n("AD#"), 144, scale=256.0)
         MM([(T[pR][:, 0:144], T.idn[:], T.CK[:], True, False, "idn CK"),
@@ -384,7 +444,8 @@ def rank_program(g, core, T, topo):
         n = lambda s: s.replace("#", str(a))
         ws, cs = part(a, 16), part(a, H)
         hN, pDn, pPn = "hb%d%d" % (k, a), n("pD#"), n("pP#")
-        h, pD, pP, RB, pl = T[hN], T[pDn], T[pPn], T[n("RB#")], T.PL[:, ws]
+        h, pD, pP, RB, pl = T["hb%d" % k], T[pDn], T[pPn], T[n("RB#")], T.PL[:, ws]
+        hs = slice(h0_of(k, a), h0_of(k, a) + H)
         th, thN = (T.THg, n("THg#")) if hop else (T.THg0, "THgc")
         t0 = H * a if hop else 0
         if hop:
@@ -395,39 +456,38 @@ def rank_program(g, core, T, topo):
                 if hop == 3:
                     after(n("dr#"))
                 MM([(pP[:, 8 * b:8 * b + 8], blk(T.gm, 2 * a + b), T.g8f[:], True, True, n("g8f gm#%d" % b))], pPn, 256)
-            V("ts", pPn, n("PL#"), pl, pP[:, 0:16], -OFF, None, A.add)
+            V("cp", pPn, n("PL#"), pl, pP[:, 0:16])
             ACT(T.THg[:, cs], T.THW[:, 0:P].indirect(T.OL[:, ws]), AF.Copy, n("THW OL#"), thN, ga(H))
         if hop < 3:
-            MM([(pD[:, 0:32], T.idn[:], T.CX1[:, part(hop, 32)], True, False, "idn CX1"),
-                (pD[:, 0:32], T.idn[:], T.CX2[:], False, False, "idn CX2")]
-               + [(pD[:, part(b, 16)], blk(h, b), T.R2m[:], False, False, "R2m " + hN) for b in range(2)], pDn)
-            for c0 in range(0, 16, 4):
-                MM([(pD[:, 0:32:2], blk(T.S, c), th[:, t0 + c:t0 + H:16], False, False, "S " + thN)
-                    for c in range(c0, c0 + 4)], pDn)
-            V("tt", n("hdrS PL# ") + hN, n("D#"), T.D[:, cs], Hwin.indirect(pl), h[:], A.max, c=ga(H))
+            MM([(pD[:, 0:128], T.idn[:], T.CX1[:], True, False, "idn CX1"),
+                (pD[:, 0:128], T.idn[:], T.CX2[:], False, False, "idn CX2")]
+               + [(pD[:, part(b, 64)], blk(h, 2 * a + b), T.R2m[:], False, False, "R2m " + hN) for b in range(2)],
+               pDn, 96)
+            wrap(pD[:, 0:128:2], T.S, "S", th, t0, thN, pDn, False)
+            V("tt", n("hdrS PL# ") + hN, n("D#"), T.D[:, cs], Hwin.indirect(pl), h[:, hs], A.max, c=ga(H))
             ACT(RB[:, H:], Hwin.indirect(pl), AF.Copy, n("hdrS PL#"), n("Rn#"), ga(H))
-            MM([(pD[:, part(b, 16)], blk(RB, 2 + b), T.R2m[:], False, False, n("R2m Rn#")) for b in range(2)], pDn)
-            MM([(pD[:, part(b, 16)], blk(T.D, 2 * a + b), T.R2[:], False, b == 1, n("R2 D#")) for b in range(2)], pDn)
-            z0, z1 = (T["Z%d" % hop][:, part(a, 32)], n("Z%d#" % hop)) if hop else (T.Z0[:], "Z0"), T["Z%d" % (hop + 1)]
-            V("scan", pDn + " " + z0[1], n("Z%d#" % (hop + 1)), z1[:, part(a, 32)], z0[0], pD[:, 0:32], 0.0, A.max, A.min)
-            V("ts", n("Z%d#" % (hop + 1)), n("q#"), T.q[:, ws], z1[:, 32 * a + 1:32 * a + 32:2], 15 * 32 + 7, None,
-              A.bitwise_and)
-            V("cp", n("q#"), n("OL#"), T.OL[:, ws], T.q[:, ws])
+            MM([(pD[:, part(b, 64)], blk(RB, 2 + b), T.R2m[:], False, False, n("R2m Rn#")) for b in range(2)], pDn)
+            MM([(pD[:, part(b, 64)], blk(T.D, 2 * a + b), T.R2[:], False, b == 1, n("R2 D#")) for b in range(2)], pDn)
+            zs, last = part(a, 128), slice(128 * a + 7, 128 * a + 128, 8)
+            V("scan", n("pD# DY#") if hop else n("pD# DZ"), n("Z#"), T.Z[:, zs], T.DY[:, zs] if hop else T.DZ[:],
+              pD[:, 0:128], 0.0, A.max, A.min, c=128)
+            V("ts", n("Z# DY"), n("DY#"), T.DY[:, last], T.Z[:, last], 15 * 32 + 7, None, A.bitwise_and)
+            V("cp", n("DY#"), n("OL#"), T.OL[:, ws], T.DY[:, last])
             return
         MM([(pP[:, 32 + 16 * b:48 + 16 * b], blk(T.THg, 2 * a + b), T.R3[:], True, True, "R3 " + thN) for b in range(2)],
            pPn)
         V("ts", pPn, n("EL#"), T.EL[:, ws], pP[:, 33:64:2], -32.0, None, A.add)
-        ACT(T.thr[:, ws], pP[:, 32:64:2], AF.Copy, pPn, n("thr#"), 64)
-        MM([(pD[:, 0:16], T.idn[:], T.zb[:, 0:16], True, False, "idn zb")]
-           + [(pD[:, part(b, 8)], blk(T.THg, 2 * a + b), T.R3b[:, 0:8], False, False, "R3b " + thN) for b in range(2)],
-           pDn)
-        V("tt", n("hdrS PL# ") + hN, n("D#"), T.D[:, cs], Hwin.indirect(pl), h[:], A.subtract, c=ga(H))
+        ACT(T.thr[:, ws], pP[:, 32:64:2], AF.Copy, pPn, n("thr#"), 64, bias=256.0 * KS)
+        MM([(pD[:, 0:64], T.idn[:], T.CM[:], True, False, "idn CM")]
+           + [(pD[:, part(b, 32)], blk(T.THg, 2 * a + b), T.R3b[:, 0:32], False, False, "R3b " + thN)
+              for b in range(2)], pDn)
+        V("tt", n("hdrS PL# ") + hN, n("D#"), T.D[:, cs], Hwin.indirect(pl), h[:, hs], A.subtract, c=ga(H))
         ACT(RB[:, H:], T.D[:, cs], AF.Abs, n("D#"), n("Rn#"), H)
-        MM([(pD[:, 0:16], blk(T.S, c), RB[:, H + c::16], False, c == 15, n("S Rn#")) for c in range(16)], pDn)
-        V("ts", pDn, n("qm#"), T.qm[:, ws], pD[:, 0:16], 1.0 / KS, 192.0, A.mult, A.add)
-        ge, q2 = T.gl[:, 32 * a:32 * a + 32:2], T.q2[:, 32 * a + 1:32 * a + 32:2]
-        V("tt", n("pD# thr# gl"), n("ge#"), ge, pD[:, 0:16], T.thr[:, ws], A.is_ge)
-        V("ts", n("qm# q2"), n("q2#"), q2, T.qm[:, ws], 60, None, A.bitwise_and)
+        wrap(pD[:, 0:64], T.S, "S", RB, H, n("Rn#"), pDn, True)
+        V("scan", n("pD# DH"), n("qm#"), T.qm[:, part(a, 64)], T.DH[:], pD[:, 0:64], 0.0, A.max, A.min)
+        ge, q2, qm = T.gl[:, 32 * a:32 * a + 32:2], T.q2[:, 32 * a + 1:32 * a + 32:2], T.qm[:, 64 * a + 3:64 * a + 64:4]
+        V("ts", n("qm# q2"), n("q2#"), q2, qm, 60 * int(KS), None, A.bitwise_and)
+        V("tt", n("qm# thr# gl"), n("ge#"), ge, qm, T.thr[:, ws], A.is_ge)
         V("tt", n("q2# ge#"), n("nd#"), T.nd[:, ws], q2, ge, A.min)
         V("tt", n("dr# EL# DIAG"), n("tt#"), T.tt[:, cs], T.DIAG[:, 0:16].indirect(T.EL[:, ws]), T.dr[:, cs], A.mult,
           c=ga(H))
@@ -440,23 +500,32 @@ def rank_program(g, core, T, topo):
         V("scan", n("q2# ge#"), n("hl#"), T.hl[:, part(a, 32)], T.q2[:, part(a, 32)], T.gl[:, part(a, 32)], 0.0,
           A.min, A.add)
         V("ts", n("hl#"), n("HL#"), T.HL[:, ws], T.hl[:, 32 * a + 1:32 * a + 32:2], float(H), None, A.mult)
-        MM([(pX, T.idn[:], T[hN][:], True, False, "idn " + hN), (pX, T.idh[:], T.D[:, cs], False, True, n("idh D#"))],
-           pPn, H)
+        MM([(pX, T.idn[:], T["hb%d" % k][:, h0_of(k, a):h0_of(k, a) + H], True, False, "idn " + hN),
+            (pX, T.idh[:], T.D[:, cs], False, True, n("idh D#"))], pPn, H)
         ACT(T.y[:, cs], pX, AF.Identity, pPn, n("y#"), H, bias=BIG, scale=1.0 - 2.0 ** -11)
         ACT(RB[:, 0:H], T.y[:, cs], AF.Copy, n("y#"), n("B#"), H, bias=-BIG)
-        hn, nx, arr, loc = ["%s%d%d" % (s, j, a) for s, j in (("hn", k), ("hb", k + 1), ("arr", k), ("loc", k))]
-        ACT(T[hn][:], RB[:, 0:P].indirect(T.HL[:, ws]), AF.Copy, n("B# Rn# HL#"), hn, ga(H))
-        node("P", [((lambda: g.remote_dma(T[nx][:], T[hn][:], T.sem[arr], T.sem[loc], pid, rid, emask)), [hn])],
-             [hn], [nx], SEND, FLY, (arr, 0))
-        nodes[-1]["remote"] = [(arr, n_eng), (loc, n_eng)]
+        hn = "hn%d%d" % (k, a)
+        o, sent = h0_of(k + 1, a), [hn]
+        ACT(T["hn%d" % k][:, o:o + H], RB[:, 0:P].indirect(T.HL[:, ws]), AF.Copy, n("B# Rn# HL#"), hn, ga(H))
+        if k < STEPS - 1:
+            bank, ds = n("pD#"), part(a, 128)
+            pu = T[bank]
+            MM([(pu[:, 0:128], T.idn[:], T.CU[:], True, False, "idn CU")], bank, 128)
+            wrap(pu[:, 1:128:2], T.WN, "WN", RB, H, n("Rn#"), bank, False)
+            MM([(pu[:, 2 * i:128:8], T.idF[:], T.nd[:, ws], False, False, n("idF nd#")) for i in range(4)], bank)
+            wrap(pu[:, 0:128:2], T.WN, "WN", RB, 0, n("B#"), bank, True)
+            V("scan", n("pD# DU"), n("ui#"), T.ui[:, ds], T.DU[:], pu[:, 0:128], 0.0, A.max, A.min, c=128)
+            address(a, T.ui[:, 128 * a + 7:128 * a + 128:8], T["XO%d" % k][:, ws], hn + "x")
+            if a == 0:
+                send(T["XL%d" % (k + 1)][:], T["XO%d" % k][:], ["hn%d0x" % k, "hn%d1x" % k],
+                     "XL%d0 XL%d1" % (k + 1, k + 1), "x%d" % k, dst, FLY - 900)
+        os = slice(o, o + H)
+        send(T["hb%d" % (k + 1)][:, os], T["hn%d" % k][:, os], sent, "hb%d%d" % (k + 1, a), "h%d%d" % (k, a), dst, FLY)
         MM([(pR[:, 10 * j:144:9], T.idK[:], T.nd[:, 16 * a:16 * a + 16 - j], False, False, n("idK nd#"))
             for j in range(1, 8)] + [(pR[:, 8:144:9], T.idL[:], T.nd[:, ws], False, True, n("idL nd#"))], pRn)
         V("scan", "rst9 " + pRn, n("ls#"), T.ls[:, ns], T.rst9[:], pR[:, 0:144], 0.0, A.mult, A.max, c=144)
-        V("ts", n("ls# pcol"), n("SL#"), T.SL[:, ws], T.ls[:, 144 * a + 8:144 * a + 144:9], pc, None, A.add)
-        tab, col = "TB", "ra"
-        if k == STEPS - 1:
-            tab, col = "yoS", "rl"
-            ACT(T.rl[:, cs], T.ra[:, cs], AF.Copy, n("ra#"), n("rl#"), H, bias=-OFF)
+        V("ts", n("ls# pcol"), n("SL#"), T.SL[:, ws], T.ls[:, 144 * a + 8:144 * a + 144:9], 16.0, pc, A.mult, A.add)
+        tab, col = "TB" if k < STEPS - 1 else "yoS", "ra"
         for j in (2 * a + 1, 2 * a):
             sl = T.SL[:, part(j, 8)]
             V("tt", n("SL# tt# %s# %s" % (col, tab)), tab, T[tab][:, 0:W + 128].indirect(sl), blk(T.tt, j),
@@ -468,8 +537,7 @@ def rank_program(g, core, T, topo):
         if k == STEPS - 1:
             for hf in range(2):
                 cs = part(hf, 512)
-                ACT(T.AL[:, cs], T.TB[:, cs], AF.Abs, "TB", "AL%d" % hf)
-                ACT(T.yoS[:, cs], T.AL[:, cs], AF.Copy, "AL%d" % hf, "yoS", bias=-OFF)
+                ACT(T.yoS[:, cs], T.TB[:, cs], AF.Abs, "TB", "yoS")
         for a in (1, 0):
             start(k, a)
         for hop in range(4):
@@ -480,9 +548,8 @@ def rank_program(g, core, T, topo):
         if k < STEPS - 1:
             tables()
 
-    for hf in range(2):
-        dma(T.yo[:, part(hf, 512)], T.yoS[:, part(hf, 512)], "st_yo%d" % hf, ["yoS"], [], 4000)
-        dma(T.yh[:, part(hf, H)], T["hb%d%d" % (STEPS, hf)][:], "st_yh%d" % hf, ["hb%d%d" % (STEPS, hf)], [])
+    dma(T.yo[:], T.yoS[:, 0:W], "st_yo", ["yoS"], [], 4000)
+    dma(T.yh[:], T["hb%d" % STEPS][:, 0:P], "st_yh", ["hb%d0" % STEPS, "hb%d1" % STEPS], [], 2500)
     ACT(T.ymS[:], T.RW[:, 0:W], AF.Copy, "RW", "ymS", 1024, bias=1.0, scale=-1.0)
     dma(T.ym[:], T.ymS[0::16, :], "st_ym", ["ymS"], [])
     if not ORDER:

@@ -23,9 +23,9 @@ sb(F32, 128, "thF")
 sb(F32, W, "G ymS")
 sb(F32, W + 128, "TB RW yoS")
 sb(F32, W + 16, "FB")
-sb(BF, 512, "S WS WN")
-sb(BF, 64, "R2 R2m R3b")
-sb(BF, 128, "ones bones idn idh idm idK idL tmpa LT prm")
+sb(BF, 512, "S Sh WS WN Vb")
+sb(BF, 32, "R2 R2m R3b")
+sb(BF, 128, "ones bones idn idh idm idK idL LT prm")
 sb(F32, 128, "permf zero idf idg")
 sb(BF, 16, "wS wN R3")
 sb(F32, 8, "g8f one")
@@ -36,9 +36,10 @@ sb(F32, 144, "rst9")
 sb(BF, 144, "zb CKa CK")
 sb(F32, 288, "ls")
 sb(BF, 288, "AD")
-sb(I32, 128, "DZ")
-sb(I32, 256, "DY Z")
-sb(BF, 128, "CX1 CX2 CU idF")
+sb(I32, 64, "DZ")
+sb(I32, 128, "DY Z")
+sb(BF, 64, "CX1 CX2")
+sb(BF, 128, "CU idF")
 sb(BF, 64, "CM CF")
 sb(F32, 64, "DH im")
 sb(F32, 128, "DU")
@@ -49,13 +50,15 @@ sb(F32, P, "pU pD0 pD1 pP0 pP1 pR0 pR1 gm sc ra WT0 WT1 dr tt y")
 SCRATCH["pW"] = ("psum", [128, 16, 32], F32)
 sb(BF, P, "D THW THg RB0 RB1")
 sb(BF, H, "THg0")
+sb(BF, P, "CQ")
+sb(BF, 1024, "S8")
 for k in range(STEPS):
     sb(BF, P, "hb%d hn%d" % (k + 1, k))
 sb(I32, 32, "zz")
 sb(I32, 64, "q2")
 sb(I32, 128, "qm")
 sb(I32, 256, "ui")
-sb(I32, 72, "uq0 uq1")
+sb(I32, 136, "uq")
 sb(I32, 128, "sq")
 sb(BF, 32, "key nd")
 sb(U16, 32, "XL0 XL1 XL2 XO0 XO1 PL OL OL0 SL HL EL")
@@ -66,10 +69,11 @@ SEMAPHORES = ["V", "A", "T", "P"] + ["ld_" + n for n in LOADS] \
     + ["arrw", "locw", "st_yo", "st_ym", "st_yh"]
 KS, HUGE = 2.0 ** 18, 3 * 2.0 ** 29
 FAR = 2.0 ** 32
-BIG = 8388608.0
-CYC, PE, GATHER, SCATTER, WAKE, DMA, SEND, FLY = 0.87, 0.44, 1.4, 3.4, 200, 2000, 1200, 2400
-ROUNDS, SLACK = 20000, 15.0
+BIG = 12582912.0
+CYC, PE, GATHER, SCATTER, WAKE, DMA, SEND, FLY = 0.87, 0.44, 1.4, 3.4, 200, 2000, 1000, 2400
+ROUNDS, SLACK, TWIN = 55000, 40.0, 0.5
 ORDER = []
+MIX = 1.0
 
 
 def rank_program(g, core, T, topo):
@@ -78,18 +82,18 @@ def rank_program(g, core, T, topo):
         return
     A, AF = AluOpType, ActivationFunctionType
     queues = {"V": g.vector, "A": g.scalar, "T": g.tensor, "P": g, "Y": g.sync}
-    nodes, marks, soft = [], {}, {}
+    nodes, marks, soft, place_in = [], {}, {}, ["setup", 0]
 
     def node(q, emit, reads, writes, cost, lat=0.0, sem=None, early=0.0):
         nodes.append({"q": q, "emit": emit, "r": reads, "w": writes, "cost": cost, "lat": lat, "sem": sem or (q, 1),
-                      "early": early})
+                      "early": early, "tag": tuple(place_in)})
+        place_in[1] += 1
 
     def mark(name):
         marks[name] = len(nodes) - 1
 
     def after(*names):
-        for name in names:
-            soft.setdefault(marks[name], []).append(len(nodes) - 1)
+        soft.setdefault(len(nodes) - 1, []).extend(marks[name] for name in names)
 
     def op(q, fn, reads, writes, cost):
         node(q, [(fn, reads)], reads, writes, cost)
@@ -135,6 +139,9 @@ def rank_program(g, core, T, topo):
             ps.pop(i, None)
             for p, gap in ps.items():
                 preds[i][p] = succ[p][i] = gap + nodes[p]["lat"]
+            for p in soft.get(i, []):
+                preds[i].setdefault(p, 0.0)
+                succ[p].setdefault(i, 0.0)
             if d["early"] and i:
                 preds[i][i - 1] = succ[i - 1][i] = 0.0
             for r in d["r"]:
@@ -146,28 +153,49 @@ def rank_program(g, core, T, topo):
         def place(order, keep, end, ready):
             end, ready, busy = list(end), list(ready), {q: [] for q in queues}
             for i in order[:keep]:
-                busy[nodes[i]["q"]].append((end[i] - nodes[i]["cost"], end[i], i))
+                busy[queue[i]].append((end[i] - costs[i], end[i], i))
             for line in busy.values():
                 line.append((1e18, 1e18, -1))
             for i in order[keep:]:
-                cost, line = nodes[i]["cost"], busy[nodes[i]["q"]]
-                t = ready[i] = max([end[p] + gap for p, gap in preds[i].items()] + [0.0])
+                cost, line, t = costs[i], busy[queue[i]], 0.0
+                for p, gap in needs[i]:
+                    if end[p] + gap > t:
+                        t = end[p] + gap
+                ready[i] = t
                 at = len(line) - 1
                 while at and line[at - 1][1] > t:
                     at -= 1
                 while t + cost > line[at][0]:
-                    t = max(t, line[at][1])
+                    if line[at][1] > t:
+                        t = line[at][1]
                     at += 1
                 line.insert(at, (t, t + cost, i))
                 end[i] = t + cost
-            ahead = {line[a][2]: line[a - 1][2] for line in busy.values() for a in range(1, len(line))}
-            return end, ready, ahead
+            return end, ready, busy
 
-        rnd = numpy.random.RandomState(0)
+        costs, queue = [d["cost"] for d in nodes], [d["q"] for d in nodes]
+        needs, last = [list(p.items()) for p in preds], [i for i in range(n) if not succ[i]]
+
+        more = {round(ga(m) * CYC): 1.35 for m in (128, H)}
+        more.update({round((m + 128 * SCATTER) * CYC): 1.5 for m in (60, 70)})
+        slow = [c * (1.3 * more.get(round(c), 1.0) if q in "VAT" else 1.0) for c, q in zip(costs, queue)]
+
+        def replay(order):
+            end, free = [0.0] * n, {q: 0.0 for q in queues}
+            for i in order:
+                t = free[queue[i]]
+                for p, gap in needs[i]:
+                    if end[p] + gap > t:
+                        t = end[p] + gap
+                end[i] = free[queue[i]] = t + slow[i]
+            return max(end[j] + nodes[j]["lat"] for j in last)
+
+        rnd, twins = numpy.random.RandomState(0), {}
+        for i, d in enumerate(nodes):
+            twins.setdefault(d["tag"], []).append(i)
         rest = [0.0] * n
         for i in range(n - 1, -1, -1):
-            rest[i] = nodes[i]["cost"] + max([rest[s] + gap for s, gap in succ[i].items()]
-                                             + [rest[s] for s in soft.get(i, [])] + [nodes[i]["lat"]])
+            rest[i] = nodes[i]["cost"] + max([rest[s] + gap for s, gap in succ[i].items()] + [nodes[i]["lat"]])
         order = sorted(range(n), key=lambda i: (-rest[i] - nodes[i]["early"], i))
         best, now, chain, lo, times = None, None, [], 0, ([0.0] * n, [0.0] * n)
         for r in range(ROUNDS):
@@ -175,21 +203,28 @@ def rank_program(g, core, T, topo):
             if chain:
                 i, back = chain[rnd.randint(len(chain))], rnd.rand() < 0.5
                 i = rnd.randint(n) if rnd.rand() > 0.7 else before.get(i, i) if back else i
-                pos, far = {v: j for j, v in enumerate(order)}, (2, 5, 10, 25, 60)[rnd.randint(5)]
-                lo, hi = (pos[i], pos[i] + far) if back else (max(0, pos[i] - far), pos[i])
-                need, todo = {i}, [i]
-                while todo:
-                    more = [p for p in (succ if back else preds)[todo.pop()] if lo <= pos[p] <= hi and p not in need]
-                    need.update(more)
-                    todo += more
-                new = order[:lo] + sorted(order[lo:hi + 1], key=lambda v: (v in need) == back) + order[hi + 1:]
-            end, ready, ahead = place(new, lo, *times)
-            i = max(range(n), key=lambda j: end[j] + nodes[j]["lat"])
-            span = end[i] + nodes[i]["lat"]
-            if now is not None and span > now + SLACK * (1.0 - r / ROUNDS) * rnd.exponential():
+                far = (2, 5, 10, 25, 60)[rnd.randint(5)]
+                for i in reversed(twins[nodes[i]["tag"]] if rnd.rand() < TWIN else [i]):
+                    lo, hi = (pos[i], pos[i] + far) if back else (max(0, pos[i] - far), pos[i])
+                    need, todo = {i}, [i]
+                    while todo:
+                        more = [p for p in (succ if back else preds)[todo.pop()] if lo <= pos[p] <= hi and p not in need]
+                        need.update(more)
+                        todo += more
+                    new = new[:lo] + sorted(new[lo:hi + 1], key=lambda v: (v in need) == back) + new[hi + 1:]
+            end, ready, busy = place(new, lo, *times)
+            i = max(last, key=lambda j: end[j] + nodes[j]["lat"])
+            span, bar = end[i] + nodes[i]["lat"], SLACK * (1.0 - r / ROUNDS) * rnd.exponential()
+            if now is not None and span > fast + bar + 300.0:
                 continue
-            now, order, chain = span, sorted(range(n), key=lambda j: (end[j] - nodes[j]["cost"], j)), [i]
-            before, times = ahead, (end, ready)
+            new = sorted(range(n), key=lambda j: (end[j] - costs[j], j))
+            both = span + MIX * replay(new)
+            if now is not None and both > now + bar:
+                continue
+            fast, span = span, both
+            now, order, chain = span, new, [i]
+            ahead = {line[a][2]: line[a - 1][2] for line in busy.values() for a in range(1, len(line))}
+            before, times, pos = ahead, (end, ready), {v: j for j, v in enumerate(order)}
             if best is None or span < best[0]:
                 best = (span, order)
             while end[i] - nodes[i]["cost"] - ready[i] > 1.0 or preds[i]:
@@ -257,11 +292,11 @@ def rank_program(g, core, T, topo):
 
     c1 = slice(0, 1)
     dma(T.mkS[0:32, :], T.marks[:], "ld_marks", [], ["mkS"], early=9e6)
-    dma(T.owS[:], T.owner[:], "ld_owner", [], ["owS"], 4000, early=8e6)
-    dma(T.wR[0:1, :], T.w[:], "ld_w", [], ["wR"], 4200, early=7e6)
-    dma(T.thR[0:1, :], T.th[:], "ld_th", [], ["thR"], 4200, early=6e6)
-    dma(T.hb0[:], T.h0[:], "ld_h0", [], ["hb00", "hb01"], 4700, early=5e6)
-    dma(T.hdrS[:], T.hdr[:], "ld_hdr", [], ["hdrS"], 7000, early=1.0)
+    dma(T.wR[0:1, :], T.w[:], "ld_w", [], ["wR"], 2000, early=8e6)
+    dma(T.thR[0:1, :], T.th[:], "ld_th", [], ["thR"], 2000, early=7e6)
+    dma(T.hb0[:], T.h0[:], "ld_h0", [], ["hb00", "hb01"], 2200, early=6e6)
+    dma(T.owS[:], T.owner[:], "ld_owner", [], ["owS"], 3400, early=5e6)
+    dma(T.hdrS[:], T.hdr[:], "ld_hdr", [], ["hdrS"], 6000, early=1.0)
 
     def iota(buf, name, pattern, base, cm, c):
         op("P", lambda: g.iota(buf, pattern, base, cm, allow_small_or_imprecise_dtypes=True), [], [name], 140 + 2 * c)
@@ -272,17 +307,18 @@ def rank_program(g, core, T, topo):
     pc = T.pcol[:, c1]
     V("ms", "", "ones", T.ones[:], 1.0)
     op("P", lambda: g.iota(T.pi[:, c1], [[0, 1]], 0, 1), [], ["pi"], 140)
-    sel(T.tmpa[:], T.ones[:], [[-16, 8], [0, 16]], A.is_ge, 0, 1, "ones", "tmpa", 128)
-    sel(T.bones[:], T.tmpa[:], [[16, 8], [0, 16]], A.is_ge, 15, -1, "tmpa", "bones", 128)
+    sel(T.bones[:], T.ones[:], [[-16, 8], [0, 16]], A.is_ge, 0, 1, "ones", "bones", 128)
+    sel(T.bones[:], T.bones[:], [[16, 8], [0, 16]], A.is_ge, 15, -1, "bones", "bones", 128)
     sel(T.idn[:], T.ones[:], [[-1, 128]], A.is_equal, 0, 1, "ones", "idn", 128)
     iota(T.jmod[:], "jmod", [[0, 16], [1, 16]], 0, 0, 256)
     iota(T.base[:], "base", [[16, 16]], 0, 0, 16)
     sel(T.prm[:], T.ones[:], [[-1, 16], [-16, 8]], A.is_equal, 0, 1, "ones", "perm", 128)
     iota(T.gcol[:], "gcol", [[0, 2], [1, 8]], 0, 0, 16)
     iota(T.im[:], "im", [[0, 16], [1, 4]], 0, 0, 64)
-    iota(T.rst9[:], "rst9i", [[0, 16], [1, 9]], 0, 0, 144)
     ACT(T.zero[:], T.ones[:], AF.Silu, "ones", "zero", 1400, scale=0.0)
     V("ms", "", "zb", T.zb[:], 0.0)
+    V("ms", "", "CQ", T.CQ[:, 0:H], -0.25, c=128)
+    V("ms", "", "CQ", T.CQ[:, H:], 0.0, c=128)
     iota(T.CKa[:], "CKa", [[0, 2], [1, 8], [0, 9]], -64, 0, 144)
     sel(T.CK[:], T.CKa[:], [[0, 2], [1, 8], [-1, 9]], A.is_ge, 0, 0, "CKa", "CK", 144, -256.0)
     V("ms", "", "CK", T.CK[:, 0::9], 0.0)
@@ -301,19 +337,25 @@ def rank_program(g, core, T, topo):
     V("ms", "", "S", T.S[:], 0.0, c=256)
     for r in range(4):
         ACT(T.S[:, 129 * r:128 * (r + 1):4], T.bones[:, r::4], AF.Copy, "bones", "S", 64, scale=KS)
+    V("ts", "S", "Sh", T.Sh[:], T.S[:], -0.5, None, A.mult, c=256)
     V("ts", "S pP0", "WS", T.WS[:], T.S[:], T.pP0[:, 0:1], 1.0 / KS, A.mult, A.mult, c=256)
     c2 = slice(1, 2)
     V("ts", "ci", "ci2", T.ci[:, c2], T.ci[:, c1], 2, None, A.arith_shift_right)
     V("cp", "ci2", "pq", T.pcol[:, c2], T.ci[:, c2])
     V("ts", "im pq", "CF", T.CF[:], T.im[:], T.pcol[:, c2], FAR, A.not_equal, A.mult)
-    V("ts", "CF", "CM", T.CM[:], T.CF[:], 256.0 * KS, None, A.add)
+    V("ts", "CF", "CM", T.CM[:], T.CF[:], 128.0 * KS, None, A.add)
     V("cp", "CF", "CU", T.CU[:, 0::2], T.CF[:])
     V("ts", "CF", "CU", T.CU[:, 1::2], T.CF[:], 2.0 ** 21, None, A.add)
-    V("cp", "CF", "CX1", T.CX1[:, 0::2], T.CF[:])
-    V("ms", "", "CX1", T.CX1[:, 1::2], FAR)
-    V("ms", "CX1", "CX1", T.CX1[:, 7::8], 512.0)
+    V("ms", "", "S8", T.S8[:], 0.0, c=512)
+    for r in range(8):
+        ACT(T.S8[:, 129 * r:128 * (r + 1):8], T.bones[:, r::8], AF.Copy, "bones", "S8", 64, scale=KS)
+    V("ts", "base pcol", "thr0", T.thr[:, 0:16], T.base[:], 0.0, pc, A.mult, A.add)
+    V("ts", "thr0", "CX1", T.CX1[:, 0::4], T.thr[:, 0:16], 8.0, FAR, A.is_ge, A.mult)
+    V("ts", "thr0", "CX1", T.CX1[:, 2::4], T.thr[:, 0:16], 8.0, FAR, A.is_lt, A.mult)
+    V("ms", "", "CX1", T.CX1[:, 1::4], FAR)
+    V("ms", "", "CX1", T.CX1[:, 3::4], 512.0)
     V("ms", "", "CX2", T.CX2[:], 0.0)
-    for n, step, kind in (("DZ", 8, int), ("DY", 8, int), ("DU", 8, float), ("DH", 4, float)):
+    for n, step, kind in (("DZ", 4, int), ("DY", 4, int), ("DU", 8, float), ("DH", 4, float)):
         V("ms", "", n, T[n][:], kind(-HUGE), c=128)
         V("ms", n, n, T[n][:, 0::step], kind(HUGE))
     V("ts", "mkS", "mkB", T.mkB[0:32, :], T.mkS[0:32, :], 2.0, -1.0, A.mult, A.add, c=256)
@@ -321,10 +363,11 @@ def rank_program(g, core, T, topo):
         cs, bank = part(hf, 512), "pR%d" % hf
         MM([(T[bank][:, part(c, 256)], T.U[0:32, part(2 * hf + c, 128)], T.mkB[0:32, :], True, True, "U mkB")
             for c in range(2)], bank, 256)
-        V("tt", "owS " + bank, "TB", T.TB[:, cs], T.owS[:, cs], T[bank][:], A.mult, c=512)
         ACT(T.RW[:, cs], T[bank][:], AF.Copy, bank, "RW", bias=0.5, scale=-0.5)
+        V("tt", "owS " + bank, "TB", T.TB[:, cs], T.owS[:, cs], T[bank][:], A.mult, c=512)
 
     def tables():
+        place_in[:] = ["tables", 0]
         V("scan", "RW TB", "FB", T.FB[:, 8:8 + W], T.RW[:, 0:W], T.TB[:, 0:W], 0.0, A.mult, A.max, c=1024)
         mark("FB")
         V("cp", "FB", "FBw", T.FB[:, 7:8], T.FB[:, 7 + W:8 + W])
@@ -336,27 +379,30 @@ def rank_program(g, core, T, topo):
             cs, bank = part(a, 256), "pR%d" % (a // 2)
             V("scan", "RW " + bank + (" G" if a else ""), "G", T.G[:, cs], T.RW[:, cs], T[bank][:, part(a % 2, 256)],
               T.G[:, 256 * a - 1:256 * a] if a else 0.0, A.mult, A.add, c=256)
+        mark("G")
 
-    V("ts", "jmod", "RST", T.RST[:], T.jmod[:], 0.0, None, A.not_equal, c=256)
+    V("ms", "", "RST", T.RST[:], 1.0, c=256)
+    V("ms", "RST", "RST", T.RST[:, 0::16], 0.0)
     V("ms", "", "q2", T.q2[:], 0)
+    for j, v in enumerate((0, 1, 0, 32)):
+        V("ms", "", "uq", T.uq[:, j::4], v)
     for a in range(2):
-        for j, v in enumerate((0, 1, 0, 32)):
-            V("ms", "", "uq%d" % a, T["uq%d" % a][:, j::4], v)
         V("ts", "base pcol", "gl", T.gl[:, 32 * a + 1:32 * a + 32:2], T.base[:], pc, 1.0 / H, A.add, A.mult)
-    V("ts", "rst9i", "rst9", T.rst9[:], T.rst9[:], 0.0, None, A.not_equal, c=144)
+    V("ms", "", "rst9", T.rst9[:], 1.0, c=144)
+    V("ms", "rst9", "rst9", T.rst9[:, 0::9], 0.0)
     V("ts", "pcol", "c32", T.c32[:, c1], pc, 32.0, None, A.mult)
     V("ts", "gcol c32", "OL0", T.OL0[:, 0:16], T.gcol[:], T.c32[:, c1], None, A.add)
-    V("cp", "OL0 DZ", "DZ", T.DZ[:, 7::8], T.OL0[:, 0:16])
-    V("cp", "gcol CX2", "CX2", T.CX2[:, 7::8], T.gcol[:])
+    V("cp", "OL0 DZ", "DZ", T.DZ[:, 3::4], T.OL0[:, 0:16])
+    V("cp", "gcol CX2", "CX2", T.CX2[:, 3::4], T.gcol[:])
     for n, f in (("idf", 1.0), ("idg", -1.0), ("idh", 0.5), ("idm", -1.0), ("idK", 128.0), ("idL", -128.0),
                  ("idF", FAR)):
         ACT(T[n][:], T.idn[:], AF.Copy, "idn", n, 128, scale=f)
     ACT(T.permf[:], T.prm[:], AF.Copy, "perm", "permf", 128)
     ACT(T.g8f[:], g8, AF.Copy, "bones", "g8f", 64)
     for n, f in (("R2", 2.0), ("R2m", -1.0)):
-        ACT(T[n][:, 0::2], T.bones[:, 0::4], AF.Copy, "bones", n, 64, scale=f * KS)
-        ACT(T[n][:, 1::2], T.bones[:, 0::4], AF.Copy, "bones", n, 64, scale=0.0)
-        ACT(T[n][:, 7::8], g8, AF.Copy, "bones " + n, n, 64, scale=f * 8.0)
+        ACT(T[n][:, 0::2], T.bones[:, 0::8], AF.Copy, "bones", n, 64, scale=f * KS)
+        ACT(T[n][:, 1::4], g8, AF.Copy, "bones", n, 64, scale=0.0)
+        ACT(T[n][:, 3::4], g8, AF.Copy, "bones", n, 64, scale=f * 8.0)
     V("ts", "thS", "ta", T.ta[:, c1], T.thS[:, c1], 8192 - 64, None, A.bitwise_and)
     V("ts", "thS", "tb", T.ta[:, c2], T.thS[:, c1], 63, None, A.bitwise_and)
     V("ts", "ta tb", "taf", T.taf[:, 0:2], T.ta[:, 0:2], -1.0, None, A.mult)
@@ -372,9 +418,10 @@ def rank_program(g, core, T, topo):
     V("tt", "wb wd", "wa", T.wa[:, c1], T.wb[:, c1], T.wd[:, c1], A.add)
     ACT(T.R3[:, 0::2], g8, AF.Identity, "bones wa", "R3", 64, scale=T.wa[:, c1])
     ACT(T.R3[:, 1::2], g8, AF.Identity, "bones wc", "R3", 64, scale=T.wc[:, c1])
-    ACT(T.R3b[:, 0:32], T.bones[:, 0::4], AF.Identity, "bones wb", "R3b", 64, scale=T.wb[:, c1])
+    V("ts", "bones wb", "R3b", T.R3b[:, 0:32], T.bones[:, 0::4], T.wb[:, c1], 0.5, A.mult, A.mult)
     ACT(T.THg0[:], T.THW[:, 0:P].indirect(T.OL0[:, 0:16]), AF.Copy, "THW OL0", "THgc", ga(H))
     tables()
+    place_in[:] = ["setup", len(nodes)]
 
     dst = T.cores[(rank + SHIFT) % N]
     Fwin, Gwin, Hwin = T.FB[:, 8:8 + W], T.G[:, 0:W], T.hdrS[:, 0:R]
@@ -390,14 +437,12 @@ def rank_program(g, core, T, topo):
         MM([(out, blk(mat, r), src[:, first + r:first + H:4], False, stop and r == 3, mN + " " + sN) for r in range(4)],
            bank)
 
-    def address(a, ui, out, oN):
-        n = lambda s: s.replace("#", str(a))
-        uq = T[n("uq#")]
-        V("ts", n("ui# uq#"), n("uq#"), uq[:, 2:64:4], ui, 4095, None, A.bitwise_and)
-        V("scan", n("uq#"), n("sq#"), T.sq[:, part(a, 64)], uq[:, 0:64], uq[:, 2:66], 0.0, A.mult, A.add)
-        V("ts", n("sq#"), n("zz#"), T.zz[:, part(a, 16)], T.sq[:, 64 * a + 2:64 * a + 64:4], 9, 63,
-          A.arith_shift_right, A.bitwise_and)
-        V("ts", n("zz# pcol"), oN, out, T.zz[:, part(a, 16)], 16.0, pc, A.mult, A.add)
+    def address(ui, out, oN):
+        uq = T.uq
+        V("ts", "ui0 ui1 uq", "uq", uq[:, 2:128:4], ui, 4095, None, A.bitwise_and)
+        V("scan", "uq", "sq", T.sq[:], uq[:, 0:128], uq[:, 2:130], 0.0, A.mult, A.add, c=128)
+        V("ts", "sq", "zz", T.zz[:], T.sq[:, 2::4], 9, 63, A.arith_shift_right, A.bitwise_and)
+        V("ts", "zz pcol", oN, out, T.zz[:], 16.0, pc, A.mult, A.add)
 
     def h0_of(k, a):
         return H * a
@@ -412,15 +457,17 @@ def rank_program(g, core, T, topo):
         pD = "pD%d" % a
         MM([(T[pD][:, 0:64], T.idn[:], T.CF[:], True, False, "idn CF")], pD)
         wrap(T[pD][:, 0:64], T.WS, "WS", T.hb0, H * a, "hb0%d" % a, pD, True)
-        V("scan", pD + " DH", "ui%d" % a, T.ui[:, 128 * a:128 * a + 64], T.DH[:], T[pD][:, 0:64], 0.0, A.max, A.min)
-        address(a, T.ui[:, 128 * a + 3:128 * a + 64:4], T.XL0[:, part(a, 16)], "XL0%d" % a)
+        V("scan", pD + " DH", "ui%d" % a, T.ui[:, part(a, 64)], T.DH[:], T[pD][:, 0:64], 0.0, A.max, A.min)
+    address(T.ui[:, 3:128:4], T.XL0[:], "XL00 XL01")
 
     def start(k, a):
+        place_in[:] = ["start%d" % a, 0]
         n = lambda s: s.replace("XL", "XL%d" % k).replace("#", str(a))
         ws, cs, ns = part(a, 16), part(a, H), part(a, 144)
         pR = n("pR#")
         xl, key = T["XL%d" % k][:, ws], key_of(k, a, 16)
-        V("ts", n("XL# pcol"), n("key#"), key, xl, pc, 1.0 / 16, A.subtract, A.mult)
+        if a:
+            V("ts", n("XL0 XL1 pcol"), "key0 key1", T.key[:], T["XL%d" % k][:], pc, 1.0 / 16, A.subtract, A.mult)
         V("tt", n("FB XL# DIAG"), n("gm#0 gm#1"), T.gm[:, cs], Fwin.indirect(xl), T.DIAG[:], A.mult, c=ga(H))
         V("scan", n("RST gm#0 gm#1"), n("sc#"), T.sc[:, cs], T.RST[:], T.gm[:, cs], 0.0, A.mult, A.add, c=H)
         V("cp", n("sc#"), n("PL#"), T.PL[:, ws], T.sc[:, H * a + 15:H * a + H:16])
@@ -441,6 +488,7 @@ def rank_program(g, core, T, topo):
             (T[pR][:, 0:144:9], T.idn[:], key, False, False, n("idn key#"))], pR, 120)
 
     def hop_of(k, a, hop):
+        place_in[:] = ["hop%d%d" % (a, hop), 0]
         n = lambda s: s.replace("#", str(a))
         ws, cs = part(a, 16), part(a, H)
         hN, pDn, pPn = "hb%d%d" % (k, a), n("pD#"), n("pP#")
@@ -454,45 +502,51 @@ def rank_program(g, core, T, topo):
                   T[n("WT#")][:, 8 * b:P].indirect(T.OL[:, 16 * a + 8 * b:16 * a + 8 * b + 8]), T.DIAG[:, 0:128], A.mult,
                   c=ga(128))
                 if hop == 3:
-                    after(n("dr#"))
+                    after("G")
                 MM([(pP[:, 8 * b:8 * b + 8], blk(T.gm, 2 * a + b), T.g8f[:], True, True, n("g8f gm#%d" % b))], pPn, 256)
             V("cp", pPn, n("PL#"), pl, pP[:, 0:16])
             ACT(T.THg[:, cs], T.THW[:, 0:P].indirect(T.OL[:, ws]), AF.Copy, n("THW OL#"), thN, ga(H))
+            if hop == 3:
+                after("dr0", "dr1")
         if hop < 3:
-            MM([(pD[:, 0:128], T.idn[:], T.CX1[:], True, False, "idn CX1"),
-                (pD[:, 0:128], T.idn[:], T.CX2[:], False, False, "idn CX2")]
-               + [(pD[:, part(b, 64)], blk(h, 2 * a + b), T.R2m[:], False, False, "R2m " + hN) for b in range(2)],
-               pDn, 96)
-            wrap(pD[:, 0:128:2], T.S, "S", th, t0, thN, pDn, False)
+            MM([(pD[:, 0:64], T.idn[:], T.CX1[:], True, False, "idn CX1"),
+                (pD[:, 0:64], T.idn[:], T.CX2[:], False, False, "idn CX2")]
+               + [(pD[:, part(b, 32)], blk(h, 2 * a + b), T.R2m[:], False, False, "R2m " + hN) for b in range(2)], pDn)
+            for r0 in (0, 4):
+                MM([(pD[:, 0:64:2], blk(T.S8, r), th[:, t0 + r:t0 + H:8], False, False, "S8 " + thN)
+                    for r in range(r0, r0 + 4)], pDn)
             V("tt", n("hdrS PL# ") + hN, n("D#"), T.D[:, cs], Hwin.indirect(pl), h[:, hs], A.max, c=ga(H))
             ACT(RB[:, H:], Hwin.indirect(pl), AF.Copy, n("hdrS PL#"), n("Rn#"), ga(H))
-            MM([(pD[:, part(b, 64)], blk(RB, 2 + b), T.R2m[:], False, False, n("R2m Rn#")) for b in range(2)], pDn)
-            MM([(pD[:, part(b, 64)], blk(T.D, 2 * a + b), T.R2[:], False, b == 1, n("R2 D#")) for b in range(2)], pDn)
-            zs, last = part(a, 128), slice(128 * a + 7, 128 * a + 128, 8)
+            MM([(pD[:, part(b, 32)], blk(RB, 2 + b), T.R2m[:], False, False, n("R2m Rn#")) for b in range(2)], pDn)
+            MM([(pD[:, part(b, 32)], blk(T.D, 2 * a + b), T.R2[:], False, b == 1, n("R2 D#")) for b in range(2)], pDn)
+            zs, last = part(a, 64), slice(64 * a + 3, 64 * a + 64, 4)
             V("scan", n("pD# DY#") if hop else n("pD# DZ"), n("Z#"), T.Z[:, zs], T.DY[:, zs] if hop else T.DZ[:],
-              pD[:, 0:128], 0.0, A.max, A.min, c=128)
+              pD[:, 0:64], 0.0, A.max, A.min)
             V("ts", n("Z# DY"), n("DY#"), T.DY[:, last], T.Z[:, last], 15 * 32 + 7, None, A.bitwise_and)
             V("cp", n("DY#"), n("OL#"), T.OL[:, ws], T.DY[:, last])
             return
         MM([(pP[:, 32 + 16 * b:48 + 16 * b], blk(T.THg, 2 * a + b), T.R3[:], True, True, "R3 " + thN) for b in range(2)],
            pPn)
         V("ts", pPn, n("EL#"), T.EL[:, ws], pP[:, 33:64:2], -32.0, None, A.add)
-        ACT(T.thr[:, ws], pP[:, 32:64:2], AF.Copy, pPn, n("thr#"), 64, bias=256.0 * KS)
+        ACT(T.thr[:, ws], pP[:, 32:64:2], AF.Copy, pPn, n("thr#"), 64, bias=128.0 * KS, scale=0.5)
         MM([(pD[:, 0:64], T.idn[:], T.CM[:], True, False, "idn CM")]
            + [(pD[:, part(b, 32)], blk(T.THg, 2 * a + b), T.R3b[:, 0:32], False, False, "R3b " + thN)
               for b in range(2)], pDn)
-        V("tt", n("hdrS PL# ") + hN, n("D#"), T.D[:, cs], Hwin.indirect(pl), h[:, hs], A.subtract, c=ga(H))
-        ACT(RB[:, H:], T.D[:, cs], AF.Abs, n("D#"), n("Rn#"), H)
-        wrap(pD[:, 0:64], T.S, "S", RB, H, n("Rn#"), pDn, True)
+        wrap(pD[:, 0:64], T.Sh, "Sh", h, H * a, hN, pDn, False)
+        V("tt", n("hdrS PL# ") + hN, n("D#"), T.D[:, cs], Hwin.indirect(pl), h[:, hs], A.max, c=ga(H))
+        ACT(T.Vb[:, cs], Hwin.indirect(pl), AF.Copy, n("hdrS PL#"), n("Vb#"), ga(H))
+        wrap(pD[:, 0:64], T.Sh, "Sh", T.Vb, H * a, n("Vb#"), pDn, False)
+        wrap(pD[:, 0:64], T.S, "S", T.D, H * a, n("D#"), pDn, True)
         V("scan", n("pD# DH"), n("qm#"), T.qm[:, part(a, 64)], T.DH[:], pD[:, 0:64], 0.0, A.max, A.min)
         ge, q2, qm = T.gl[:, 32 * a:32 * a + 32:2], T.q2[:, 32 * a + 1:32 * a + 32:2], T.qm[:, 64 * a + 3:64 * a + 64:4]
-        V("ts", n("qm# q2"), n("q2#"), q2, qm, 60 * int(KS), None, A.bitwise_and)
+        V("ts", n("qm# q2"), n("q2#"), q2, qm, 30 * int(KS), None, A.bitwise_and)
         V("tt", n("qm# thr# gl"), n("ge#"), ge, qm, T.thr[:, ws], A.is_ge)
         V("tt", n("q2# ge#"), n("nd#"), T.nd[:, ws], q2, ge, A.min)
         V("tt", n("dr# EL# DIAG"), n("tt#"), T.tt[:, cs], T.DIAG[:, 0:16].indirect(T.EL[:, ws]), T.dr[:, cs], A.mult,
           c=ga(H))
 
     def finish(k, a):
+        place_in[:] = ["finish%d" % a, 0]
         n = lambda s: s.replace("#", str(a))
         ws, cs, ns = part(a, 16), part(a, H), part(a, 144)
         hN, pPn, pRn = "hb%d%d" % (k, a), n("pP#"), n("pR#")
@@ -500,10 +554,15 @@ def rank_program(g, core, T, topo):
         V("scan", n("q2# ge#"), n("hl#"), T.hl[:, part(a, 32)], T.q2[:, part(a, 32)], T.gl[:, part(a, 32)], 0.0,
           A.min, A.add)
         V("ts", n("hl#"), n("HL#"), T.HL[:, ws], T.hl[:, 32 * a + 1:32 * a + 32:2], float(H), None, A.mult)
-        MM([(pX, T.idn[:], T["hb%d" % k][:, h0_of(k, a):h0_of(k, a) + H], True, False, "idn " + hN),
-            (pX, T.idh[:], T.D[:, cs], False, True, n("idh D#"))], pPn, H)
-        ACT(T.y[:, cs], pX, AF.Identity, pPn, n("y#"), H, bias=BIG, scale=1.0 - 2.0 ** -11)
+        pPn, h = ("pW", "pU")[a], T["hb%d" % k][:, cs]
+        pXY, pX, pY = (T.pU[:], T.pU[:, 0:H], T.pU[:, H:]) if a else (T.pW[:], T.pW[:, 0:8, :], T.pW[:, 8:16, :])
+        MM([(pXY, T.idn[:], T.CQ[:], True, False, "idn CQ")], pPn, P)
+        MM([(pX, T.idh[:], h, False, False, "idh " + hN), (pY, T.idm[:], h, False, False, "idm " + hN)], pPn, H)
+        MM([(pX, T.idh[:], T.Vb[:, cs], False, False, n("idh Vb#")),
+            (pY, T.idn[:], T.Vb[:, cs], False, True, n("idn Vb#"))], pPn, H)
+        ACT(T.y[:, cs], pX, AF.Identity, pPn, n("y#"), H, bias=BIG)
         ACT(RB[:, 0:H], T.y[:, cs], AF.Copy, n("y#"), n("B#"), H, bias=-BIG)
+        ACT(RB[:, H:], pY, AF.Abs, pPn, n("Rn#"), H)
         hn = "hn%d%d" % (k, a)
         o, sent = h0_of(k + 1, a), [hn]
         ACT(T["hn%d" % k][:, o:o + H], RB[:, 0:P].indirect(T.HL[:, ws]), AF.Copy, n("B# Rn# HL#"), hn, ga(H))
@@ -515,12 +574,12 @@ def rank_program(g, core, T, topo):
             MM([(pu[:, 2 * i:128:8], T.idF[:], T.nd[:, ws], False, False, n("idF nd#")) for i in range(4)], bank)
             wrap(pu[:, 0:128:2], T.WN, "WN", RB, 0, n("B#"), bank, True)
             V("scan", n("pD# DU"), n("ui#"), T.ui[:, ds], T.DU[:], pu[:, 0:128], 0.0, A.max, A.min, c=128)
-            address(a, T.ui[:, 128 * a + 7:128 * a + 128:8], T["XO%d" % k][:, ws], hn + "x")
             if a == 0:
-                send(T["XL%d" % (k + 1)][:], T["XO%d" % k][:], ["hn%d0x" % k, "hn%d1x" % k],
-                     "XL%d0 XL%d1" % (k + 1, k + 1), "x%d" % k, dst, FLY - 900)
-        os = slice(o, o + H)
-        send(T["hb%d" % (k + 1)][:, os], T["hn%d" % k][:, os], sent, "hb%d%d" % (k + 1, a), "h%d%d" % (k, a), dst, FLY)
+                address(T.ui[:, 7::8], T["XO%d" % k][:], "XO%d" % k)
+                send(T["XL%d" % (k + 1)][:], T["XO%d" % k][:], ["XO%d" % k],
+                     "XL%d0 XL%d1" % (k + 1, k + 1), "x%d" % k, dst, FLY - 1000)
+        send(T["hb%d" % (k + 1)][:, cs], T["hn%d" % k][:, cs], [hn], "hb%d%d" % (k + 1, a), "h%d%d" % (k, a), dst, FLY)
+        place_in[:] = ["write%d" % a, 0]
         MM([(pR[:, 10 * j:144:9], T.idK[:], T.nd[:, 16 * a:16 * a + 16 - j], False, False, n("idK nd#"))
             for j in range(1, 8)] + [(pR[:, 8:144:9], T.idL[:], T.nd[:, ws], False, True, n("idL nd#"))], pRn)
         V("scan", "rst9 " + pRn, n("ls#"), T.ls[:, ns], T.rst9[:], pR[:, 0:144], 0.0, A.mult, A.max, c=144)
@@ -535,6 +594,7 @@ def rank_program(g, core, T, topo):
 
     for k in range(STEPS):
         if k == STEPS - 1:
+            place_in[:] = ["image", 0]
             for hf in range(2):
                 cs = part(hf, 512)
                 ACT(T.yoS[:, cs], T.TB[:, cs], AF.Abs, "TB", "yoS")
@@ -548,6 +608,7 @@ def rank_program(g, core, T, topo):
         if k < STEPS - 1:
             tables()
 
+    place_in[:] = ["out", 0]
     dma(T.yo[:], T.yoS[:, 0:W], "st_yo", ["yoS"], [], 4000)
     dma(T.yh[:], T["hb%d" % STEPS][:, 0:P], "st_yh", ["hb%d0" % STEPS, "hb%d1" % STEPS], [], 2500)
     ACT(T.ymS[:], T.RW[:, 0:W], AF.Copy, "RW", "ymS", 1024, bias=1.0, scale=-1.0)

import numpy
from concourse.mybir import dt, AluOpType, AxisListType, ActivationFunctionType

N, W, R, P, STEPS, SHIFT = 6, 1024, 8192, 512, 3, 2
H = P // 2
F32, BF, I32, U16 = "float32", "bfloat16", "int32", "uint16"
SCRATCH = {}


def sb(dtype, cols, names):
    for n in names.split():
        SCRATCH[n] = ("psum" if n[0] == "p" and n[1].isupper() else "sbuf", [128, cols], dtype)


sb(BF, R, "hdrS")
sb(I32, W, "owS")
sb(I32, 256, "mkS")
sb(BF, 256, "mkB")
sb(BF, 512, "U hb0")
sb(BF, 128, "wR")
sb(I32, 128, "thR")
sb(F32, 128, "thF")
sb(F32, W, "G ymS")
sb(F32, W + 128, "TB RW yoS")
sb(F32, W + 16, "FB")
sb(BF, 512, "S Sh WS WN Vb")
sb(BF, 32, "R2 R2m R3b")
sb(BF, 128, "ones bones idn idh idm idK idL LT prm")
sb(F32, 128, "permf zero idf idg")
sb(BF, 16, "wS wN R3")
sb(F32, 8, "g8f one")
sb(I32, 8, "thS pi ci ta")
sb(F32, 8, "pcol c32 taf wa wb wc wd")
sb(F32, 256, "jmod DIAG RST")
sb(F32, 144, "rst9")
sb(BF, 144, "zb CKa CK")
sb(F32, 288, "ls")
sb(BF, 288, "AD")
sb(I32, 64, "DZ")
sb(I32, 128, "DY Z")
sb(BF, 64, "CX1 CX2")
sb(BF, 128, "CU idF")
sb(BF, 64, "CM CF")
sb(F32, 64, "DH im")
sb(F32, 128, "DU")
sb(F32, 16, "base gcol")
sb(F32, 32, "thr")
sb(F32, 64, "gl hl")
sb(F32, P, "pU pD0 pD1 pP0 pP1 pR0 pR1 gm sc ra WT0 WT1 dr tt y")
SCRATCH["pW"] = ("psum", [128, 16, 32], F32)
sb(BF, P, "D THW THg RB0 RB1")
sb(BF, H, "THg0")
sb(BF, P, "CQ")
sb(BF, 1024, "S8")
for k in range(STEPS):
    sb(BF, P, "hb%d hn%d" % (k + 1, k))
sb(I32, 32, "zz")
sb(I32, 64, "q2")
sb(I32, 128, "qm")
sb(I32, 256, "ui")
sb(I32, 136, "uq")
sb(I32, 128, "sq")
sb(BF, 32, "key nd")
sb(U16, 32, "XL0 XL1 XL2 XO0 XO1 PL OL OL0 SL HL EL")
LOADS = ["marks", "owner", "w", "th", "h0", "hdr"]
SEMAPHORES = ["V", "A", "T", "P"] + ["ld_" + n for n in LOADS] \
    + ["%s%d%d" % (n, k, a) for n in ("arrh", "loch") for k in range(STEPS) for a in range(2)] \
    + ["%s%d" % (n, k) for n in ("arrx", "locx") for k in range(STEPS - 1)] \
    + ["arrw", "locw", "st_yo", "st_ym", "st_yh"]
KS, HUGE = 2.0 ** 18, 3 * 2.0 ** 29
FAR = 2.0 ** 32
BIG = 12582912.0
CYC, PE, GATHER, SCATTER, WAKE, DMA, SEND, FLY = 0.87, 0.44, 1.4, 3.4, 200, 2000, 1000, 2400
ROUNDS, SLACK, TWIN = 55000, 40.0, 0.5
ORDER = []
MIX = 1.0


def rank_program(g, core, T, topo):
    rank = T.rank_of(core)
    if rank is None:
        return
    A, AF = AluOpType, ActivationFunctionType
    queues = {"V": g.vector, "A": g.scalar, "T": g.tensor, "P": g, "Y": g.sync}
    nodes, marks, soft, place_in = [], {}, {}, ["setup", 0]

    def node(q, emit, reads, writes, cost, lat=0.0, sem=None, early=0.0):
        nodes.append({"q": q, "emit": emit, "r": reads, "w": writes, "cost": cost, "lat": lat, "sem": sem or (q, 1),
                      "early": early, "tag": tuple(place_in)})
        place_in[1] += 1

    def mark(name):
        marks[name] = len(nodes) - 1

    def after(*names):
        soft.setdefault(len(nodes) - 1, []).extend(marks[name] for name in names)

    def op(q, fn, reads, writes, cost):
        node(q, [(fn, reads)], reads, writes, cost)

    vec = {"tt": g.vector.tensor_tensor, "ts": g.vector.tensor_scalar, "cp": g.vector.tensor_copy,
           "scan": g.vector.tensor_tensor_scan, "ms": g.vector.memset}

    def V(name, reads, writes, *args, c=64):
        op("V", lambda: vec[name](*args), reads.split(), writes.split(), c * CYC)

    def ACT(out, in_, func, reads, writes, c=512, bias=0.0, scale=1.0):
        op("A", lambda: g.scalar.activation(out, in_, func, bias=bias, scale=scale), reads.split(), writes.split(),
           c * CYC)

    def MM(items, bank, n=64):
        emit = [((lambda it=it: g.tensor.matmul(it[0], it[1], it[2], it[3], it[4])), it[5].split()) for it in items]
        node("T", emit, [r for e in emit for r in e[1]], [bank], len(items) * n * PE)

    def dma(out, in_, sem, reads, writes, lat=DMA, early=0.0):
        node("Y", [((lambda: g.sync.dma_start(out, in_)), reads)], reads, writes, 60, lat, (sem, 16), early)

    def ga(n):
        return 60 + GATHER * n

    def is_bank(r):
        return r[0] == "p" and r[1].isupper()

    def schedule():
        lastw, rd = {}, {}
        n = len(nodes)
        preds, succ = [{} for _ in range(n)], [{} for _ in range(n)]
        for i, d in enumerate(nodes):
            ps = {}
            for w in d["w"]:
                for p in rd.get(w, []) + lastw.get(w, []):
                    ps[p] = 0.0 if nodes[p]["sem"][0] == d["sem"][0] else WAKE
            for r in d["r"]:
                for p in rd.get(r, []) if is_bank(r) else []:
                    ps[p] = 0.0 if nodes[p]["sem"][0] == d["sem"][0] else WAKE
            for r in d["r"]:
                for p in lastw.get(r, []):
                    ps[p] = WAKE
            ps.pop(i, None)
            for p, gap in ps.items():
                preds[i][p] = succ[p][i] = gap + nodes[p]["lat"]
            for p in soft.get(i, []):
                preds[i].setdefault(p, 0.0)
                succ[p].setdefault(i, 0.0)
            if d["early"] and i:
                preds[i][i - 1] = succ[i - 1][i] = 0.0
            for r in d["r"]:
                rd.setdefault(r, []).append(i)
            for w in d["w"]:
                lastw[w] = [i]
                rd[w] = []

        def place(order, keep, end, ready):
            end, ready, busy = list(end), list(ready), {q: [] for q in queues}
            for i in order[:keep]:
                busy[queue[i]].append((end[i] - costs[i], end[i], i))
            for line in busy.values():
                line.append((1e18, 1e18, -1))
            for i in order[keep:]:
                cost, line, t = costs[i], busy[queue[i]], 0.0
                for p, gap in needs[i]:
                    if end[p] + gap > t:
                        t = end[p] + gap
                ready[i] = t
                at = len(line) - 1
                while at and line[at - 1][1] > t:
                    at -= 1
                while t + cost > line[at][0]:
                    if line[at][1] > t:
                        t = line[at][1]
                    at += 1
                line.insert(at, (t, t + cost, i))
                end[i] = t + cost
            return end, ready, busy

        costs, queue = [d["cost"] for d in nodes], [d["q"] for d in nodes]
        needs, last = [list(p.items()) for p in preds], [i for i in range(n) if not succ[i]]

        more = {round(ga(m) * CYC): 1.35 for m in (128, H)}
        more.update({round((m + 128 * SCATTER) * CYC): 1.5 for m in (60, 70)})
        slow = [c * (1.3 * more.get(round(c), 1.0) if q in "VAT" else 1.0) for c, q in zip(costs, queue)]

        def replay(order):
            end, free = [0.0] * n, {q: 0.0 for q in queues}
            for i in order:
                t = free[queue[i]]
                for p, gap in needs[i]:
                    if end[p] + gap > t:
                        t = end[p] + gap
                end[i] = free[queue[i]] = t + slow[i]
            return max(end[j] + nodes[j]["lat"] for j in last)

        rnd, twins = numpy.random.RandomState(0), {}
        for i, d in enumerate(nodes):
            twins.setdefault(d["tag"], []).append(i)
        rest = [0.0] * n
        for i in range(n - 1, -1, -1):
            rest[i] = nodes[i]["cost"] + max([rest[s] + gap for s, gap in succ[i].items()] + [nodes[i]["lat"]])
        order = sorted(range(n), key=lambda i: (-rest[i] - nodes[i]["early"], i))
        best, now, chain, lo, times = None, None, [], 0, ([0.0] * n, [0.0] * n)
        for r in range(ROUNDS):
            new = order
            if chain:
                i, back = chain[rnd.randint(len(chain))], rnd.rand() < 0.5
                i = rnd.randint(n) if rnd.rand() > 0.7 else before.get(i, i) if back else i
                far = (2, 5, 10, 25, 60)[rnd.randint(5)]
                for i in reversed(twins[nodes[i]["tag"]] if rnd.rand() < TWIN else [i]):
                    lo, hi = (pos[i], pos[i] + far) if back else (max(0, pos[i] - far), pos[i])
                    need, todo = {i}, [i]
                    while todo:
                        more = [p for p in (succ if back else preds)[todo.pop()] if lo <= pos[p] <= hi and p not in need]
                        need.update(more)
                        todo += more
                    new = new[:lo] + sorted(new[lo:hi + 1], key=lambda v: (v in need) == back) + new[hi + 1:]
            end, ready, busy = place(new, lo, *times)
            i = max(last, key=lambda j: end[j] + nodes[j]["lat"])
            span, bar = end[i] + nodes[i]["lat"], SLACK * (1.0 - r / ROUNDS) * rnd.exponential()
            if now is not None and span > fast + bar + 300.0:
                continue
            new = sorted(range(n), key=lambda j: (end[j] - costs[j], j))
            both = span + MIX * replay(new)
            if now is not None and both > now + bar:
                continue
            fast, span = span, both
            now, order, chain = span, new, [i]
            ahead = {line[a][2]: line[a - 1][2] for line in busy.values() for a in range(1, len(line))}
            before, times, pos = ahead, (end, ready), {v: j for j, v in enumerate(order)}
            if best is None or span < best[0]:
                best = (span, order)
            while end[i] - nodes[i]["cost"] - ready[i] > 1.0 or preds[i]:
                late = end[i] - nodes[i]["cost"] - ready[i] > 1.0
                i = ahead[i] if late else max(preds[i], key=lambda p: end[p] + preds[i][p])
                chain.append(i)
        return best[1]

    def issue(order):
        known = {q: {} for q in queues}
        clock, total, lastw, rd = {}, {}, {}, {}

        def wait_for(q, deps):
            best = {}
            for s, v in deps:
                best[s] = max(v, best.get(s, 0))
            todo = [(s, v) for s, v in best.items() if known[q].get(s, 0) < v]
            todo = [d for d in todo if not any(o != d and clock[o].get(d[0], 0) >= d[1] for o in todo)]
            for s, v in todo:
                queues[q].wait_ge(T.sem[s], v)
                for a, b in clock[(s, v)].items():
                    known[q][a] = max(b, known[q].get(a, 0))
                known[q][s] = max(v, known[q].get(s, 0))

        for i in order:
            d = nodes[i]
            q, (sem, inc) = d["q"], d["sem"]
            ins = None
            for j, (fn, reads) in enumerate(d["emit"]):
                deps = []
                for r in reads:
                    if r in lastw:
                        deps.append(lastw[r])
                    if is_bank(r):
                        deps += [x for x in rd.get(r, {}).items() if x[0] != sem]
                for w in d["w"] if j == 0 else []:
                    if w in lastw and lastw[w][0] != sem:
                        deps.append(lastw[w])
                    deps += [x for x in rd.get(w, {}).items() if x[0] != sem]
                wait_for(q, deps)
                ins = fn()
            if inc == 0:
                key, rkey = d["remote"]
                for s, v in (key, rkey):
                    total[s] = v
                    clock[(s, v)] = {}
            else:
                ins.then_inc(T.sem[sem], inc)
                total[sem] = total.get(sem, 0) + inc
                clock[(sem, total[sem])] = dict(known[q])
                key = rkey = (sem, total[sem])
            for r in d["r"]:
                rd.setdefault(r, {})[rkey[0]] = rkey[1]
            for w in d["w"]:
                lastw[w] = key
                rd[w] = {}
        for s, v in total.items():
            g.wait_ge(T.sem[s], v)

    def part(a, n):
        return slice(a * n, a * n + n)

    def blk(buf, c):
        return buf[:, 128 * c:128 * c + 128]

    c1 = slice(0, 1)
    dma(T.mkS[0:32, :], T.marks[:], "ld_marks", [], ["mkS"], early=9e6)
    dma(T.wR[0:1, :], T.w[:], "ld_w", [], ["wR"], 2000, early=8e6)
    dma(T.thR[0:1, :], T.th[:], "ld_th", [], ["thR"], 2000, early=7e6)
    dma(T.hb0[:], T.h0[:], "ld_h0", [], ["hb00", "hb01"], 2200, early=6e6)
    dma(T.owS[:], T.owner[:], "ld_owner", [], ["owS"], 3400, early=5e6)
    dma(T.hdrS[:], T.hdr[:], "ld_hdr", [], ["hdrS"], 6000, early=1.0)

    def iota(buf, name, pattern, base, cm, c):
        op("P", lambda: g.iota(buf, pattern, base, cm, allow_small_or_imprecise_dtypes=True), [], [name], 140 + 2 * c)

    def sel(out, in_, pattern, cmp, base, cm, reads, writes, c, fill=0.0):
        op("P", lambda: g.affine_select(out, in_, pattern, cmp, fill, base, cm), [reads], [writes], 180 + 2 * c)

    pc = T.pcol[:, c1]
    V("ms", "", "ones", T.ones[:], 1.0)
    op("P", lambda: g.iota(T.pi[:, c1], [[0, 1]], 0, 1), [], ["pi"], 140)
    sel(T.bones[:], T.ones[:], [[-16, 8], [0, 16]], A.is_ge, 0, 1, "ones", "bones", 128)
    sel(T.bones[:], T.bones[:], [[16, 8], [0, 16]], A.is_ge, 15, -1, "bones", "bones", 128)
    sel(T.idn[:], T.ones[:], [[-1, 128]], A.is_equal, 0, 1, "ones", "idn", 128)
    iota(T.jmod[:], "jmod", [[0, 16], [1, 16]], 0, 0, 256)
    iota(T.base[:], "base", [[16, 16]], 0, 0, 16)
    sel(T.prm[:], T.ones[:], [[-1, 16], [-16, 8]], A.is_equal, 0, 1, "ones", "perm", 128)
    iota(T.gcol[:], "gcol", [[0, 2], [1, 8]], 0, 0, 16)
    iota(T.im[:], "im", [[0, 16], [1, 4]], 0, 0, 64)
    ACT(T.zero[:], T.ones[:], AF.Silu, "ones", "zero", 1400, scale=0.0)
    V("ms", "", "zb", T.zb[:], 0.0)
    V("ms", "", "CQ", T.CQ[:, 0:H], -0.25, c=128)
    V("ms", "", "CQ", T.CQ[:, H:], 0.0, c=128)
    iota(T.CKa[:], "CKa", [[0, 2], [1, 8], [0, 9]], -64, 0, 144)
    sel(T.CK[:], T.CKa[:], [[0, 2], [1, 8], [-1, 9]], A.is_ge, 0, 0, "CKa", "CK", 144, -256.0)
    V("ms", "", "CK", T.CK[:, 0::9], 0.0)
    V("ts", "CKa", "CK", T.CK[:, 8::9], T.CKa[:, 8::9], 128.0, None, A.add)
    g8 = T.bones[:, 0::16]
    V("ts", "pi", "ci", T.ci[:, c1], T.pi[:, c1], 15, None, A.bitwise_and)
    V("cp", "ci", "pcol", pc, T.ci[:, c1])
    V("ts", "jmod pcol", "DIAG", T.DIAG[:], T.jmod[:], pc, None, A.is_equal, c=256)
    V("ms", "", "U", T.U[0:32, :], 1.0, c=256)
    sel(T.U[0:32, :], T.U[0:32, :], [[-1, 4], [-4, 8], [0, 16]], A.is_equal, 0, 1, "U", "U", 512)
    V("cp", "thR", "thF", T.thF[0:1, :], T.thR[0:1, :], c=128)
    V("ms", "", "one", T.one[0:1, c1], 1.0)
    MM([(T.pP0[:, 0:1], T.wR[0:1, :], T.ones[0:1, c1], True, True, "wR ones")], "pP0")
    MM([(T.pP1[:, 0:1], T.thF[0:1, :], T.one[0:1, c1], True, True, "thF one")], "pP1", 256)
    V("cp", "pP1", "thS", T.thS[:, c1], T.pP1[:, 0:1])
    V("ms", "", "S", T.S[:], 0.0, c=256)
    for r in range(4):
        ACT(T.S[:, 129 * r:128 * (r + 1):4], T.bones[:, r::4], AF.Copy, "bones", "S", 64, scale=KS)
    V("ts", "S", "Sh", T.Sh[:], T.S[:], -0.5, None, A.mult, c=256)
    V("ts", "S pP0", "WS", T.WS[:], T.S[:], T.pP0[:, 0:1], 1.0 / KS, A.mult, A.mult, c=256)
    c2 = slice(1, 2)
    V("ts", "ci", "ci2", T.ci[:, c2], T.ci[:, c1], 2, None, A.arith_shift_right)
    V("cp", "ci2", "pq", T.pcol[:, c2], T.ci[:, c2])
    V("ts", "im pq", "CF", T.CF[:], T.im[:], T.pcol[:, c2], FAR, A.not_equal, A.mult)
    V("ts", "CF", "CM", T.CM[:], T.CF[:], 128.0 * KS, None, A.add)
    V("cp", "CF", "CU", T.CU[:, 0::2], T.CF[:])
    V("ts", "CF", "CU", T.CU[:, 1::2], T.CF[:], 2.0 ** 21, None, A.add)
    V("ms", "", "S8", T.S8[:], 0.0, c=512)
    for r in range(8):
        ACT(T.S8[:, 129 * r:128 * (r + 1):8], T.bones[:, r::8], AF.Copy, "bones", "S8", 64, scale=KS)
    V("ts", "base pcol", "thr0", T.thr[:, 0:16], T.base[:], 0.0, pc, A.mult, A.add)
    V("ts", "thr0", "CX1", T.CX1[:, 0::4], T.thr[:, 0:16], 8.0, FAR, A.is_ge, A.mult)
    V("ts", "thr0", "CX1", T.CX1[:, 2::4], T.thr[:, 0:16], 8.0, FAR, A.is_lt, A.mult)
    V("ms", "", "CX1", T.CX1[:, 1::4], FAR)
    V("ms", "", "CX1", T.CX1[:, 3::4], 512.0)
    V("ms", "", "CX2", T.CX2[:], 0.0)
    for n, step, kind in (("DZ", 4, int), ("DY", 4, int), ("DU", 8, float), ("DH", 4, float)):
        V("ms", "", n, T[n][:], kind(-HUGE), c=128)
        V("ms", n, n, T[n][:, 0::step], kind(HUGE))
    V("ts", "mkS", "mkB", T.mkB[0:32, :], T.mkS[0:32, :], 2.0, -1.0, A.mult, A.add, c=256)
    for hf in range(2):
        cs, bank = part(hf, 512), "pR%d" % hf
        MM([(T[bank][:, part(c, 256)], T.U[0:32, part(2 * hf + c, 128)], T.mkB[0:32, :], True, True, "U mkB")
            for c in range(2)], bank, 256)
        ACT(T.RW[:, cs], T[bank][:], AF.Copy, bank, "RW", bias=0.5, scale=-0.5)
        V("tt", "owS " + bank, "TB", T.TB[:, cs], T.owS[:, cs], T[bank][:], A.mult, c=512)

    def tables():
        place_in[:] = ["tables", 0]
        V("scan", "RW TB", "FB", T.FB[:, 8:8 + W], T.RW[:, 0:W], T.TB[:, 0:W], 0.0, A.mult, A.max, c=1024)
        mark("FB")
        V("cp", "FB", "FBw", T.FB[:, 7:8], T.FB[:, 7 + W:8 + W])
        for a in range(8):
            bank = "pR%d" % (a // 4)
            MM([(blk(T[bank], a % 4), T.idg[:], T.FB[:, 8 + 128 * a:136 + 128 * a], True, False, "idg FB")], bank, 512)
            MM([(blk(T[bank], a % 4), T.idf[:], T.FB[:, 7 + 128 * a:135 + 128 * a], False, True, "idf FB FBw")], bank, 512)
        for a in range(4):
            cs, bank = part(a, 256), "pR%d" % (a // 2)
            V("scan", "RW " + bank + (" G" if a else ""), "G", T.G[:, cs], T.RW[:, cs], T[bank][:, part(a % 2, 256)],
              T.G[:, 256 * a - 1:256 * a] if a else 0.0, A.mult, A.add, c=256)
        mark("G")

    V("ms", "", "RST", T.RST[:], 1.0, c=256)
    V("ms", "RST", "RST", T.RST[:, 0::16], 0.0)
    V("ms", "", "q2", T.q2[:], 0)
    for j, v in enumerate((0, 1, 0, 32)):
        V("ms", "", "uq", T.uq[:, j::4], v)
    for a in range(2):
        V("ts", "base pcol", "gl", T.gl[:, 32 * a + 1:32 * a + 32:2], T.base[:], pc, 1.0 / H, A.add, A.mult)
    V("ms", "", "rst9", T.rst9[:], 1.0, c=144)
    V("ms", "rst9", "rst9", T.rst9[:, 0::9], 0.0)
    V("ts", "pcol", "c32", T.c32[:, c1], pc, 32.0, None, A.mult)
    V("ts", "gcol c32", "OL0", T.OL0[:, 0:16], T.gcol[:], T.c32[:, c1], None, A.add)
    V("cp", "OL0 DZ", "DZ", T.DZ[:, 3::4], T.OL0[:, 0:16])
    V("cp", "gcol CX2", "CX2", T.CX2[:, 3::4], T.gcol[:])
    for n, f in (("idf", 1.0), ("idg", -1.0), ("idh", 0.5), ("idm", -1.0), ("idK", 128.0), ("idL", -128.0),
                 ("idF", FAR)):
        ACT(T[n][:], T.idn[:], AF.Copy, "idn", n, 128, scale=f)
    ACT(T.permf[:], T.prm[:], AF.Copy, "perm", "permf", 128)
    ACT(T.g8f[:], g8, AF.Copy, "bones", "g8f", 64)
    for n, f in (("R2", 2.0), ("R2m", -1.0)):
        ACT(T[n][:, 0::2], T.bones[:, 0::8], AF.Copy, "bones", n, 64, scale=f * KS)
        ACT(T[n][:, 1::4], g8, AF.Copy, "bones", n, 64, scale=0.0)
        ACT(T[n][:, 3::4], g8, AF.Copy, "bones", n, 64, scale=f * 8.0)
    V("ts", "thS", "ta", T.ta[:, c1], T.thS[:, c1], 8192 - 64, None, A.bitwise_and)
    V("ts", "thS", "tb", T.ta[:, c2], T.thS[:, c1], 63, None, A.bitwise_and)
    V("ts", "ta tb", "taf", T.taf[:, 0:2], T.ta[:, 0:2], -1.0, None, A.mult)
    V("ts", "pcol", "s32", T.taf[:, 2:3], pc, 32.0, 1.0 / 64, A.add, A.mult)
    V("ms", "", "LT", T.LT[:], 0.0)
    for t in range(3):
        ACT(T.LT[:, t::16], T.ones[:, 0:8], AF.Identity, "ones taf s32", "LT", 64, scale=T.taf[:, t:t + 1])
    MM([(T.pW[:, :, 8 * b:8 * b + 8], T.LT[:], T.prm[:], True, True, "LT perm") for b in range(4)], "pW", 128)
    ACT(T.THW[:], T.pW[:], AF.Copy, "pW", "THW")
    V("ts", "pcol", "wc", T.wc[:, c1], pc, 2.0, 64.0, A.is_equal, A.mult)
    V("ts", "wc", "wb", T.wb[:, c1], T.wc[:, c1], -4.0 * KS, None, A.mult)
    V("ts", "pcol", "wd", T.wd[:, c1], pc, 2.0, -KS, A.is_lt, A.mult)
    V("tt", "wb wd", "wa", T.wa[:, c1], T.wb[:, c1], T.wd[:, c1], A.add)
    ACT(T.R3[:, 0::2], g8, AF.Identity, "bones wa", "R3", 64, scale=T.wa[:, c1])
    ACT(T.R3[:, 1::2], g8, AF.Identity, "bones wc", "R3", 64, scale=T.wc[:, c1])
    V("ts", "bones wb", "R3b", T.R3b[:, 0:32], T.bones[:, 0::4], T.wb[:, c1], 0.5, A.mult, A.mult)
    ACT(T.THg0[:], T.THW[:, 0:P].indirect(T.OL0[:, 0:16]), AF.Copy, "THW OL0", "THgc", ga(H))
    tables()
    place_in[:] = ["setup", len(nodes)]

    dst = T.cores[(rank + SHIFT) % N]
    Fwin, Gwin, Hwin = T.FB[:, 8:8 + W], T.G[:, 0:W], T.hdrS[:, 0:R]

    def send(out, in_, reads, writes, name, to, fly):
        rid, pid, _ = topo.addr(to)
        count = len(topo.engines(core, to))
        node("P", [((lambda: g.remote_dma(out, in_, T.sem["arr" + name], T.sem["loc" + name], pid, rid,
                                          topo.mask(core, to))), reads)], reads, writes.split(), SEND, fly, (name, 0))
        nodes[-1]["remote"] = [("arr" + name, count), ("loc" + name, count)]

    def wrap(out, mat, mN, src, first, sN, bank, stop):
        MM([(out, blk(mat, r), src[:, first + r:first + H:4], False, stop and r == 3, mN + " " + sN) for r in range(4)],
           bank)

    def address(ui, out, oN):
        uq = T.uq
        V("ts", "ui0 ui1 uq", "uq", uq[:, 2:128:4], ui, 4095, None, A.bitwise_and)
        V("scan", "uq", "sq", T.sq[:], uq[:, 0:128], uq[:, 2:130], 0.0, A.mult, A.add, c=128)
        V("ts", "sq", "zz", T.zz[:], T.sq[:, 2::4], 9, 63, A.arith_shift_right, A.bitwise_and)
        V("ts", "zz pcol", oN, out, T.zz[:], 16.0, pc, A.mult, A.add)

    def h0_of(k, a):
        return H * a

    def key_of(k, a, n):
        return T.key[:, 16 * a:16 * a + n]

    V("cp", "pP0", "wS", T.wS[:, c1], T.pP0[:, 0:1])
    send(T.wN[:, c1], T.wS[:, c1], ["wS"], "wN", "w", T.cores[(rank - SHIFT) % N], FLY - 700)
    V("ts", "S wN", "WN", T.WN[:], T.S[:], T.wN[:, c1], 1.0 / KS, A.mult, A.mult, c=256)
    for a in (1, 0):
        pD = "pD%d" % a
        MM([(T[pD][:, 0:64], T.idn[:], T.CF[:], True, False, "idn CF")], pD)
        wrap(T[pD][:, 0:64], T.WS, "WS", T.hb0, H * a, "hb0%d" % a, pD, True)
        V("scan", pD + " DH", "ui%d" % a, T.ui[:, part(a, 64)], T.DH[:], T[pD][:, 0:64], 0.0, A.max, A.min)
    address(T.ui[:, 3:128:4], T.XL0[:], "XL00 XL01")

    def start(k, a):
        place_in[:] = ["start%d" % a, 0]
        n = lambda s: s.replace("XL", "XL%d" % k).replace("#", str(a))
        ws, cs, ns = part(a, 16), part(a, H), part(a, 144)
        pR = n("pR#")
        xl, key = T["XL%d" % k][:, ws], key_of(k, a, 16)
        if a:
            V("ts", n("XL0 XL1 pcol"), "key0 key1", T.key[:], T["XL%d" % k][:], pc, 1.0 / 16, A.subtract, A.mult)
        V("tt", n("FB XL# DIAG"), n("gm#0 gm#1"), T.gm[:, cs], Fwin.indirect(xl), T.DIAG[:], A.mult, c=ga(H))
        V("scan", n("RST gm#0 gm#1"), n("sc#"), T.sc[:, cs], T.RST[:], T.gm[:, cs], 0.0, A.mult, A.add, c=H)
        V("cp", n("sc#"), n("PL#"), T.PL[:, ws], T.sc[:, H * a + 15:H * a + H:16])
        ACT(T.ra[:, cs], Fwin.indirect(xl), AF.Copy, n("FB XL#"), n("ra#"), ga(H))
        for b in range(2):
            MM([(T.pW[:, :, 8 * b:8 * b + 8], blk(T.ra, 2 * a + b), T.permf[:], True, True, n("permf ra#"))], "pW", 512)
        ACT(T[n("WT#")][:], T.pW[:], AF.Copy, "pW", n("WT#"))
        ACT(T.dr[:, cs], Gwin.indirect(xl), AF.Copy, n("G XL#"), n("dr#"), ga(H))
        mark(n("dr#"))
        it = [(T.pU[:, 0:144], T.idn[:], T.zb[:], True, False, "idn zb")]
        for j in range(1, 8):
            it.append((T.pU[:, j:144:9], T.idn[:], key, False, False, n("idn key#")))
            it.append((T.pU[:, 10 * j:144:9], T.idm[:], key_of(k, a, 16 - j), False, j == 7, n("idm key#")))
        MM(it, "pU")
        ACT(T.AD[:, ns], T.pU[:, 0:144], AF.Abs, "pU", n("AD#"), 144, scale=256.0)
        MM([(T[pR][:, 0:144], T.idn[:], T.CK[:], True, False, "idn CK"),
            (T[pR][:, 0:144], T.idm[:], T.AD[:, ns], False, False, n("idm AD#")),
            (T[pR][:, 0:144:9], T.idn[:], key, False, False, n("idn key#"))], pR, 120)

    def hop_of(k, a, hop):
        place_in[:] = ["hop%d%d" % (a, hop), 0]
        n = lambda s: s.replace("#", str(a))
        ws, cs = part(a, 16), part(a, H)
        hN, pDn, pPn = "hb%d%d" % (k, a), n("pD#"), n("pP#")
        h, pD, pP, RB, pl = T["hb%d" % k], T[pDn], T[pPn], T[n("RB#")], T.PL[:, ws]
        hs = slice(h0_of(k, a), h0_of(k, a) + H)
        th, thN = (T.THg, n("THg#")) if hop else (T.THg0, "THgc")
        t0 = H * a if hop else 0
        if hop:
            for b in range(2):
                V("tt", n("WT# OL# DIAG"), n("gm#%d" % b), blk(T.gm, 2 * a + b),
                  T[n("WT#")][:, 8 * b:P].indirect(T.OL[:, 16 * a + 8 * b:16 * a + 8 * b + 8]), T.DIAG[:, 0:128], A.mult,
                  c=ga(128))
                if hop == 3:
                    after("G")
                MM([(pP[:, 8 * b:8 * b + 8], blk(T.gm, 2 * a + b), T.g8f[:], True, True, n("g8f gm#%d" % b))], pPn, 256)
            V("cp", pPn, n("PL#"), pl, pP[:, 0:16])
            ACT(T.THg[:, cs], T.THW[:, 0:P].indirect(T.OL[:, ws]), AF.Copy, n("THW OL#"), thN, ga(H))
            if hop == 3:
                after("dr0", "dr1")
        if hop < 3:
            MM([(pD[:, 0:64], T.idn[:], T.CX1[:], True, False, "idn CX1"),
                (pD[:, 0:64], T.idn[:], T.CX2[:], False, False, "idn CX2")]
               + [(pD[:, part(b, 32)], blk(h, 2 * a + b), T.R2m[:], False, False, "R2m " + hN) for b in range(2)], pDn)
            for r0 in (0, 4):
                MM([(pD[:, 0:64:2], blk(T.S8, r), th[:, t0 + r:t0 + H:8], False, False, "S8 " + thN)
                    for r in range(r0, r0 + 4)], pDn)
            V("tt", n("hdrS PL# ") + hN, n("D#"), T.D[:, cs], Hwin.indirect(pl), h[:, hs], A.max, c=ga(H))
            ACT(RB[:, H:], Hwin.indirect(pl), AF.Copy, n("hdrS PL#"), n("Rn#"), ga(H))
            MM([(pD[:, part(b, 32)], blk(RB, 2 + b), T.R2m[:], False, False, n("R2m Rn#")) for b in range(2)], pDn)
            MM([(pD[:, part(b, 32)], blk(T.D, 2 * a + b), T.R2[:], False, b == 1, n("R2 D#")) for b in range(2)], pDn)
            zs, last = part(a, 64), slice(64 * a + 3, 64 * a + 64, 4)
            V("scan", n("pD# DY#") if hop else n("pD# DZ"), n("Z#"), T.Z[:, zs], T.DY[:, zs] if hop else T.DZ[:],
              pD[:, 0:64], 0.0, A.max, A.min)
            V("ts", n("Z# DY"), n("DY#"), T.DY[:, last], T.Z[:, last], 15 * 32 + 7, None, A.bitwise_and)
            V("cp", n("DY#"), n("OL#"), T.OL[:, ws], T.DY[:, last])
            return
        MM([(pP[:, 32 + 16 * b:48 + 16 * b], blk(T.THg, 2 * a + b), T.R3[:], True, True, "R3 " + thN) for b in range(2)],
           pPn)
        V("ts", pPn, n("EL#"), T.EL[:, ws], pP[:, 33:64:2], -32.0, None, A.add)
        ACT(T.thr[:, ws], pP[:, 32:64:2], AF.Copy, pPn, n("thr#"), 64, bias=128.0 * KS, scale=0.5)
        MM([(pD[:, 0:64], T.idn[:], T.CM[:], True, False, "idn CM")]
           + [(pD[:, part(b, 32)], blk(T.THg, 2 * a + b), T.R3b[:, 0:32], False, False, "R3b " + thN)
              for b in range(2)], pDn)
        wrap(pD[:, 0:64], T.Sh, "Sh", h, H * a, hN, pDn, False)
        V("tt", n("hdrS PL# ") + hN, n("D#"), T.D[:, cs], Hwin.indirect(pl), h[:, hs], A.max, c=ga(H))
        ACT(T.Vb[:, cs], Hwin.indirect(pl), AF.Copy, n("hdrS PL#"), n("Vb#"), ga(H))
        wrap(pD[:, 0:64], T.Sh, "Sh", T.Vb, H * a, n("Vb#"), pDn, False)
        wrap(pD[:, 0:64], T.S, "S", T.D, H * a, n("D#"), pDn, True)
        V("scan", n("pD# DH"), n("qm#"), T.qm[:, part(a, 64)], T.DH[:], pD[:, 0:64], 0.0, A.max, A.min)
        ge, q2, qm = T.gl[:, 32 * a:32 * a + 32:2], T.q2[:, 32 * a + 1:32 * a + 32:2], T.qm[:, 64 * a + 3:64 * a + 64:4]
        V("ts", n("qm# q2"), n("q2#"), q2, qm, 30 * int(KS), None, A.bitwise_and)
        V("tt", n("qm# thr# gl"), n("ge#"), ge, qm, T.thr[:, ws], A.is_ge)
        V("tt", n("q2# ge#"), n("nd#"), T.nd[:, ws], q2, ge, A.min)
        V("tt", n("dr# EL# DIAG"), n("tt#"), T.tt[:, cs], T.DIAG[:, 0:16].indirect(T.EL[:, ws]), T.dr[:, cs], A.mult,
          c=ga(H))

    def finish(k, a):
        place_in[:] = ["finish%d" % a, 0]
        n = lambda s: s.replace("#", str(a))
        ws, cs, ns = part(a, 16), part(a, H), part(a, 144)
        hN, pPn, pRn = "hb%d%d" % (k, a), n("pP#"), n("pR#")
        pX, pR, RB = T[pPn][:, H:], T[pRn], T[n("RB#")]
        V("scan", n("q2# ge#"), n("hl#"), T.hl[:, part(a, 32)], T.q2[:, part(a, 32)], T.gl[:, part(a, 32)], 0.0,
          A.min, A.add)
        V("ts", n("hl#"), n("HL#"), T.HL[:, ws], T.hl[:, 32 * a + 1:32 * a + 32:2], float(H), None, A.mult)
        pPn, h = ("pW", "pU")[a], T["hb%d" % k][:, cs]
        pXY, pX, pY = (T.pU[:], T.pU[:, 0:H], T.pU[:, H:]) if a else (T.pW[:], T.pW[:, 0:8, :], T.pW[:, 8:16, :])
        MM([(pXY, T.idn[:], T.CQ[:], True, False, "idn CQ")], pPn, P)
        MM([(pX, T.idh[:], h, False, False, "idh " + hN), (pY, T.idm[:], h, False, False, "idm " + hN)], pPn, H)
        MM([(pX, T.idh[:], T.Vb[:, cs], False, False, n("idh Vb#")),
            (pY, T.idn[:], T.Vb[:, cs], False, True, n("idn Vb#"))], pPn, H)
        ACT(T.y[:, cs], pX, AF.Identity, pPn, n("y#"), H, bias=BIG)
        ACT(RB[:, 0:H], T.y[:, cs], AF.Copy, n("y#"), n("B#"), H, bias=-BIG)
        ACT(RB[:, H:], pY, AF.Abs, pPn, n("Rn#"), H)
        hn = "hn%d%d" % (k, a)
        o, sent = h0_of(k + 1, a), [hn]
        ACT(T["hn%d" % k][:, o:o + H], RB[:, 0:P].indirect(T.HL[:, ws]), AF.Copy, n("B# Rn# HL#"), hn, ga(H))
        if k < STEPS - 1:
            bank, ds = n("pD#"), part(a, 128)
            pu = T[bank]
            MM([(pu[:, 0:128], T.idn[:], T.CU[:], True, False, "idn CU")], bank, 128)
            wrap(pu[:, 1:128:2], T.WN, "WN", RB, H, n("Rn#"), bank, False)
            MM([(pu[:, 2 * i:128:8], T.idF[:], T.nd[:, ws], False, False, n("idF nd#")) for i in range(4)], bank)
            wrap(pu[:, 0:128:2], T.WN, "WN", RB, 0, n("B#"), bank, True)
            V("scan", n("pD# DU"), n("ui#"), T.ui[:, ds], T.DU[:], pu[:, 0:128], 0.0, A.max, A.min, c=128)
            if a == 0:
                address(T.ui[:, 7::8], T["XO%d" % k][:], "XO%d" % k)
                send(T["XL%d" % (k + 1)][:], T["XO%d" % k][:], ["XO%d" % k],
                     "XL%d0 XL%d1" % (k + 1, k + 1), "x%d" % k, dst, FLY - 1000)
        send(T["hb%d" % (k + 1)][:, cs], T["hn%d" % k][:, cs], [hn], "hb%d%d" % (k + 1, a), "h%d%d" % (k, a), dst, FLY)
        place_in[:] = ["write%d" % a, 0]
        MM([(pR[:, 10 * j:144:9], T.idK[:], T.nd[:, 16 * a:16 * a + 16 - j], False, False, n("idK nd#"))
            for j in range(1, 8)] + [(pR[:, 8:144:9], T.idL[:], T.nd[:, ws], False, True, n("idL nd#"))], pRn)
        V("scan", "rst9 " + pRn, n("ls#"), T.ls[:, ns], T.rst9[:], pR[:, 0:144], 0.0, A.mult, A.max, c=144)
        V("ts", n("ls# pcol"), n("SL#"), T.SL[:, ws], T.ls[:, 144 * a + 8:144 * a + 144:9], 16.0, pc, A.mult, A.add)
        tab, col = "TB" if k < STEPS - 1 else "yoS", "ra"
        for j in (2 * a + 1, 2 * a):
            sl = T.SL[:, part(j, 8)]
            V("tt", n("SL# tt# %s# %s" % (col, tab)), tab, T[tab][:, 0:W + 128].indirect(sl), blk(T.tt, j),
              blk(T[col], j), A.add, c=60 + 128 * SCATTER)
            op("A", lambda sl=sl: g.scalar.activation(T.RW[:, 0:W + 128].indirect(sl), T.zero[:], AF.Silu),
               [n("SL#"), "zero", "RW"], ["RW"], (70 + 128 * SCATTER) * CYC)

    for k in range(STEPS):
        if k == STEPS - 1:
            place_in[:] = ["image", 0]
            for hf in range(2):
                cs = part(hf, 512)
                ACT(T.yoS[:, cs], T.TB[:, cs], AF.Abs, "TB", "yoS")
        for a in (1, 0):
            start(k, a)
        for hop in range(4):
            for a in (1, 0):
                hop_of(k, a, hop)
        for a in (1, 0):
            finish(k, a)
        if k < STEPS - 1:
            tables()

    place_in[:] = ["out", 0]
    dma(T.yo[:], T.yoS[:, 0:W], "st_yo", ["yoS"], [], 4000)
    dma(T.yh[:], T["hb%d" % STEPS][:, 0:P], "st_yh", ["hb%d0" % STEPS, "hb%d1" % STEPS], [], 2500)
    ACT(T.ymS[:], T.RW[:, 0:W], AF.Copy, "RW", "ymS", 1024, bias=1.0, scale=-1.0)
    dma(T.ym[:], T.ymS[0::16, :], "st_ym", ["ymS"], [])
    if not ORDER:
        ORDER.extend(schedule())
    issue(ORDER)
